import numpy as np
import ml_dtypes


def mxq(x, axis, fmt="e4m3"):
    dtype, down = {"e4m3": (ml_dtypes.float8_e4m3fn, 7), "e5m2": (ml_dtypes.float8_e5m2, 14)}[fmt]
    v = np.moveaxis(np.asarray(x, np.float32).astype(ml_dtypes.bfloat16).astype(np.float64), axis, -1)
    blocks = v.reshape(v.shape[:-1] + (-1, 32))
    amax = np.abs(blocks).max(-1, keepdims=True)
    byte = np.maximum(np.where(amax > 0, np.frexp(amax)[1] - 1 + 127, 0) - down, 1)
    scale = np.exp2(byte - 127.0)
    codes = (blocks / scale).astype(np.float32).astype(dtype).astype(np.float64)
    return np.moveaxis((codes * scale).reshape(v.shape), -1, axis)


WIDE = False


def mx_kscale(k):
    if not WIDE:
        return np.ones(k)
    levels = np.array([18, -18])
    if k % 512:
        return np.exp2(np.random.permutation(np.resize(levels, k // 32))).repeat(32)
    a = np.empty((k // 512, 16))
    for p in range(k // 512):
        a[p, :8] = np.random.permutation(np.resize(levels, 8))
        for g in range(8):
            far = levels[np.abs(levels - a[p, g]) >= 10]
            a[p, g + 8] = far[np.random.randint(len(far))]
    return np.exp2(a.ravel()).repeat(32)


def f64(x):
    return np.asarray(x).astype(np.float64)


def striped(idx):
    return np.tile(np.asarray(idx).reshape(-1, 16).T, (8, 1)).astype(np.uint16)


def unstriped(offs):
    return offs[:16].T.reshape(-1).astype(np.int64)


B, N, T, D, R, TU = 1, 512, 2048, 512, 1024, 2048


def setup_inputs():
    n = np.random.standard_normal
    idx = np.random.permutation(T)[:B * N]
    uidx = np.random.permutation(TU)[:B * R]
    s = mx_kscale(D)[:, None]
    z = np.ones(TU)
    z[uidx] = mx_kscale(B * R)
    u = np.ones(T)
    u[idx] = mx_kscale(B * N)
    r = np.random.uniform(0.5, 2.0, T) * u
    ur = np.random.uniform(0.5, 2.0, TU) * z
    return {
        "uT": (n((D, TU)) * s / ur).astype(np.float32),
        "vT": (n((D, T)) * (1.00 / np.sqrt(D)) / s / r).astype(np.float32),
        "y": np.random.randint(0, 2, (B, R, N)).astype(np.float32),
        "us": ur[uidx].reshape(B, R, 1).astype(np.float32),
        "ts": np.tile(r, (128, 1)).astype(np.float32),
        "offs": striped(idx),
        "uoffs": striped(uidx),
    }


def reference(uT, vT, y, us, ts, offs, uoffs):
    idx = unstriped(offs)
    pick = lambda x: x[:, idx].reshape(x.shape[0], B, N).transpose(1, 0, 2)
    uidx = unstriped(uoffs)
    w = pick(f64(vT))
    x = f64(uT)[:, uidx].reshape(D, B, R).transpose(1, 0, 2)
    a = mxq(x, 1, "e4m3").transpose(0, 2, 1) @ mxq(w, 1, "e4m3")
    sc = f64(us) * pick(f64(ts))[:, :1, :]
    a = a * sc
    g = (1.0 / (1.0 + np.exp(-a)) - f64(y))
    h = sc * g
    dv = mxq(x, 2, "e4m3") @ mxq(h, 1, "e5m2")
    gv = np.zeros((D, T))
    gv[:, idx] = dv.transpose(1, 0, 2).reshape(D, B * N)
    return gv

@@ -1,0 +1,181 @@
+from contextlib import ExitStack
+
+import concourse.mybir as mybir
+from concourse.masks import make_identity
+
+F32 = mybir.dt.float32
+BF16 = mybir.dt.bfloat16
+U32 = mybir.dt.uint32
+U16 = mybir.dt.uint16
+U8 = mybir.dt.uint8
+I32 = mybir.dt.int32
+E4M3 = mybir.dt.float8_e4m3fn_x4
+E5M2 = mybir.dt.float8_e5m2_x4
+ACT = mybir.ActivationFunctionType
+ALU = mybir.AluOpType
+
+P = 128
+D, R, N, T = 512, 1024, 512, 2048
+PACK = 4
+PASSES = R // (P * PACK)
+CHUNK = 1024
+FLOPS = 2 * 2 * D * R * N
+
+
+def tile_attend_gmf_nce_v_kernel(tc, uT, vT, y, us, ts, offs, uoffs, out):
+    nc = tc.nc
+    with ExitStack() as ctx:
+        keep = ctx.enter_context(tc.tile_pool(name="keep", bufs=1))
+        stage = ctx.enter_context(tc.tile_pool(name="stage", bufs=6))
+        psum = ctx.enter_context(tc.psum_pool(name="psum", bufs=4))
+
+        def kept(shape, dtype, name):
+            return keep.tile(shape, dtype, name=name, align_bytes=64)
+
+        tail_list = kept([P, N // 16], U16, "tail_list")
+        head_list = kept([P, R // 16], U16, "head_list")
+        u_planes = uT.rearrange("(p t) c -> p t c", t=PACK)
+        v_planes = vT.rearrange("(p t) c -> p t c", t=PACK)
+
+        ts_window = kept([P, T], F32, "ts_window")
+        warm = kept([P, 2], F32, "warm")
+        nc.vector.memset(warm[:, 0:1], 0.0)
+        nc.scalar.activation(warm[:, 1:2], warm[:, 0:1], ACT.Sigmoid)
+        nc.vector.memset(ts_window[:, :CHUNK], 0.0)
+        nc.gpsimd.memset(ts_window[:, CHUNK:], 0.0)
+        ident = kept([P, P], F32, "ident")
+        make_identity(nc, ident[:])
+        nc.sync.dma_start(ts_window[0:1, :], ts[0:1, :])
+
+        def load_pair(planes, pair, name, fine=False):
+            window = kept([P, T, 2], BF16, name)
+            for c0 in range(0, T, CHUNK):
+                raw = stage.tile([P, 2, CHUNK], F32, name="raw", tag="raw")
+                if fine and c0 == 0:
+                    for h0 in range(0, CHUNK, CHUNK // 2):
+                        cols = slice(h0, h0 + CHUNK // 2)
+                        for e in range(2):
+                            nc.sync.dma_start(raw[:, e, cols], planes[:, 2 * pair + e, cols])
+                        nc.scalar.activation(window[:, cols, :], raw[:, :, cols].rearrange("p e c -> p c e"), ACT.Copy)
+                    continue
+                nc.sync.dma_start(raw[:], planes[:, 2 * pair : 2 * pair + 2, c0 : c0 + CHUNK])
+                nc.scalar.activation(window[:, c0 : c0 + CHUNK, :], raw[:].rearrange("p e c -> p c e"), ACT.Copy)
+            return window[:].rearrange("p c e -> p (c e)").bitcast(U32)
+
+        nc.sync.dma_start(tail_list[:], offs)
+        nc.sync.dma_start(head_list[:], uoffs)
+        row_scale = [kept([P, PACK], F32, "row_scale%d" % g) for g in range(PASSES)]
+        for g in range(PASSES):
+            nc.sync.dma_start(row_scale[g][:], us[0].rearrange("(g p t) o -> g p (t o)", g=PASSES, t=PACK)[g])
+
+        ts_row = kept([P, N], F32, "ts_row")
+        nc.vector.tensor_copy(ts_row[:], ts_window[:].indirect(tail_list[:]))
+        bank = psum.tile([P, PACK, P], F32, name="side", tag="side")
+        for b in range(PACK):
+            nc.tensor.transpose(bank[:, b, :], ts_row[:, b * P : (b + 1) * P], ident[:])
+        ts_cols = kept([P, PACK, P], F32, "ts_cols")
+        nc.vector.tensor_copy(ts_cols[:], bank[:, :, 0:1].to_broadcast([P, PACK, P]))
+        bank = psum.tile([P, PACK, P], F32, name="side", tag="side")
+        for b in range(PACK):
+            nc.tensor.transpose(bank[:, b, :], ts_cols[:, b, :], ident[:])
+        ts_all = kept([P, N], F32, "ts_all")
+        nc.vector.tensor_copy(ts_all[:], bank[:].rearrange("p b i -> p (b i)"))
+        scale = [kept([P, PACK, N], F32, "scale%d" % g) for g in range(PASSES)]
+        for g in range(PASSES):
+            for t in range(PACK):
+                nc.gpsimd.tensor_scalar(scale[g][:, t, :], ts_all[:], row_scale[g][:, t : t + 1], 0.0, ALU.mult, ALU.add)
+
+        heads = [kept([P, PACK * P * PACK], BF16, "heads%d" % g) for g in range(PASSES)]
+        heads_t = [kept([P, PACK * P * PACK], BF16, "heads_t%d" % g) for g in range(PASSES)]
+        x_codes = [kept([P, N], U32, "x_codes%d" % g) for g in range(PASSES)]
+        x_scales = [kept([P, N], U8, "x_scales%d" % g) for g in range(PASSES)]
+        xt_codes = [kept([P, N], U32, "xt_codes%d" % g) for g in range(PASSES)]
+        xt_scales = [kept([P, N], U8, "xt_scales%d" % g) for g in range(PASSES)]
+        for u in range(2):
+            words = load_pair(u_planes, u, "u_pair%d" % u, u == 0)
+            for g in range(PASSES):
+                dst = heads[g][:].bitcast(U32).rearrange("p (t m u) -> p m t u", t=PACK, u=2)[:, :, :, u]
+                nc.vector.tensor_copy(dst, words.indirect(head_list[:, 32 * g : 32 * (g + 1)]))
+            for g in range(PASSES):
+                src = heads[g][:].bitcast(F32).rearrange("p (t m u) -> p t u m", t=PACK, u=2)
+                bank = psum.tile([P, PACK, P], F32, name="side", tag="side")
+                for t in range(PACK):
+                    nc.tensor.transpose(bank[:, t, :], src[:, t, u, :], ident[:])
+                nc.scalar.copy(
+                    heads_t[g][:, u * 1024 : (u + 1) * 1024].rearrange("m (e p t) -> m e p t", e=2, t=PACK),
+                    bank[:].rearrange("m t p -> m (t p)").bitcast(BF16).rearrange("m (t p e) -> m e p t", t=PACK, e=2),
+                )
+        for g in range(PASSES):
+            nc.vector.quantize_mx(x_codes[g][:].bitcast(E4M3), x_scales[g][:], heads[g][:])
+
+        tails = kept([P, N, PACK], BF16, "tails")
+        words = load_pair(v_planes, 0, "v_pair0")
+        dst = tails[:].rearrange("p i t -> p (i t)").bitcast(U32).rearrange("p (i u) -> p i u", u=2)[:, :, 0]
+        nc.vector.tensor_copy(dst, words.indirect(tail_list[:]))
+        picked = kept([P, 2, N], F32, "picked")
+        for e in range(2):
+            plane = kept([P, T], F32, "v_plane%d" % e)
+            nc.sync.dma_start(plane[:], v_planes[:, 2 + e, :])
+            nc.vector.tensor_copy(picked[:, e, :], plane[:].indirect(tail_list[:]))
+        nc.vector.tensor_copy(tails[:, :, 2:4], picked[:].rearrange("p e i -> p i e"))
+        w_codes = kept([P, N], U32, "w_codes")
+        w_scales = kept([P, N], U8, "w_scales")
+        nc.vector.quantize_mx(w_codes[:].bitcast(E4M3), w_scales[:], tails[:].rearrange("p i t -> p (i t)"))
+        for g in range(PASSES):
+            nc.vector.quantize_mx(xt_codes[g][:].bitcast(E4M3), xt_scales[g][:], heads_t[g][:])
+
+        labels = []
+        for g in range(PASSES):
+            label = stage.tile([P, PACK, N], F32, name="raw", tag="raw")
+            nc.sync.dma_start(label[:], y[0].rearrange("(g p t) i -> g p t i", g=PASSES, t=PACK)[g])
+            labels.append(label)
+
+        h_codes = [kept([P, N], U32, "h_codes%d" % g) for g in range(PASSES)]
+        h_scales = [kept([P, N], U8, "h_scales%d" % g) for g in range(PASSES)]
+        for g in range(PASSES):
+            z = kept([P, PACK, N], F32, "z%d" % g)
+            for t in range(PACK):
+                acc = psum.tile([P, N], F32, name="acc", tag="acc")
+                cols = slice(t * P, (t + 1) * P)
+                nc.tensor.matmul_mx(
+                    out=acc[:], lhsT=x_codes[g][:, cols].bitcast(E4M3), lhsT_scale=x_scales[g][:, cols],
+                    rhs=w_codes[:].bitcast(E4M3), rhs_scale=w_scales[:], start=True, stop=True,
+                )
+                nc.vector.tensor_tensor(z[:, t, :], acc[:], scale[g][:, t, :], ALU.mult)
+                nc.scalar.activation(z[:, t, :], z[:, t, :], ACT.Sigmoid)
+            for t in range(PACK):
+                nc.vector.tensor_tensor(z[:, t, :], z[:, t, :], labels[g][:, t, :], ALU.subtract)
+            h = kept([P, N * PACK], BF16, "h%d" % g)
+            half = N // 2
+            for k in range(2):
+                slots = slice(k * half, (k + 1) * half)
+                nc.vector.tensor_tensor(
+                    h[:, k * half * PACK : (k + 1) * half * PACK].rearrange("p (c i t) -> p c t i", i=4, t=PACK),
+                    z[:, :, slots].rearrange("p t (c i) -> p c t i", i=4),
+                    scale[g][:, :, slots].rearrange("p t (c i) -> p c t i", i=4),
+                    ALU.mult,
+                )
+            for k in range(2):
+                slots = slice(k * half, (k + 1) * half)
+                nc.vector.quantize_mx(
+                    h_codes[g][:, slots].bitcast(E5M2), h_scales[g][:, slots],
+                    h[:, k * half * PACK : (k + 1) * half * PACK],
+                )
+
+        windows = [kept([P, T], F32, "window%d" % td) for td in range(PACK)]
+        for td in range(PACK):
+            for c0 in range(0, T, CHUNK):
+                nc.gpsimd.memset(windows[td][:, c0 : c0 + CHUNK], 0.0)
+        out_planes = out.rearrange("(p t) c -> t p c", t=PACK)
+        for td in range(PACK):
+            acc = psum.tile([P, N], F32, name="side", tag="side")
+            cols = slice(td * P, (td + 1) * P)
+            for g in range(PASSES):
+                nc.tensor.matmul_mx(
+                    out=acc[:], lhsT=xt_codes[g][:, cols].bitcast(E4M3), lhsT_scale=xt_scales[g][:, cols],
+                    rhs=h_codes[g][:].bitcast(E5M2), rhs_scale=h_scales[g][:], start=(g == 0), stop=(g == PASSES - 1),
+                )
+            grad = kept([P, N], F32, "grad%d" % td)
+            nc.scalar.copy(grad[:], acc[:])
+            nc.vector.tensor_copy(windows[td][:].indirect(tail_list[:]), grad[:])
+            nc.sync.dma_start(out_planes[td], windows[td][:])

@@ -26,11 +26,11 @@ def tile_attend_gmf_nce_v_kernel(tc, uT, vT, y, us, ts, offs, uoffs, out):
     nc = tc.nc
     with ExitStack() as ctx:
         keep = ctx.enter_context(tc.tile_pool(name="keep", bufs=1))
-        stage = ctx.enter_context(tc.tile_pool(name="stage", bufs=6))
+        stage = ctx.enter_context(tc.tile_pool(name="stage", bufs=5))
         psum = ctx.enter_context(tc.psum_pool(name="psum", bufs=4))
 
-        def kept(shape, dtype, name):
-            return keep.tile(shape, dtype, name=name, align_bytes=64)
+        def kept(shape, dtype, name, tag=None):
+            return keep.tile(shape, dtype, name=name, tag=tag or name, align_bytes=64)
 
         tail_list = kept([P, N // 16], U16, "tail_list")
         head_list = kept([P, R // 16], U16, "head_list")
@@ -45,39 +45,52 @@ def tile_attend_gmf_nce_v_kernel(tc, uT, vT, y, us, ts, offs, uoffs, out):
         nc.gpsimd.memset(ts_window[:, CHUNK:], 0.0)
         ident = kept([P, P], F32, "ident")
         make_identity(nc, ident[:])
-        nc.sync.dma_start(ts_window[0:1, :], ts[0:1, :])
 
-        def load_pair(planes, pair, name, fine=False):
+        def load_chunk(planes, pair, c0, fine):
+            raw = stage.tile([P, 2, CHUNK], F32, name="raw", tag="raw")
+            if fine:
+                for h0 in range(0, CHUNK, CHUNK // 2):
+                    for e in range(2):
+                        nc.sync.dma_start(raw[:, e, h0 : h0 + CHUNK // 2], planes[:, 2 * pair + e, c0 + h0 : c0 + h0 + CHUNK // 2])
+            else:
+                nc.sync.dma_start(raw[:], planes[:, 2 * pair : 2 * pair + 2, c0 : c0 + CHUNK])
+            return raw
+
+        def cast(window, raw, c0, shared):
+            for k in range(2):
+                cols = slice(k * CHUNK // 2, (k + 1) * CHUNK // 2)
+                dst = window[:, c0 + cols.start : c0 + cols.stop, :]
+                src = raw[:, :, cols].rearrange("p e c -> p c e")
+                if shared and k == 1:
+                    nc.vector.tensor_copy(dst, src)
+                else:
+                    nc.scalar.activation(dst, src, ACT.Copy)
+
+        def load_pair(planes, pair, name, first=None, shared=False):
             window = kept([P, T, 2], BF16, name)
             for c0 in range(0, T, CHUNK):
-                raw = stage.tile([P, 2, CHUNK], F32, name="raw", tag="raw")
-                if fine and c0 == 0:
-                    for h0 in range(0, CHUNK, CHUNK // 2):
-                        cols = slice(h0, h0 + CHUNK // 2)
-                        for e in range(2):
-                            nc.sync.dma_start(raw[:, e, cols], planes[:, 2 * pair + e, cols])
-                        nc.scalar.activation(window[:, cols, :], raw[:, :, cols].rearrange("p e c -> p c e"), ACT.Copy)
-                    continue
-                nc.sync.dma_start(raw[:], planes[:, 2 * pair : 2 * pair + 2, c0 : c0 + CHUNK])
-                nc.scalar.activation(window[:, c0 : c0 + CHUNK, :], raw[:].rearrange("p e c -> p c e"), ACT.Copy)
+                raw = first if (first is not None and c0 == 0) else load_chunk(planes, pair, c0, False)
+                cast(window, raw, c0, shared and c0 + CHUNK == T)
             return window[:].rearrange("p c e -> p (c e)").bitcast(U32)
 
+        first_chunk = load_chunk(u_planes, 0, 0, True)
         nc.sync.dma_start(tail_list[:], offs)
         nc.sync.dma_start(head_list[:], uoffs)
         row_scale = [kept([P, PACK], F32, "row_scale%d" % g) for g in range(PASSES)]
         for g in range(PASSES):
             nc.sync.dma_start(row_scale[g][:], us[0].rearrange("(g p t) o -> g p (t o)", g=PASSES, t=PACK)[g])
+        nc.sync.dma_start(ts_window[0:1, :], ts[0:1, :])
 
         ts_row = kept([P, N], F32, "ts_row")
         nc.vector.tensor_copy(ts_row[:], ts_window[:].indirect(tail_list[:]))
         bank = psum.tile([P, PACK, P], F32, name="side", tag="side")
         for b in range(PACK):
             nc.tensor.transpose(bank[:, b, :], ts_row[:, b * P : (b + 1) * P], ident[:])
-        ts_cols = kept([P, PACK, P], F32, "ts_cols")
-        nc.vector.tensor_copy(ts_cols[:], bank[:, :, 0:1].to_broadcast([P, PACK, P]))
+        ts_cols = kept([P, PACK], F32, "ts_cols")
+        nc.vector.tensor_copy(ts_cols[:], bank[:, :, 0])
         bank = psum.tile([P, PACK, P], F32, name="side", tag="side")
         for b in range(PACK):
-            nc.tensor.transpose(bank[:, b, :], ts_cols[:, b, :], ident[:])
+            nc.tensor.transpose(bank[:, b, :], ts_cols[:, b : b + 1].to_broadcast([P, P]), ident[:])
         ts_all = kept([P, N], F32, "ts_all")
         nc.vector.tensor_copy(ts_all[:], bank[:].rearrange("p b i -> p (b i)"))
         scale = [kept([P, PACK, N], F32, "scale%d" % g) for g in range(PASSES)]
@@ -91,20 +104,16 @@ def tile_attend_gmf_nce_v_kernel(tc, uT, vT, y, us, ts, offs, uoffs, out):
         x_scales = [kept([P, N], U8, "x_scales%d" % g) for g in range(PASSES)]
         xt_codes = [kept([P, N], U32, "xt_codes%d" % g) for g in range(PASSES)]
         xt_scales = [kept([P, N], U8, "xt_scales%d" % g) for g in range(PASSES)]
+        pairs = [kept([P, 2, N * 2], BF16, "pairs%d" % g) for g in range(PASSES)]
         for u in range(2):
-            words = load_pair(u_planes, u, "u_pair%d" % u, u == 0)
+            words = load_pair(u_planes, u, "u_pair%d" % u, first_chunk if u == 0 else None, u == 1)
             for g in range(PASSES):
-                dst = heads[g][:].bitcast(U32).rearrange("p (t m u) -> p m t u", t=PACK, u=2)[:, :, :, u]
-                nc.vector.tensor_copy(dst, words.indirect(head_list[:, 32 * g : 32 * (g + 1)]))
-            for g in range(PASSES):
-                src = heads[g][:].bitcast(F32).rearrange("p (t m u) -> p t u m", t=PACK, u=2)
-                bank = psum.tile([P, PACK, P], F32, name="side", tag="side")
-                for t in range(PACK):
-                    nc.tensor.transpose(bank[:, t, :], src[:, t, u, :], ident[:])
-                nc.scalar.copy(
-                    heads_t[g][:, u * 1024 : (u + 1) * 1024].rearrange("m (e p t) -> m e p t", e=2, t=PACK),
-                    bank[:].rearrange("m t p -> m (t p)").bitcast(BF16).rearrange("m (t p e) -> m e p t", t=PACK, e=2),
-                )
+                nc.vector.tensor_copy(pairs[g][:, u, :].bitcast(U32), words.indirect(head_list[:, 32 * g : 32 * (g + 1)]))
+        for g in range(PASSES):
+            nc.vector.tensor_copy(
+                heads[g][:].bitcast(F32).rearrange("p (t m u) -> p m t u", t=PACK, u=2),
+                pairs[g][:].rearrange("p u w -> p (u w)").bitcast(F32).rearrange("p (u m t) -> p m t u", t=PACK, u=2),
+            )
         for g in range(PASSES):
             nc.vector.quantize_mx(x_codes[g][:].bitcast(E4M3), x_scales[g][:], heads[g][:])
 
@@ -122,6 +131,15 @@ def tile_attend_gmf_nce_v_kernel(tc, uT, vT, y, us, ts, offs, uoffs, out):
         w_scales = kept([P, N], U8, "w_scales")
         nc.vector.quantize_mx(w_codes[:].bitcast(E4M3), w_scales[:], tails[:].rearrange("p i t -> p (i t)"))
         for g in range(PASSES):
+            src = heads[g][:].bitcast(F32).rearrange("p (t m u) -> p t u m", t=PACK, u=2)
+            for u in range(2):
+                bank = psum.tile([P, PACK, P], F32, name="side", tag="side")
+                for t in range(PACK):
+                    nc.tensor.transpose(bank[:, t, :], src[:, t, u, :], ident[:])
+                nc.scalar.copy(
+                    heads_t[g][:, u * 1024 : (u + 1) * 1024].rearrange("m (e p t) -> m e p t", e=2, t=PACK),
+                    bank[:].rearrange("m t p -> m (t p)").bitcast(BF16).rearrange("m (t p e) -> m e p t", t=PACK, e=2),
+                )
             nc.vector.quantize_mx(xt_codes[g][:].bitcast(E4M3), xt_scales[g][:], heads_t[g][:])
 
         labels = []
@@ -134,15 +152,31 @@ def tile_attend_gmf_nce_v_kernel(tc, uT, vT, y, us, ts, offs, uoffs, out):
         h_scales = [kept([P, N], U8, "h_scales%d" % g) for g in range(PASSES)]
         for g in range(PASSES):
             z = kept([P, PACK, N], F32, "z%d" % g)
-            for t in range(PACK):
-                acc = psum.tile([P, N], F32, name="acc", tag="acc")
-                cols = slice(t * P, (t + 1) * P)
-                nc.tensor.matmul_mx(
-                    out=acc[:], lhsT=x_codes[g][:, cols].bitcast(E4M3), lhsT_scale=x_scales[g][:, cols],
-                    rhs=w_codes[:].bitcast(E4M3), rhs_scale=w_scales[:], start=True, stop=True,
-                )
-                nc.vector.tensor_tensor(z[:, t, :], acc[:], scale[g][:, t, :], ALU.mult)
-                nc.scalar.activation(z[:, t, :], z[:, t, :], ACT.Sigmoid)
+            if g == 0:
+                for t in range(PACK):
+                    acc = psum.tile([P, N], F32, name="acc", tag="acc")
+                    cols = slice(t * P, (t + 1) * P)
+                    nc.tensor.matmul_mx(
+                        out=acc[:], lhsT=x_codes[g][:, cols].bitcast(E4M3), lhsT_scale=x_scales[g][:, cols],
+                        rhs=w_codes[:].bitcast(E4M3), rhs_scale=w_scales[:], start=True, stop=True,
+                    )
+                    nc.vector.tensor_tensor(z[:, t, :], acc[:], scale[g][:, t, :], ALU.mult)
+                    nc.scalar.activation(z[:, t, :], z[:, t, :], ACT.Sigmoid)
+            else:
+                turned = kept([P, PACK, N], F32, "turned", "ts_window")
+                for b in range(PACK):
+                    acc = psum.tile([P, N], F32, name="side", tag="side")
+                    cols = slice(b * P, (b + 1) * P)
+                    nc.tensor.matmul_mx(
+                        out=acc[:], lhsT=w_codes[:, cols].bitcast(E4M3), lhsT_scale=w_scales[:, cols],
+                        rhs=x_codes[g][:].bitcast(E4M3), rhs_scale=x_scales[g][:], start=True, stop=True,
+                    )
+                    nc.scalar.activation(turned[:, b, :], acc[:], ACT.Copy, scale=ts_cols[:, b : b + 1])
+                for t in range(PACK):
+                    acc = psum.tile([P, N], F32, name="acc", tag="acc")
+                    for b in range(PACK):
+                        nc.tensor.transpose(acc[:, b * P : (b + 1) * P], turned[:, b, t * P : (t + 1) * P], ident[:])
+                    nc.scalar.activation(z[:, t, :], acc[:], ACT.Sigmoid, scale=row_scale[g][:, t : t + 1])
             for t in range(PACK):
                 nc.vector.tensor_tensor(z[:, t, :], z[:, t, :], labels[g][:, t, :], ALU.subtract)
             h = kept([P, N * PACK], BF16, "h%d" % g)
@@ -162,10 +196,10 @@ def tile_attend_gmf_nce_v_kernel(tc, uT, vT, y, us, ts, offs, uoffs, out):
                     h[:, k * half * PACK : (k + 1) * half * PACK],
                 )
 
-        windows = [kept([P, T], F32, "window%d" % td) for td in range(PACK)]
+        windows = [kept([P, T], F32, "window%d" % td, tag) for td, tag in enumerate((None, "tails", "x_codes0", "x_codes1"))]
         for td in range(PACK):
-            for c0 in range(0, T, CHUNK):
-                nc.gpsimd.memset(windows[td][:, c0 : c0 + CHUNK], 0.0)
+            for c0 in range(0, T, N):
+                nc.gpsimd.memset(windows[td][:, c0 : c0 + N], 0.0)
         out_planes = out.rearrange("(p t) c -> t p c", t=PACK)
         for td in range(PACK):
             acc = psum.tile([P, N], F32, name="side", tag="side")

@@ -8,7 +8,6 @@ BF16 = mybir.dt.bfloat16
 U32 = mybir.dt.uint32
 U16 = mybir.dt.uint16
 U8 = mybir.dt.uint8
-I32 = mybir.dt.int32
 E4M3 = mybir.dt.float8_e4m3fn_x4
 E5M2 = mybir.dt.float8_e5m2_x4
 ACT = mybir.ActivationFunctionType
@@ -17,8 +16,10 @@ ALU = mybir.AluOpType
 P = 128
 D, R, N, T = 512, 1024, 512, 2048
 PACK = 4
-PASSES = R // (P * PACK)
-CHUNK = 1024
+K = P * PACK
+PASSES = R // K
+BLOCKS = N // P
+HALF = N // 2
 FLOPS = 2 * 2 * D * R * N
 
 
@@ -26,183 +27,179 @@ def tile_attend_gmf_nce_v_kernel(tc, uT, vT, y, us, ts, offs, uoffs, out):
     nc = tc.nc
     with ExitStack() as ctx:
         keep = ctx.enter_context(tc.tile_pool(name="keep", bufs=1))
-        stage = ctx.enter_context(tc.tile_pool(name="stage", bufs=5))
-        psum = ctx.enter_context(tc.psum_pool(name="psum", bufs=4))
+        stage = ctx.enter_context(tc.tile_pool(name="stage", bufs=8))
+        ring = ctx.enter_context(tc.tile_pool(name="ring", bufs=4))
+        psum = ctx.enter_context(tc.psum_pool(name="psum", bufs=2))
+        psum_out = ctx.enter_context(tc.psum_pool(name="psum_out", bufs=4))
 
         def kept(shape, dtype, name, tag=None):
             return keep.tile(shape, dtype, name=name, tag=tag or name, align_bytes=64)
 
         tail_list = kept([P, N // 16], U16, "tail_list")
         head_list = kept([P, R // 16], U16, "head_list")
-        u_planes = uT.rearrange("(p t) c -> p t c", t=PACK)
-        v_planes = vT.rearrange("(p t) c -> p t c", t=PACK)
+        u_planes = uT.rearrange("(p t) c -> t p c", t=PACK)
+        v_planes = vT.rearrange("(p t) c -> t p c", t=PACK)
 
-        ts_window = kept([P, T], F32, "ts_window")
         warm = kept([P, 2], F32, "warm")
         nc.vector.memset(warm[:, 0:1], 0.0)
         nc.scalar.activation(warm[:, 1:2], warm[:, 0:1], ACT.Sigmoid)
-        nc.vector.memset(ts_window[:, :CHUNK], 0.0)
-        nc.gpsimd.memset(ts_window[:, CHUNK:], 0.0)
         ident = kept([P, P], F32, "ident")
         make_identity(nc, ident[:])
-
-        def load_chunk(planes, pair, c0, fine):
-            raw = stage.tile([P, 2, CHUNK], F32, name="raw", tag="raw")
-            if fine:
-                for h0 in range(0, CHUNK, CHUNK // 2):
-                    for e in range(2):
-                        nc.sync.dma_start(raw[:, e, h0 : h0 + CHUNK // 2], planes[:, 2 * pair + e, c0 + h0 : c0 + h0 + CHUNK // 2])
-            else:
-                nc.sync.dma_start(raw[:], planes[:, 2 * pair : 2 * pair + 2, c0 : c0 + CHUNK])
-            return raw
-
-        def cast(window, raw, c0, shared):
-            for k in range(2):
-                cols = slice(k * CHUNK // 2, (k + 1) * CHUNK // 2)
-                dst = window[:, c0 + cols.start : c0 + cols.stop, :]
-                src = raw[:, :, cols].rearrange("p e c -> p c e")
-                if shared and k == 1:
-                    nc.vector.tensor_copy(dst, src)
-                else:
-                    nc.scalar.activation(dst, src, ACT.Copy)
-
-        def load_pair(planes, pair, name, first=None, shared=False):
-            window = kept([P, T, 2], BF16, name)
-            for c0 in range(0, T, CHUNK):
-                raw = first if (first is not None and c0 == 0) else load_chunk(planes, pair, c0, False)
-                cast(window, raw, c0, shared and c0 + CHUNK == T)
-            return window[:].rearrange("p c e -> p (c e)").bitcast(U32)
-
-        first_chunk = load_chunk(u_planes, 0, 0, True)
-        nc.sync.dma_start(tail_list[:], offs)
-        nc.sync.dma_start(head_list[:], uoffs)
-        row_scale = [kept([P, PACK], F32, "row_scale%d" % g) for g in range(PASSES)]
-        for g in range(PASSES):
-            nc.sync.dma_start(row_scale[g][:], us[0].rearrange("(g p t) o -> g p (t o)", g=PASSES, t=PACK)[g])
-        nc.sync.dma_start(ts_window[0:1, :], ts[0:1, :])
-
-        ts_row = kept([P, N], F32, "ts_row")
-        nc.vector.tensor_copy(ts_row[:], ts_window[:].indirect(tail_list[:]))
-        bank = psum.tile([P, PACK, P], F32, name="side", tag="side")
-        for b in range(PACK):
-            nc.tensor.transpose(bank[:, b, :], ts_row[:, b * P : (b + 1) * P], ident[:])
-        ts_cols = kept([P, PACK], F32, "ts_cols")
-        nc.vector.tensor_copy(ts_cols[:], bank[:, :, 0])
-        bank = psum.tile([P, PACK, P], F32, name="side", tag="side")
-        for b in range(PACK):
-            nc.tensor.transpose(bank[:, b, :], ts_cols[:, b : b + 1].to_broadcast([P, P]), ident[:])
-        ts_all = kept([P, N], F32, "ts_all")
-        nc.vector.tensor_copy(ts_all[:], bank[:].rearrange("p b i -> p (b i)"))
-        scale = [kept([P, PACK, N], F32, "scale%d" % g) for g in range(PASSES)]
-        for g in range(PASSES):
-            for t in range(PACK):
-                nc.gpsimd.tensor_scalar(scale[g][:, t, :], ts_all[:], row_scale[g][:, t : t + 1], 0.0, ALU.mult, ALU.add)
-
-        heads = [kept([P, PACK * P * PACK], BF16, "heads%d" % g) for g in range(PASSES)]
-        heads_t = [kept([P, PACK * P * PACK], BF16, "heads_t%d" % g) for g in range(PASSES)]
-        x_codes = [kept([P, N], U32, "x_codes%d" % g) for g in range(PASSES)]
-        x_scales = [kept([P, N], U8, "x_scales%d" % g) for g in range(PASSES)]
-        xt_codes = [kept([P, N], U32, "xt_codes%d" % g) for g in range(PASSES)]
-        xt_scales = [kept([P, N], U8, "xt_scales%d" % g) for g in range(PASSES)]
-        pairs = [kept([P, 2, N * 2], BF16, "pairs%d" % g) for g in range(PASSES)]
-        for u in range(2):
-            words = load_pair(u_planes, u, "u_pair%d" % u, first_chunk if u == 0 else None, u == 1)
-            for g in range(PASSES):
-                nc.vector.tensor_copy(pairs[g][:, u, :].bitcast(U32), words.indirect(head_list[:, 32 * g : 32 * (g + 1)]))
-        for g in range(PASSES):
-            nc.vector.tensor_copy(
-                heads[g][:].bitcast(F32).rearrange("p (t m u) -> p m t u", t=PACK, u=2),
-                pairs[g][:].rearrange("p u w -> p (u w)").bitcast(F32).rearrange("p (u m t) -> p m t u", t=PACK, u=2),
-            )
-        for g in range(PASSES):
-            nc.vector.quantize_mx(x_codes[g][:].bitcast(E4M3), x_scales[g][:], heads[g][:])
-
-        tails = kept([P, N, PACK], BF16, "tails")
-        words = load_pair(v_planes, 0, "v_pair0")
-        dst = tails[:].rearrange("p i t -> p (i t)").bitcast(U32).rearrange("p (i u) -> p i u", u=2)[:, :, 0]
-        nc.vector.tensor_copy(dst, words.indirect(tail_list[:]))
-        picked = kept([P, 2, N], F32, "picked")
-        for e in range(2):
-            plane = kept([P, T], F32, "v_plane%d" % e)
-            nc.sync.dma_start(plane[:], v_planes[:, 2 + e, :])
-            nc.vector.tensor_copy(picked[:, e, :], plane[:].indirect(tail_list[:]))
-        nc.vector.tensor_copy(tails[:, :, 2:4], picked[:].rearrange("p e i -> p i e"))
-        w_codes = kept([P, N], U32, "w_codes")
-        w_scales = kept([P, N], U8, "w_scales")
-        nc.vector.quantize_mx(w_codes[:].bitcast(E4M3), w_scales[:], tails[:].rearrange("p i t -> p (i t)"))
-        for g in range(PASSES):
-            src = heads[g][:].bitcast(F32).rearrange("p (t m u) -> p t u m", t=PACK, u=2)
-            for u in range(2):
-                bank = psum.tile([P, PACK, P], F32, name="side", tag="side")
-                for t in range(PACK):
-                    nc.tensor.transpose(bank[:, t, :], src[:, t, u, :], ident[:])
-                nc.scalar.copy(
-                    heads_t[g][:, u * 1024 : (u + 1) * 1024].rearrange("m (e p t) -> m e p t", e=2, t=PACK),
-                    bank[:].rearrange("m t p -> m (t p)").bitcast(BF16).rearrange("m (t p e) -> m e p t", t=PACK, e=2),
-                )
-            nc.vector.quantize_mx(xt_codes[g][:].bitcast(E4M3), xt_scales[g][:], heads_t[g][:])
-
-        labels = []
-        for g in range(PASSES):
-            label = stage.tile([P, PACK, N], F32, name="raw", tag="raw")
-            nc.sync.dma_start(label[:], y[0].rearrange("(g p t) i -> g p t i", g=PASSES, t=PACK)[g])
-            labels.append(label)
-
-        h_codes = [kept([P, N], U32, "h_codes%d" % g) for g in range(PASSES)]
-        h_scales = [kept([P, N], U8, "h_scales%d" % g) for g in range(PASSES)]
-        for g in range(PASSES):
-            z = kept([P, PACK, N], F32, "z%d" % g)
-            if g == 0:
-                for t in range(PACK):
-                    acc = psum.tile([P, N], F32, name="acc", tag="acc")
-                    cols = slice(t * P, (t + 1) * P)
-                    nc.tensor.matmul_mx(
-                        out=acc[:], lhsT=x_codes[g][:, cols].bitcast(E4M3), lhsT_scale=x_scales[g][:, cols],
-                        rhs=w_codes[:].bitcast(E4M3), rhs_scale=w_scales[:], start=True, stop=True,
-                    )
-                    nc.vector.tensor_tensor(z[:, t, :], acc[:], scale[g][:, t, :], ALU.mult)
-                    nc.scalar.activation(z[:, t, :], z[:, t, :], ACT.Sigmoid)
-            else:
-                turned = kept([P, PACK, N], F32, "turned", "ts_window")
-                for b in range(PACK):
-                    acc = psum.tile([P, N], F32, name="side", tag="side")
-                    cols = slice(b * P, (b + 1) * P)
-                    nc.tensor.matmul_mx(
-                        out=acc[:], lhsT=w_codes[:, cols].bitcast(E4M3), lhsT_scale=w_scales[:, cols],
-                        rhs=x_codes[g][:].bitcast(E4M3), rhs_scale=x_scales[g][:], start=True, stop=True,
-                    )
-                    nc.scalar.activation(turned[:, b, :], acc[:], ACT.Copy, scale=ts_cols[:, b : b + 1])
-                for t in range(PACK):
-                    acc = psum.tile([P, N], F32, name="acc", tag="acc")
-                    for b in range(PACK):
-                        nc.tensor.transpose(acc[:, b * P : (b + 1) * P], turned[:, b, t * P : (t + 1) * P], ident[:])
-                    nc.scalar.activation(z[:, t, :], acc[:], ACT.Sigmoid, scale=row_scale[g][:, t : t + 1])
-            for t in range(PACK):
-                nc.vector.tensor_tensor(z[:, t, :], z[:, t, :], labels[g][:, t, :], ALU.subtract)
-            h = kept([P, N * PACK], BF16, "h%d" % g)
-            half = N // 2
-            for k in range(2):
-                slots = slice(k * half, (k + 1) * half)
-                nc.vector.tensor_tensor(
-                    h[:, k * half * PACK : (k + 1) * half * PACK].rearrange("p (c i t) -> p c t i", i=4, t=PACK),
-                    z[:, :, slots].rearrange("p t (c i) -> p c t i", i=4),
-                    scale[g][:, :, slots].rearrange("p t (c i) -> p c t i", i=4),
-                    ALU.mult,
-                )
-            for k in range(2):
-                slots = slice(k * half, (k + 1) * half)
-                nc.vector.quantize_mx(
-                    h_codes[g][:, slots].bitcast(E5M2), h_scales[g][:, slots],
-                    h[:, k * half * PACK : (k + 1) * half * PACK],
-                )
-
-        windows = [kept([P, T], F32, "window%d" % td, tag) for td, tag in enumerate((None, "tails", "x_codes0", "x_codes1"))]
+        windows = [kept([P, T], F32, "window%d" % td) for td in range(PACK)]
         for td in range(PACK):
             for c0 in range(0, T, N):
                 nc.gpsimd.memset(windows[td][:, c0 : c0 + N], 0.0)
+
+        nc.sync.dma_start(tail_list[:], offs)
+        nc.sync.dma_start(head_list[:], uoffs)
+        ts_folded = kept([P, T // P], F32, "ts_folded")
+        nc.scalar.dma_start(ts_folded[:], ts[0].rearrange("(p j) -> p j", p=P))
+        row_scale = kept([P, PASSES, PACK], F32, "row_scale")
+        nc.scalar.dma_start(row_scale[:], us[0].rearrange("(g p t) o -> p g (t o)", g=PASSES, t=PACK))
+
+        def load(source):
+            tile = stage.tile([P, T], F32, name="raw", tag="raw")
+            nc.sync.dma_start(tile[:], source)
+            return tile
+
+        u_raw = [load(u_planes[td]) for td in range(PACK)]
+        v_raw = [load(v_planes[td]) for td in range(PACK)]
+
+        ts_cols = kept([P, BLOCKS], F32, "ts_cols")
+        scale = [kept([P, PACK, N], F32, "scale%d" % g) for g in range(PASSES)]
+
+        ts_window = kept([P, T], F32, "ts_window")
+        for a in range(T // N):
+            bank = psum_out.tile([P, PACK, P], F32, name="wide", tag="wide")
+            for j in range(PACK):
+                column = PACK * a + j
+                nc.tensor.transpose(bank[:, j, :], ts_folded[:, column : column + 1].to_broadcast([P, P]), ident[:])
+            nc.scalar.activation(
+                ts_window[:].rearrange("q (p a j) -> q a p j", a=T // N, j=PACK)[:, a], bank[:].rearrange("q j p -> q p j"), ACT.Copy
+            )
+        ts_all = kept([P, N], F32, "ts_all")
+        nc.vector.tensor_copy(ts_all[:], ts_window[:].indirect(tail_list[:]))
+        for g in range(PASSES):
+            for t in range(PACK):
+                nc.gpsimd.tensor_scalar(scale[g][:, t, :], ts_all[:], row_scale[:, g, t : t + 1], 0.0, ALU.mult, ALU.add)
+        bank = psum.tile([P, BLOCKS, P], F32, name="score", tag="score")
+        for b in range(BLOCKS):
+            nc.tensor.transpose(bank[:, b, :], ts_all[:, b * P : (b + 1) * P], ident[:])
+        nc.scalar.copy(ts_cols[:], bank[:, :, 0])
+
+        heads = [kept([P, PACK * K], BF16, "heads%d" % g) for g in range(PASSES)]
+        heads_t = kept([P, PASSES * D * PACK], BF16, "heads_t")
+        heads_t_words = heads_t[:].bitcast(F32).rearrange("m (g d p u) -> m d g p u", g=PASSES, d=PACK, u=2)
+
+        def turn_heads(td):
+            bank = psum_out.tile([P, PASSES, 2, P], F32, name="wide", tag="wide")
+            for g in range(PASSES):
+                words = heads[g][:, td * K : (td + 1) * K].bitcast(F32)
+                for u in range(2):
+                    nc.tensor.transpose(bank[:, g, u, :], words[:, u : K // 2 : 2], ident[:])
+            nc.scalar.copy(heads_t_words[:, td], bank[:].rearrange("m g u p -> m g p u"))
+
+        for td in range(PACK):
+            for g in range(PASSES):
+                nc.vector.tensor_copy(heads[g][:, td * K : (td + 1) * K], u_raw[td][:].indirect(head_list[:, 32 * g : 32 * (g + 1)]))
+            if td < PACK - 1:
+                turn_heads(td)
+        x_scales = [kept([P, K], U8, "x_scales%d" % g) for g in range(PASSES)]
+        woven = [kept([P, K * PACK], BF16, "woven%d" % g) for g in range(PASSES)]
+        for g in range(PASSES):
+            nc.scalar.copy(
+                woven[g][:].rearrange("p (t c e d) -> p c t e d", t=PACK, e=2, d=PACK),
+                heads[g][:].rearrange("p (d c e t) -> p c t e d", d=PACK, e=2, t=PACK),
+            )
+        turn_heads(PACK - 1)
+        x_first = kept([P, K], U32, "x_first")
+        nc.vector.quantize_mx(x_first[:].bitcast(E4M3), x_scales[0][:], woven[0][:])
+
+        tails = kept([P, N * PACK], BF16, "tails")
+        places = tails[:].rearrange("p (i d) -> p i d", d=PACK)
+        for td in range(2):
+            nc.vector.tensor_copy(places[:, :, td], v_raw[td][:].indirect(tail_list[:]))
+        picked = kept([P, N], BF16, "picked", "woven0")
+        nc.vector.tensor_copy(picked[:], v_raw[2][:].indirect(tail_list[:]))
+        nc.vector.tensor_copy(places[:, :, 2], picked[:])
+        xt_scales = [kept([P, D], U8, "xt_scales%d" % g) for g in range(PASSES)]
+        w_codes = kept([P, N], U32, "w_codes")
+        w_scales = kept([P, N], U8, "w_scales")
+        for k in range(2):
+            slots = slice(k * HALF, (k + 1) * HALF)
+            nc.vector.tensor_copy(places[:, slots, 3], v_raw[3][:].indirect(tail_list[:, 16 * k : 16 * (k + 1)]))
+        for k in range(2):
+            slots = slice(k * HALF, (k + 1) * HALF)
+            nc.vector.quantize_mx(w_codes[:, slots].bitcast(E4M3), w_scales[:, slots], tails[:, k * HALF * PACK : (k + 1) * HALF * PACK])
+        late = kept([P, 3 * K], U32, "late", "tails")
+        x_codes = [x_first[:], late[:, 0:K]]
+        xt_codes = [late[:, K : 2 * K], late[:, 2 * K :]]
+        nc.vector.quantize_mx(x_codes[1].bitcast(E4M3), x_scales[1][:], woven[1][:])
+        for g in range(PASSES):
+            nc.vector.quantize_mx(xt_codes[g].bitcast(E4M3), xt_scales[g][:], heads_t[:, g * D * PACK : (g + 1) * D * PACK])
+
+        labels = [load(y[0].rearrange("(g p t) i -> g p (t i)", g=PASSES, t=PACK)[g]) for g in range(PASSES)]
+
+        h_codes = [kept([P, N], U32, "h_codes%d" % g) for g in range(PASSES)]
+        h_scales = [kept([P, N], U8, "h_scales%d" % g) for g in range(PASSES)]
+        h = [kept([P, N * PACK], BF16, "h%d" % g) for g in range(PASSES)]
+        steps = [(g, k) for g in range(PASSES) for k in range(2)]
+        z = [kept([P, PACK, HALF], F32, "z%d" % n) for n in range(len(steps))]
+
+        def logistic(n, j):
+            g, k = steps[n]
+            b = 2 * k + j
+            slots = slice(b * P, (b + 1) * P)
+            acc = psum.tile([P, K], F32, name="score", tag="score")
+            nc.tensor.matmul_mx(
+                out=acc[:], lhsT=w_codes[:, slots].bitcast(E4M3), lhsT_scale=w_scales[:, slots],
+                rhs=x_codes[g].bitcast(E4M3), rhs_scale=x_scales[g][:], start=True, stop=True,
+            )
+            turned = ring.tile([P, K], F32, name="turned", tag="turned")
+            nc.scalar.activation(turned[:], acc[:], ACT.Copy, scale=ts_cols[:, b : b + 1])
+            acc = psum.tile([P, PACK, P], F32, name="turn", tag="turn")
+            for t in range(PACK):
+                nc.tensor.transpose(acc[:, t, :], turned[:, t * P : (t + 1) * P], ident[:])
+            for t in range(PACK):
+                nc.scalar.activation(z[n][:, t, j * P : (j + 1) * P], acc[:, t, :], ACT.Sigmoid, scale=row_scale[:, g, t : t + 1])
+
+        def residual(n):
+            g, k = steps[n]
+            label = labels[g][:].rearrange("p (t i) -> p t i", t=PACK)
+            for j in range(2):
+                logistic(n, j)
+                b = 2 * k + j
+                cols = z[n][:, :, j * P : (j + 1) * P]
+                nc.vector.tensor_tensor(cols, cols, label[:, :, b * P : (b + 1) * P], ALU.subtract)
+
+        def pieces(n):
+            g, k = steps[n]
+            width = P if n == len(steps) - 1 else HALF
+            return [(g, c0, k * HALF + c0, width) for c0 in range(0, HALF, width)]
+
+        def weigh(n):
+            for g, c0, i0, width in pieces(n):
+                nc.vector.tensor_tensor(
+                    h[g][:, i0 * PACK : (i0 + width) * PACK].rearrange("p (c i t) -> p c t i", i=4, t=PACK),
+                    z[n][:, :, c0 : c0 + width].rearrange("p t (c i) -> p c t i", i=4),
+                    scale[g][:, :, i0 : i0 + width].rearrange("p t (c i) -> p c t i", i=4),
+                    ALU.mult,
+                )
+
+        def quantise(n):
+            for g, c0, i0, width in pieces(n):
+                slots = slice(i0, i0 + width)
+                nc.vector.quantize_mx(h_codes[g][:, slots].bitcast(E5M2), h_scales[g][:, slots], h[g][:, i0 * PACK : (i0 + width) * PACK])
+
+        stages = (residual, weigh, quantise)
+        for step in range(len(steps) + len(stages) - 1):
+            for lag, stage_of in enumerate(stages):
+                if 0 <= step - lag < len(steps):
+                    stage_of(step - lag)
+
         out_planes = out.rearrange("(p t) c -> t p c", t=PACK)
         for td in range(PACK):
-            acc = psum.tile([P, N], F32, name="side", tag="side")
+            acc = psum_out.tile([P, N], F32, name="wide", tag="wide")
             cols = slice(td * P, (td + 1) * P)
             for g in range(PASSES):
                 nc.tensor.matmul_mx(

@@ -6,6 +6,7 @@ from concourse.masks import make_identity
 F32 = mybir.dt.float32
 BF16 = mybir.dt.bfloat16
 U32 = mybir.dt.uint32
+I32 = mybir.dt.int32
 U16 = mybir.dt.uint16
 U8 = mybir.dt.uint8
 E4M3 = mybir.dt.float8_e4m3fn_x4
@@ -47,8 +48,7 @@ def tile_attend_gmf_nce_v_kernel(tc, uT, vT, y, us, ts, offs, uoffs, out):
         make_identity(nc, ident[:])
         windows = [kept([P, T], F32, "window%d" % td) for td in range(PACK)]
         for td in range(PACK):
-            for c0 in range(0, T, N):
-                nc.gpsimd.memset(windows[td][:, c0 : c0 + N], 0.0)
+            nc.vector.memset(windows[td][:].bitcast(I32), 0)
 
         nc.sync.dma_start(tail_list[:], offs)
         nc.sync.dma_start(head_list[:], uoffs)
@@ -77,15 +77,17 @@ def tile_attend_gmf_nce_v_kernel(tc, uT, vT, y, us, ts, offs, uoffs, out):
             nc.scalar.activation(
                 ts_window[:].rearrange("q (p a j) -> q a p j", a=T // N, j=PACK)[:, a], bank[:].rearrange("q j p -> q p j"), ACT.Copy
             )
-        ts_all = kept([P, N], F32, "ts_all")
-        nc.vector.tensor_copy(ts_all[:], ts_window[:].indirect(tail_list[:]))
-        for g in range(PASSES):
-            for t in range(PACK):
-                nc.gpsimd.tensor_scalar(scale[g][:, t, :], ts_all[:], row_scale[:, g, t : t + 1], 0.0, ALU.mult, ALU.add)
-        bank = psum.tile([P, BLOCKS, P], F32, name="score", tag="score")
-        for b in range(BLOCKS):
-            nc.tensor.transpose(bank[:, b, :], ts_all[:, b * P : (b + 1) * P], ident[:])
-        nc.scalar.copy(ts_cols[:], bank[:, :, 0])
+
+        def spread_scales():
+            ts_all = kept([P, N], F32, "ts_all")
+            nc.vector.tensor_copy(ts_all[:], ts_window[:].indirect(tail_list[:]))
+            for g in range(PASSES):
+                for t in range(PACK):
+                    nc.scalar.activation(scale[g][:, t, :], ts_all[:], ACT.Copy, scale=row_scale[:, g, t : t + 1])
+            bank = psum.tile([P, BLOCKS, P], F32, name="score", tag="score")
+            for b in range(BLOCKS):
+                nc.tensor.transpose(bank[:, b, :], ts_all[:, b * P : (b + 1) * P], ident[:])
+            nc.scalar.copy(ts_cols[:], bank[:, :, 0])
 
         heads = [kept([P, PACK * K], BF16, "heads%d" % g) for g in range(PASSES)]
         heads_t = kept([P, PASSES * D * PACK], BF16, "heads_t")
@@ -102,6 +104,8 @@ def tile_attend_gmf_nce_v_kernel(tc, uT, vT, y, us, ts, offs, uoffs, out):
         for td in range(PACK):
             for g in range(PASSES):
                 nc.vector.tensor_copy(heads[g][:, td * K : (td + 1) * K], u_raw[td][:].indirect(head_list[:, 32 * g : 32 * (g + 1)]))
+                if td == 0 and g == 0:
+                    spread_scales()
             if td < PACK - 1:
                 turn_heads(td)
         x_scales = [kept([P, K], U8, "x_scales%d" % g) for g in range(PASSES)]
@@ -117,8 +121,10 @@ def tile_attend_gmf_nce_v_kernel(tc, uT, vT, y, us, ts, offs, uoffs, out):
 
         tails = kept([P, N * PACK], BF16, "tails")
         places = tails[:].rearrange("p (i d) -> p i d", d=PACK)
+        pair = kept([P, 2 * N], BF16, "pair")
         for td in range(2):
-            nc.vector.tensor_copy(places[:, :, td], v_raw[td][:].indirect(tail_list[:]))
+            nc.vector.tensor_copy(pair[:, td * N : (td + 1) * N], v_raw[td][:].indirect(tail_list[:]))
+        nc.vector.tensor_copy(places[:, :, 0:2], pair[:].rearrange("p (e i) -> p i e", e=2))
         picked = kept([P, N], BF16, "picked", "woven0")
         nc.vector.tensor_copy(picked[:], v_raw[2][:].indirect(tail_list[:]))
         nc.vector.tensor_copy(places[:, :, 2], picked[:])

@@ -48,7 +48,7 @@ def tile_attend_gmf_nce_v_kernel(tc, uT, vT, y, us, ts, offs, uoffs, out):
         make_identity(nc, ident[:])
         windows = [kept([P, T], F32, "window%d" % td) for td in range(PACK)]
         for td in range(PACK):
-            nc.vector.memset(windows[td][:].bitcast(I32), 0)
+            (nc.vector if td < PACK // 2 else nc.gpsimd).memset(windows[td][:].bitcast(I32), 0)
 
         nc.sync.dma_start(tail_list[:], offs)
         nc.sync.dma_start(head_list[:], uoffs)

@@ -21,6 +21,7 @@ K = P * PACK
 PASSES = R // K
 BLOCKS = N // P
 HALF = N // 2
+DIRECT = 2
 FLOPS = 2 * 2 * D * R * N
 
 
@@ -91,7 +92,7 @@ def tile_attend_gmf_nce_v_kernel(tc, uT, vT, y, us, ts, offs, uoffs, out):
 
         heads = [kept([P, PACK * K], BF16, "heads%d" % g) for g in range(PASSES)]
         heads_t = kept([P, PASSES * D * PACK], BF16, "heads_t")
-        heads_t_words = heads_t[:].bitcast(F32).rearrange("m (g d p u) -> m d g p u", g=PASSES, d=PACK, u=2)
+        heads_t_words = heads_t[:].bitcast(F32).rearrange("m (d g p u) -> m d g p u", g=PASSES, d=PACK, u=2)
 
         def turn_heads(td):
             bank = psum_out.tile([P, PASSES, 2, P], F32, name="wide", tag="wide")
@@ -128,7 +129,7 @@ def tile_attend_gmf_nce_v_kernel(tc, uT, vT, y, us, ts, offs, uoffs, out):
         picked = kept([P, N], BF16, "picked", "woven0")
         nc.vector.tensor_copy(picked[:], v_raw[2][:].indirect(tail_list[:]))
         nc.vector.tensor_copy(places[:, :, 2], picked[:])
-        xt_scales = [kept([P, D], U8, "xt_scales%d" % g) for g in range(PASSES)]
+        xt_scales = kept([P, PACK * PASSES * P], U8, "xt_scales")
         w_codes = kept([P, N], U32, "w_codes")
         w_scales = kept([P, N], U8, "w_scales")
         for k in range(2):
@@ -137,12 +138,16 @@ def tile_attend_gmf_nce_v_kernel(tc, uT, vT, y, us, ts, offs, uoffs, out):
         for k in range(2):
             slots = slice(k * HALF, (k + 1) * HALF)
             nc.vector.quantize_mx(w_codes[:, slots].bitcast(E4M3), w_scales[:, slots], tails[:, k * HALF * PACK : (k + 1) * HALF * PACK])
-        late = kept([P, 3 * K], U32, "late", "tails")
+        plane = PASSES * P
+
+        def quantise_turned(td, codes):
+            nc.vector.quantize_mx(codes.bitcast(E4M3), xt_scales[:, td * plane : (td + 1) * plane], heads_t[:, td * plane * PACK : (td + 1) * plane * PACK])
+
+        late = kept([P, K + plane], U32, "late", "tails")
         x_codes = [x_first[:], late[:, 0:K]]
-        xt_codes = [late[:, K : 2 * K], late[:, 2 * K :]]
+        xt_codes = [late[:, K:]]
         nc.vector.quantize_mx(x_codes[1].bitcast(E4M3), x_scales[1][:], woven[1][:])
-        for g in range(PASSES):
-            nc.vector.quantize_mx(xt_codes[g].bitcast(E4M3), xt_scales[g][:], heads_t[:, g * D * PACK : (g + 1) * D * PACK])
+        quantise_turned(0, xt_codes[0])
 
         labels = [load(y[0].rearrange("(g p t) i -> g p (t i)", g=PASSES, t=PACK)[g]) for g in range(PASSES)]
 
@@ -156,6 +161,18 @@ def tile_attend_gmf_nce_v_kernel(tc, uT, vT, y, us, ts, offs, uoffs, out):
             g, k = steps[n]
             b = 2 * k + j
             slots = slice(b * P, (b + 1) * P)
+            if 2 * n + j < DIRECT:
+                acc = psum.tile([P, PACK, P], F32, name="turn", tag="turn")
+                for t in range(PACK):
+                    cols = slice(t * P, (t + 1) * P)
+                    nc.tensor.matmul_mx(
+                        out=acc[:, t, :], lhsT=x_codes[g][:, cols].bitcast(E4M3), lhsT_scale=x_scales[g][:, cols],
+                        rhs=w_codes[:, slots].bitcast(E4M3), rhs_scale=w_scales[:, slots], start=True, stop=True,
+                    )
+                tile = z[n][:, :, j * P : (j + 1) * P]
+                nc.vector.tensor_tensor(tile, acc[:], scale[g][:, :, slots], ALU.mult)
+                nc.scalar.activation(tile, tile, ACT.Sigmoid)
+                return
             acc = psum.tile([P, K], F32, name="score", tag="score")
             nc.tensor.matmul_mx(
                 out=acc[:], lhsT=w_codes[:, slots].bitcast(E4M3), lhsT_scale=w_scales[:, slots],
@@ -203,13 +220,18 @@ def tile_attend_gmf_nce_v_kernel(tc, uT, vT, y, us, ts, offs, uoffs, out):
                 if 0 <= step - lag < len(steps):
                     stage_of(step - lag)
 
+        last = kept([P, (PACK - 1) * plane], U32, "last", "h1")
+        for td in range(1, PACK):
+            xt_codes.append(last[:, (td - 1) * plane : td * plane])
+            quantise_turned(td, xt_codes[td])
+
         out_planes = out.rearrange("(p t) c -> t p c", t=PACK)
         for td in range(PACK):
             acc = psum_out.tile([P, N], F32, name="wide", tag="wide")
-            cols = slice(td * P, (td + 1) * P)
             for g in range(PASSES):
                 nc.tensor.matmul_mx(
-                    out=acc[:], lhsT=xt_codes[g][:, cols].bitcast(E4M3), lhsT_scale=xt_scales[g][:, cols],
+                    out=acc[:], lhsT=xt_codes[td][:, g * P : (g + 1) * P].bitcast(E4M3),
+                    lhsT_scale=xt_scales[:, td * plane + g * P : td * plane + (g + 1) * P],
                     rhs=h_codes[g][:].bitcast(E5M2), rhs_scale=h_scales[g][:], start=(g == 0), stop=(g == PASSES - 1),
                 )
             grad = kept([P, N], F32, "grad%d" % td)

@@ -22,6 +22,8 @@ PASSES = R // K
 BLOCKS = N // P
 HALF = N // 2
 DIRECT = 2
+WINDOWS = 3
+PLACED = {"ts_all": 0, "turned_early": 0, "woven0": 4096, "woven1": 8192}
 FLOPS = 2 * 2 * D * R * N
 
 
@@ -29,12 +31,14 @@ def tile_attend_gmf_nce_v_kernel(tc, uT, vT, y, us, ts, offs, uoffs, out):
     nc = tc.nc
     with ExitStack() as ctx:
         keep = ctx.enter_context(tc.tile_pool(name="keep", bufs=1))
-        stage = ctx.enter_context(tc.tile_pool(name="stage", bufs=8))
         ring = ctx.enter_context(tc.tile_pool(name="ring", bufs=4))
+        shared = ctx.enter_context(tc.tile_pool(name="shared", bufs=1))
         psum = ctx.enter_context(tc.psum_pool(name="psum", bufs=2))
         psum_out = ctx.enter_context(tc.psum_pool(name="psum_out", bufs=4))
 
         def kept(shape, dtype, name, tag=None):
+            if (tag or name) in PLACED:
+                return shared.tile(shape, dtype, name=name, tag=tag or name, align_bytes=64, offset=PLACED[tag or name])
             return keep.tile(shape, dtype, name=name, tag=tag or name, align_bytes=64)
 
         tail_list = kept([P, N // 16], U16, "tail_list")
@@ -43,72 +47,77 @@ def tile_attend_gmf_nce_v_kernel(tc, uT, vT, y, us, ts, offs, uoffs, out):
         v_planes = vT.rearrange("(p t) c -> t p c", t=PACK)
 
         warm = kept([P, 2], F32, "warm")
-        nc.vector.memset(warm[:, 0:1], 0.0)
+        nc.gpsimd.memset(warm[:, 0:1], 0.0)
         nc.scalar.activation(warm[:, 1:2], warm[:, 0:1], ACT.Sigmoid)
+        ts_window = kept([P, T], F32, "ts_window")
+        nc.gpsimd.memset(ts_window[0 : P - 1, :].bitcast(I32), 0)
         ident = kept([P, P], F32, "ident")
         make_identity(nc, ident[:])
-        windows = [kept([P, T], F32, "window%d" % td) for td in range(PACK)]
-        for td in range(PACK):
-            (nc.vector if td < PACK // 2 else nc.gpsimd).memset(windows[td][:].bitcast(I32), 0)
+        windows = [kept([P, T], F32, "window%d" % w) for w in range(WINDOWS)]
+        for w in range(WINDOWS):
+            nc.gpsimd.memset(windows[w][:].bitcast(I32), 0)
+        h_codes = [kept([P, N], U32, "h_codes%d" % g) for g in range(PASSES)]
+        h_scales = [kept([P, N], U8, "h_scales%d" % g) for g in range(PASSES)]
+        for g in range(PASSES):
+            nc.gpsimd.memset(h_codes[g][:, HALF:], 0)
+            nc.gpsimd.memset(h_scales[g][:, HALF:], 0)
 
+        nc.scalar.dma_start(ts_window[P - 1 : P, :], ts[0:1, :])
         nc.sync.dma_start(tail_list[:], offs)
         nc.sync.dma_start(head_list[:], uoffs)
-        ts_folded = kept([P, T // P], F32, "ts_folded")
-        nc.scalar.dma_start(ts_folded[:], ts[0].rearrange("(p j) -> p j", p=P))
         row_scale = kept([P, PASSES, PACK], F32, "row_scale")
         nc.scalar.dma_start(row_scale[:], us[0].rearrange("(g p t) o -> p g (t o)", g=PASSES, t=PACK))
 
-        def load(source):
-            tile = stage.tile([P, T], F32, name="raw", tag="raw")
+        def load(source, name, tag=None):
+            tile = kept([P, T], F32, name, tag)
             nc.sync.dma_start(tile[:], source)
             return tile
 
-        u_raw = [load(u_planes[td]) for td in range(PACK)]
-        v_raw = [load(v_planes[td]) for td in range(PACK)]
+        u_raw = [load(u_planes[td], "u_raw%d" % td) for td in range(PACK)]
+        v_raw = [load(v_planes[td], "v_raw%d" % td) for td in range(PACK)]
 
         ts_cols = kept([P, BLOCKS], F32, "ts_cols")
         scale = [kept([P, PACK, N], F32, "scale%d" % g) for g in range(PASSES)]
-
-        ts_window = kept([P, T], F32, "ts_window")
-        for a in range(T // N):
-            bank = psum_out.tile([P, PACK, P], F32, name="wide", tag="wide")
-            for j in range(PACK):
-                column = PACK * a + j
-                nc.tensor.transpose(bank[:, j, :], ts_folded[:, column : column + 1].to_broadcast([P, P]), ident[:])
-            nc.scalar.activation(
-                ts_window[:].rearrange("q (p a j) -> q a p j", a=T // N, j=PACK)[:, a], bank[:].rearrange("q j p -> q p j"), ACT.Copy
-            )
-
-        def spread_scales():
-            ts_all = kept([P, N], F32, "ts_all")
-            nc.vector.tensor_copy(ts_all[:], ts_window[:].indirect(tail_list[:]))
-            for g in range(PASSES):
-                for t in range(PACK):
-                    nc.scalar.activation(scale[g][:, t, :], ts_all[:], ACT.Copy, scale=row_scale[:, g, t : t + 1])
-            bank = psum.tile([P, BLOCKS, P], F32, name="score", tag="score")
-            for b in range(BLOCKS):
-                nc.tensor.transpose(bank[:, b, :], ts_all[:, b * P : (b + 1) * P], ident[:])
-            nc.scalar.copy(ts_cols[:], bank[:, :, 0])
+        ts_picked = kept([P, N], F32, "ts_picked")
+        nc.vector.tensor_copy(ts_picked[:], ts_window[:].indirect(tail_list[:]))
+        bank = psum.tile([P, BLOCKS, P], F32, name="score", tag="score")
+        for b in range(BLOCKS):
+            nc.tensor.transpose(bank[:, b, :], ts_picked[:, b * P : (b + 1) * P], ident[:])
+        nc.scalar.copy(ts_cols[:], bank[:, :, P - 1])
+        ts_rows = psum.tile([P, N], F32, name="score", tag="score")
+        for b in range(BLOCKS):
+            nc.tensor.transpose(ts_rows[:, b * P : (b + 1) * P], ts_cols[:, b : b + 1].to_broadcast([P, P]), ident[:])
+        ts_all = kept([P, 6 * N], F32, "ts_all")
+        nc.scalar.copy(ts_all[:, 0:N], ts_rows[:])
+        for g in range(PASSES):
+            for t in range(PACK):
+                nc.scalar.activation(scale[g][:, t, :], ts_all[:, 0:N], ACT.Copy, scale=row_scale[:, g, t : t + 1])
 
         heads = [kept([P, PACK * K], BF16, "heads%d" % g) for g in range(PASSES)]
-        heads_t = kept([P, PASSES * D * PACK], BF16, "heads_t")
-        heads_t_words = heads_t[:].bitcast(F32).rearrange("m (d g p u) -> m d g p u", g=PASSES, d=PACK, u=2)
+        plane = PASSES * P
+        turned_banks = {}
 
         def turn_heads(td):
-            bank = psum_out.tile([P, PASSES, 2, P], F32, name="wide", tag="wide")
+            bank = psum.tile([P, PASSES, 2, P], F32, name="score", tag="score")
             for g in range(PASSES):
                 words = heads[g][:, td * K : (td + 1) * K].bitcast(F32)
                 for u in range(2):
                     nc.tensor.transpose(bank[:, g, u, :], words[:, u : K // 2 : 2], ident[:])
-            nc.scalar.copy(heads_t_words[:, td], bank[:].rearrange("m g u p -> m g p u"))
+            turned_banks[td] = bank
 
-        for td in range(PACK):
-            for g in range(PASSES):
-                nc.vector.tensor_copy(heads[g][:, td * K : (td + 1) * K], u_raw[td][:].indirect(head_list[:, 32 * g : 32 * (g + 1)]))
-                if td == 0 and g == 0:
-                    spread_scales()
-            if td < PACK - 1:
+        def copy_turned(planes, name, tag):
+            tile = kept([P, len(planes) * plane * PACK], BF16, name, tag)
+            words = tile[:].bitcast(F32).rearrange("m (d g p u) -> m d g p u", g=PASSES, d=len(planes), u=2)
+            for n, td in enumerate(planes):
+                nc.scalar.copy(words[:, n], turned_banks[td][:].rearrange("m g u p -> m g p u"))
+            return tile
+
+        for td, g in [(0, 0), (0, 1), (1, 0), (1, 1), (2, 0), (3, 0), (2, 1), (3, 1)]:
+            nc.vector.tensor_copy(heads[g][:, td * K : (td + 1) * K], u_raw[td][:].indirect(head_list[:, 32 * g : 32 * (g + 1)]))
+            if g == PASSES - 1:
                 turn_heads(td)
+            if (td, g) == (1, 1):
+                turned_early = copy_turned([0, 1], "turned_early", None)
         x_scales = [kept([P, K], U8, "x_scales%d" % g) for g in range(PASSES)]
         woven = [kept([P, K * PACK], BF16, "woven%d" % g) for g in range(PASSES)]
         for g in range(PASSES):
@@ -116,45 +125,41 @@ def tile_attend_gmf_nce_v_kernel(tc, uT, vT, y, us, ts, offs, uoffs, out):
                 woven[g][:].rearrange("p (t c e d) -> p c t e d", t=PACK, e=2, d=PACK),
                 heads[g][:].rearrange("p (d c e t) -> p c t e d", d=PACK, e=2, t=PACK),
             )
-        turn_heads(PACK - 1)
-        x_first = kept([P, K], U32, "x_first")
-        nc.vector.quantize_mx(x_first[:].bitcast(E4M3), x_scales[0][:], woven[0][:])
+        x_codes = [kept([P, K], U32, "x_codes%d" % g) for g in range(PASSES)]
+        xt_scales = kept([P, PACK * plane], U8, "xt_scales")
 
-        tails = kept([P, N * PACK], BF16, "tails")
+        def quantise_turned(planes, turned, name, tag):
+            codes = kept([P, len(planes) * plane], U32, name, tag)
+            width = len(planes) * plane
+            nc.vector.quantize_mx(codes[:].bitcast(E4M3), xt_scales[:, planes[0] * plane : planes[0] * plane + width], turned[:])
+            return [codes[:, n * plane : (n + 1) * plane] for n in range(len(planes))]
+
+        tails = kept([P, N * PACK], BF16, "tails", "heads1")
         places = tails[:].rearrange("p (i d) -> p i d", d=PACK)
         pair = kept([P, 2 * N], BF16, "pair")
-        for td in range(2):
-            nc.vector.tensor_copy(pair[:, td * N : (td + 1) * N], v_raw[td][:].indirect(tail_list[:]))
-        nc.vector.tensor_copy(places[:, :, 0:2], pair[:].rearrange("p (e i) -> p i e", e=2))
-        picked = kept([P, N], BF16, "picked", "woven0")
-        nc.vector.tensor_copy(picked[:], v_raw[2][:].indirect(tail_list[:]))
-        nc.vector.tensor_copy(places[:, :, 2], picked[:])
-        xt_scales = kept([P, PACK * PASSES * P], U8, "xt_scales")
+        nc.vector.tensor_copy(pair[:, 0:N], v_raw[0][:].indirect(tail_list[:]))
+        xt_codes = quantise_turned([0, 1], turned_early, "xt_early", "u_raw3")
+        nc.vector.tensor_copy(pair[:, N:], v_raw[1][:].indirect(tail_list[:]))
+        nc.scalar.copy(places[:, :, 0:2], pair[:].rearrange("p (e i) -> p i e", e=2))
+        turned_late = copy_turned([2, 3], "turned_late", "pair")
+        for g in range(PASSES):
+            nc.vector.quantize_mx(x_codes[g][:].bitcast(E4M3), x_scales[g][:], woven[g][:])
+        pair = kept([P, 2 * N], BF16, "late_pair", "woven1")
+        nc.vector.tensor_copy(pair[:, 0:N], v_raw[2][:].indirect(tail_list[:]))
         w_codes = kept([P, N], U32, "w_codes")
         w_scales = kept([P, N], U8, "w_scales")
+        halves = [slice(k * HALF, (k + 1) * HALF) for k in range(2)]
         for k in range(2):
-            slots = slice(k * HALF, (k + 1) * HALF)
-            nc.vector.tensor_copy(places[:, slots, 3], v_raw[3][:].indirect(tail_list[:, 16 * k : 16 * (k + 1)]))
+            nc.vector.tensor_copy(pair[:, N + k * HALF : N + (k + 1) * HALF], v_raw[3][:].indirect(tail_list[:, 16 * k : 16 * (k + 1)]))
+            nc.scalar.copy(places[:, halves[k], 2:4], pair[:].rearrange("p (e i) -> p i e", e=2)[:, halves[k]])
         for k in range(2):
-            slots = slice(k * HALF, (k + 1) * HALF)
-            nc.vector.quantize_mx(w_codes[:, slots].bitcast(E4M3), w_scales[:, slots], tails[:, k * HALF * PACK : (k + 1) * HALF * PACK])
-        plane = PASSES * P
+            nc.vector.quantize_mx(w_codes[:, halves[k]].bitcast(E4M3), w_scales[:, halves[k]], tails[:, k * HALF * PACK : (k + 1) * HALF * PACK])
+        xt_codes.extend(quantise_turned([2, 3], turned_late, "xt_late", "woven1"))
 
-        def quantise_turned(td, codes):
-            nc.vector.quantize_mx(codes.bitcast(E4M3), xt_scales[:, td * plane : (td + 1) * plane], heads_t[:, td * plane * PACK : (td + 1) * plane * PACK])
+        labels = [load(y[0].rearrange("(g p t) i -> g p (t i)", g=PASSES, t=PACK)[g], "labels%d" % g, "u_raw%d" % g) for g in range(PASSES)]
 
-        late = kept([P, K + plane], U32, "late", "tails")
-        x_codes = [x_first[:], late[:, 0:K]]
-        xt_codes = [late[:, K:]]
-        nc.vector.quantize_mx(x_codes[1].bitcast(E4M3), x_scales[1][:], woven[1][:])
-        quantise_turned(0, xt_codes[0])
-
-        labels = [load(y[0].rearrange("(g p t) i -> g p (t i)", g=PASSES, t=PACK)[g]) for g in range(PASSES)]
-
-        h_codes = [kept([P, N], U32, "h_codes%d" % g) for g in range(PASSES)]
-        h_scales = [kept([P, N], U8, "h_scales%d" % g) for g in range(PASSES)]
         h = [kept([P, N * PACK], BF16, "h%d" % g) for g in range(PASSES)]
-        steps = [(g, k) for g in range(PASSES) for k in range(2)]
+        steps = [(g, k) for k in range(2) for g in range(PASSES)]
         z = [kept([P, PACK, HALF], F32, "z%d" % n) for n in range(len(steps))]
 
         def logistic(n, j):
@@ -176,7 +181,7 @@ def tile_attend_gmf_nce_v_kernel(tc, uT, vT, y, us, ts, offs, uoffs, out):
             acc = psum.tile([P, K], F32, name="score", tag="score")
             nc.tensor.matmul_mx(
                 out=acc[:], lhsT=w_codes[:, slots].bitcast(E4M3), lhsT_scale=w_scales[:, slots],
-                rhs=x_codes[g].bitcast(E4M3), rhs_scale=x_scales[g][:], start=True, stop=True,
+                rhs=x_codes[g][:].bitcast(E4M3), rhs_scale=x_scales[g][:], start=True, stop=True,
             )
             turned = ring.tile([P, K], F32, name="turned", tag="turned")
             nc.scalar.activation(turned[:], acc[:], ACT.Copy, scale=ts_cols[:, b : b + 1])
@@ -214,19 +219,7 @@ def tile_attend_gmf_nce_v_kernel(tc, uT, vT, y, us, ts, offs, uoffs, out):
                 slots = slice(i0, i0 + width)
                 nc.vector.quantize_mx(h_codes[g][:, slots].bitcast(E5M2), h_scales[g][:, slots], h[g][:, i0 * PACK : (i0 + width) * PACK])
 
-        stages = (residual, weigh, quantise)
-        for step in range(len(steps) + len(stages) - 1):
-            for lag, stage_of in enumerate(stages):
-                if 0 <= step - lag < len(steps):
-                    stage_of(step - lag)
-
-        last = kept([P, (PACK - 1) * plane], U32, "last", "h1")
-        for td in range(1, PACK):
-            xt_codes.append(last[:, (td - 1) * plane : td * plane])
-            quantise_turned(td, xt_codes[td])
-
-        out_planes = out.rearrange("(p t) c -> t p c", t=PACK)
-        for td in range(PACK):
+        def product(td):
             acc = psum_out.tile([P, N], F32, name="wide", tag="wide")
             for g in range(PASSES):
                 nc.tensor.matmul_mx(
@@ -234,7 +227,24 @@ def tile_attend_gmf_nce_v_kernel(tc, uT, vT, y, us, ts, offs, uoffs, out):
                     lhsT_scale=xt_scales[:, td * plane + g * P : td * plane + (g + 1) * P],
                     rhs=h_codes[g][:].bitcast(E5M2), rhs_scale=h_scales[g][:], start=(g == 0), stop=(g == PASSES - 1),
                 )
-            grad = kept([P, N], F32, "grad%d" % td)
-            nc.scalar.copy(grad[:], acc[:])
-            nc.vector.tensor_copy(windows[td][:].indirect(tail_list[:]), grad[:])
-            nc.sync.dma_start(out_planes[td], windows[td][:])
+            return acc
+
+        def scatter(td, acc, first, count, name, tag=None):
+            grad = kept([P, count], F32, name, tag)
+            nc.scalar.copy(grad[:], acc[:, first : first + count])
+            nc.vector.tensor_copy(windows[td % WINDOWS][:].indirect(tail_list[:, first // 16 : (first + count) // 16]), grad[:])
+
+        stages = (residual, weigh, quantise)
+        for step in range(len(steps) + len(stages) - 1):
+            for lag, stage_of in enumerate(stages):
+                if 0 <= step - lag < len(steps):
+                    stage_of(step - lag)
+                if stage_of is quantise and step - lag == PASSES - 1:
+                    early = product(0)
+
+        scatter(0, early, 0, HALF, "grad_early", "z%d" % (len(steps) - 1))
+        out_planes = out.rearrange("(p t) c -> t p c", t=PACK)
+        for td in range(PACK):
+            first = HALF if td == 0 else 0
+            scatter(td, product(td), first, N - first, "grad%d" % td)
+            nc.sync.dma_start(out_planes[td], windows[td % WINDOWS][:])

@@ -21,7 +21,6 @@ K = P * PACK
 PASSES = R // K
 BLOCKS = N // P
 HALF = N // 2
-DIRECT = 2
 WINDOWS = 3
 PLACED = {"ts_all": 0, "turned_early": 0, "woven0": 4096, "woven1": 8192}
 FLOPS = 2 * 2 * D * R * N
@@ -49,10 +48,10 @@ def tile_attend_gmf_nce_v_kernel(tc, uT, vT, y, us, ts, offs, uoffs, out):
         warm = kept([P, 2], F32, "warm")
         nc.gpsimd.memset(warm[:, 0:1], 0.0)
         nc.scalar.activation(warm[:, 1:2], warm[:, 0:1], ACT.Sigmoid)
-        ts_window = kept([P, T], F32, "ts_window")
-        nc.gpsimd.memset(ts_window[0 : P - 1, :].bitcast(I32), 0)
         ident = kept([P, P], F32, "ident")
         make_identity(nc, ident[:])
+        ts_window = kept([P, T], F32, "ts_window")
+        nc.gpsimd.memset(ts_window[0 : P - 1, :].bitcast(I32), 0)
         windows = [kept([P, T], F32, "window%d" % w) for w in range(WINDOWS)]
         for w in range(WINDOWS):
             nc.gpsimd.memset(windows[w][:].bitcast(I32), 0)
@@ -148,12 +147,12 @@ def tile_attend_gmf_nce_v_kernel(tc, uT, vT, y, us, ts, offs, uoffs, out):
         nc.vector.tensor_copy(pair[:, 0:N], v_raw[2][:].indirect(tail_list[:]))
         w_codes = kept([P, N], U32, "w_codes")
         w_scales = kept([P, N], U8, "w_scales")
-        halves = [slice(k * HALF, (k + 1) * HALF) for k in range(2)]
-        for k in range(2):
-            nc.vector.tensor_copy(pair[:, N + k * HALF : N + (k + 1) * HALF], v_raw[3][:].indirect(tail_list[:, 16 * k : 16 * (k + 1)]))
-            nc.scalar.copy(places[:, halves[k], 2:4], pair[:].rearrange("p (e i) -> p i e", e=2)[:, halves[k]])
-        for k in range(2):
-            nc.vector.quantize_mx(w_codes[:, halves[k]].bitcast(E4M3), w_scales[:, halves[k]], tails[:, k * HALF * PACK : (k + 1) * HALF * PACK])
+        parts = [slice(0, P), slice(P, HALF), slice(HALF, N)]
+        for part in parts:
+            nc.vector.tensor_copy(pair[:, N + part.start : N + part.stop], v_raw[3][:].indirect(tail_list[:, part.start // 16 : part.stop // 16]))
+            nc.scalar.copy(places[:, part, 2:4], pair[:].rearrange("p (e i) -> p i e", e=2)[:, part])
+        for part in parts:
+            nc.vector.quantize_mx(w_codes[:, part].bitcast(E4M3), w_scales[:, part], tails[:, part.start * PACK : part.stop * PACK])
         xt_codes.extend(quantise_turned([2, 3], turned_late, "xt_late", "woven1"))
 
         labels = [load(y[0].rearrange("(g p t) i -> g p (t i)", g=PASSES, t=PACK)[g], "labels%d" % g, "u_raw%d" % g) for g in range(PASSES)]
@@ -162,43 +161,46 @@ def tile_attend_gmf_nce_v_kernel(tc, uT, vT, y, us, ts, offs, uoffs, out):
         steps = [(g, k) for k in range(2) for g in range(PASSES)]
         z = [kept([P, PACK, HALF], F32, "z%d" % n) for n in range(len(steps))]
 
-        def logistic(n, j):
+        def direct_scores(n):
             g, k = steps[n]
-            b = 2 * k + j
-            slots = slice(b * P, (b + 1) * P)
-            if 2 * n + j < DIRECT:
+            for j in range(2):
+                block = slice(k * HALF + j * P, k * HALF + (j + 1) * P)
                 acc = psum.tile([P, PACK, P], F32, name="turn", tag="turn")
                 for t in range(PACK):
                     cols = slice(t * P, (t + 1) * P)
                     nc.tensor.matmul_mx(
                         out=acc[:, t, :], lhsT=x_codes[g][:, cols].bitcast(E4M3), lhsT_scale=x_scales[g][:, cols],
-                        rhs=w_codes[:, slots].bitcast(E4M3), rhs_scale=w_scales[:, slots], start=True, stop=True,
+                        rhs=w_codes[:, block].bitcast(E4M3), rhs_scale=w_scales[:, block], start=True, stop=True,
                     )
                 tile = z[n][:, :, j * P : (j + 1) * P]
-                nc.vector.tensor_tensor(tile, acc[:], scale[g][:, :, slots], ALU.mult)
+                nc.vector.tensor_tensor(tile, acc[:], scale[g][:, :, block], ALU.mult)
                 nc.scalar.activation(tile, tile, ACT.Sigmoid)
-                return
-            acc = psum.tile([P, K], F32, name="score", tag="score")
-            nc.tensor.matmul_mx(
-                out=acc[:], lhsT=w_codes[:, slots].bitcast(E4M3), lhsT_scale=w_scales[:, slots],
-                rhs=x_codes[g][:].bitcast(E4M3), rhs_scale=x_scales[g][:], start=True, stop=True,
-            )
-            turned = ring.tile([P, K], F32, name="turned", tag="turned")
-            nc.scalar.activation(turned[:], acc[:], ACT.Copy, scale=ts_cols[:, b : b + 1])
-            acc = psum.tile([P, PACK, P], F32, name="turn", tag="turn")
+            return [(slice(0, PACK), slice(j * P, (j + 1) * P)) for j in range(2)]
+
+        def turned_scores(n):
+            g, k = steps[n]
+            banks = [psum.tile([P, 2, HALF], F32, name="turn", tag="turn") for u in range(2)]
+            for j in range(2):
+                b = 2 * k + j
+                block = slice(b * P, (b + 1) * P)
+                acc = psum.tile([P, K], F32, name="score", tag="score")
+                nc.tensor.matmul_mx(
+                    out=acc[:], lhsT=w_codes[:, block].bitcast(E4M3), lhsT_scale=w_scales[:, block],
+                    rhs=x_codes[g][:].bitcast(E4M3), rhs_scale=x_scales[g][:], start=True, stop=True,
+                )
+                turned = ring.tile([P, K], F32, name="turned", tag="turned")
+                nc.scalar.activation(turned[:], acc[:], ACT.Copy, scale=ts_cols[:, b : b + 1])
+                for t in range(PACK):
+                    nc.tensor.transpose(banks[t // 2][:, t % 2, j * P : (j + 1) * P], turned[:, t * P : (t + 1) * P], ident[:])
             for t in range(PACK):
-                nc.tensor.transpose(acc[:, t, :], turned[:, t * P : (t + 1) * P], ident[:])
-            for t in range(PACK):
-                nc.scalar.activation(z[n][:, t, j * P : (j + 1) * P], acc[:, t, :], ACT.Sigmoid, scale=row_scale[:, g, t : t + 1])
+                nc.scalar.activation(z[n][:, t, :], banks[t // 2][:, t % 2, :], ACT.Sigmoid, scale=row_scale[:, g, t : t + 1])
+            return [(slice(2 * u, 2 * u + 2), slice(0, HALF)) for u in range(2)]
 
         def residual(n):
             g, k = steps[n]
-            label = labels[g][:].rearrange("p (t i) -> p t i", t=PACK)
-            for j in range(2):
-                logistic(n, j)
-                b = 2 * k + j
-                cols = z[n][:, :, j * P : (j + 1) * P]
-                nc.vector.tensor_tensor(cols, cols, label[:, :, b * P : (b + 1) * P], ALU.subtract)
+            label = labels[g][:].rearrange("p (t i) -> p t i", t=PACK)[:, :, k * HALF : (k + 1) * HALF]
+            for rows, cols in (direct_scores if n == 0 else turned_scores)(n):
+                nc.vector.tensor_tensor(z[n][:, rows, cols], z[n][:, rows, cols], label[:, rows, cols], ALU.subtract)
 
         def pieces(n):
             g, k = steps[n]

@@ -199,7 +199,7 @@ def tile_attend_gmf_nce_v_kernel(tc, uT, vT, y, us, ts, offs, uoffs, out):
         def residual(n):
             g, k = steps[n]
             label = labels[g][:].rearrange("p (t i) -> p t i", t=PACK)[:, :, k * HALF : (k + 1) * HALF]
-            for rows, cols in (direct_scores if n == 0 else turned_scores)(n):
+            for rows, cols in (direct_scores if n < PASSES else turned_scores)(n):
                 nc.vector.tensor_tensor(z[n][:, rows, cols], z[n][:, rows, cols], label[:, rows, cols], ALU.subtract)
 
         def pieces(n):

@@ -22,6 +22,7 @@ PASSES = R // K
 BLOCKS = N // P
 HALF = N // 2
 WINDOWS = 3
+TURNED = (0, 1, 2, 2)
 PLACED = {"ts_all": 0, "turned_early": 0, "woven0": 4096, "woven1": 8192}
 FLOPS = 2 * 2 * D * R * N
 
@@ -63,7 +64,6 @@ def tile_attend_gmf_nce_v_kernel(tc, uT, vT, y, us, ts, offs, uoffs, out):
 
         nc.scalar.dma_start(ts_window[P - 1 : P, :], ts[0:1, :])
         nc.sync.dma_start(tail_list[:], offs)
-        nc.sync.dma_start(head_list[:], uoffs)
         row_scale = kept([P, PASSES, PACK], F32, "row_scale")
         nc.scalar.dma_start(row_scale[:], us[0].rearrange("(g p t) o -> p g (t o)", g=PASSES, t=PACK))
 
@@ -72,11 +72,12 @@ def tile_attend_gmf_nce_v_kernel(tc, uT, vT, y, us, ts, offs, uoffs, out):
             nc.sync.dma_start(tile[:], source)
             return tile
 
-        u_raw = [load(u_planes[td], "u_raw%d" % td) for td in range(PACK)]
+        u_raw = [load(u_planes[0], "u_raw0")]
+        nc.sync.dma_start(head_list[:], uoffs)
+        u_raw.extend(load(u_planes[td], "u_raw%d" % td) for td in range(1, PACK))
         v_raw = [load(v_planes[td], "v_raw%d" % td) for td in range(PACK)]
 
         ts_cols = kept([P, BLOCKS], F32, "ts_cols")
-        scale = [kept([P, PACK, N], F32, "scale%d" % g) for g in range(PASSES)]
         ts_picked = kept([P, N], F32, "ts_picked")
         nc.vector.tensor_copy(ts_picked[:], ts_window[:].indirect(tail_list[:]))
         bank = psum.tile([P, BLOCKS, P], F32, name="score", tag="score")
@@ -88,9 +89,17 @@ def tile_attend_gmf_nce_v_kernel(tc, uT, vT, y, us, ts, offs, uoffs, out):
             nc.tensor.transpose(ts_rows[:, b * P : (b + 1) * P], ts_cols[:, b : b + 1].to_broadcast([P, P]), ident[:])
         ts_all = kept([P, 6 * N], F32, "ts_all")
         nc.scalar.copy(ts_all[:, 0:N], ts_rows[:])
-        for g in range(PASSES):
+        ts_late = kept([P, HALF], F32, "ts_late")
+        nc.scalar.copy(ts_late[:], ts_rows[:, HALF:])
+        steps = [(g, k) for k in range(2) for g in range(PASSES)]
+
+        def make_scale(n, source, tag=None):
+            tile = kept([P, PACK, HALF], F32, "scale%d" % n, tag)
             for t in range(PACK):
-                nc.scalar.activation(scale[g][:, t, :], ts_all[:, 0:N], ACT.Copy, scale=row_scale[:, g, t : t + 1])
+                nc.scalar.activation(tile[:, t, :], source, ACT.Copy, scale=row_scale[:, steps[n][0], t : t + 1])
+            return tile
+
+        scale = [make_scale(n, ts_all[:, steps[n][1] * HALF : (steps[n][1] + 1) * HALF]) for n in range(len(steps) - 1)]
 
         heads = [kept([P, PACK * K], BF16, "heads%d" % g) for g in range(PASSES)]
         plane = PASSES * P
@@ -158,29 +167,28 @@ def tile_attend_gmf_nce_v_kernel(tc, uT, vT, y, us, ts, offs, uoffs, out):
         labels = [load(y[0].rearrange("(g p t) i -> g p (t i)", g=PASSES, t=PACK)[g], "labels%d" % g, "u_raw%d" % g) for g in range(PASSES)]
 
         h = [kept([P, N * PACK], BF16, "h%d" % g) for g in range(PASSES)]
-        steps = [(g, k) for k in range(2) for g in range(PASSES)]
         z = [kept([P, PACK, HALF], F32, "z%d" % n) for n in range(len(steps))]
 
-        def direct_scores(n):
+        def direct_scores(n, j):
             g, k = steps[n]
-            for j in range(2):
-                block = slice(k * HALF + j * P, k * HALF + (j + 1) * P)
-                acc = psum.tile([P, PACK, P], F32, name="turn", tag="turn")
-                for t in range(PACK):
-                    cols = slice(t * P, (t + 1) * P)
-                    nc.tensor.matmul_mx(
-                        out=acc[:, t, :], lhsT=x_codes[g][:, cols].bitcast(E4M3), lhsT_scale=x_scales[g][:, cols],
-                        rhs=w_codes[:, block].bitcast(E4M3), rhs_scale=w_scales[:, block], start=True, stop=True,
-                    )
-                tile = z[n][:, :, j * P : (j + 1) * P]
-                nc.vector.tensor_tensor(tile, acc[:], scale[g][:, :, block], ALU.mult)
-                nc.scalar.activation(tile, tile, ACT.Sigmoid)
-            return [(slice(0, PACK), slice(j * P, (j + 1) * P)) for j in range(2)]
+            block = slice(k * HALF + j * P, k * HALF + (j + 1) * P)
+            acc = psum.tile([P, PACK, P], F32, name="turn", tag="turn")
+            for t in range(PACK):
+                cols = slice(t * P, (t + 1) * P)
+                nc.tensor.matmul_mx(
+                    out=acc[:, t, :], lhsT=x_codes[g][:, cols].bitcast(E4M3), lhsT_scale=x_scales[g][:, cols],
+                    rhs=w_codes[:, block].bitcast(E4M3), rhs_scale=w_scales[:, block], start=True, stop=True,
+                )
+            tile = z[n][:, :, j * P : (j + 1) * P]
+            nc.vector.tensor_tensor(tile, acc[:], scale[n][:, :, j * P : (j + 1) * P], ALU.mult)
+            nc.scalar.activation(tile, tile, ACT.Sigmoid)
+            return [(slice(0, PACK), slice(j * P, (j + 1) * P))]
 
-        def turned_scores(n):
+        def turned_scores(n, count):
             g, k = steps[n]
-            banks = [psum.tile([P, 2, HALF], F32, name="turn", tag="turn") for u in range(2)]
-            for j in range(2):
+            share = PACK // count
+            banks = [psum.tile([P, share, count * P], F32, name="turn", tag="turn") for u in range(count)]
+            for j in range(count):
                 b = 2 * k + j
                 block = slice(b * P, (b + 1) * P)
                 acc = psum.tile([P, K], F32, name="score", tag="score")
@@ -191,15 +199,19 @@ def tile_attend_gmf_nce_v_kernel(tc, uT, vT, y, us, ts, offs, uoffs, out):
                 turned = ring.tile([P, K], F32, name="turned", tag="turned")
                 nc.scalar.activation(turned[:], acc[:], ACT.Copy, scale=ts_cols[:, b : b + 1])
                 for t in range(PACK):
-                    nc.tensor.transpose(banks[t // 2][:, t % 2, j * P : (j + 1) * P], turned[:, t * P : (t + 1) * P], ident[:])
+                    nc.tensor.transpose(banks[t // share][:, t % share, j * P : (j + 1) * P], turned[:, t * P : (t + 1) * P], ident[:])
             for t in range(PACK):
-                nc.scalar.activation(z[n][:, t, :], banks[t // 2][:, t % 2, :], ACT.Sigmoid, scale=row_scale[:, g, t : t + 1])
-            return [(slice(2 * u, 2 * u + 2), slice(0, HALF)) for u in range(2)]
+                nc.scalar.activation(z[n][:, t, 0 : count * P], banks[t // share][:, t % share, :], ACT.Sigmoid, scale=row_scale[:, g, t : t + 1])
+            return [(slice(share * u, share * (u + 1)), slice(0, count * P)) for u in range(count)]
 
         def residual(n):
             g, k = steps[n]
             label = labels[g][:].rearrange("p (t i) -> p t i", t=PACK)[:, :, k * HALF : (k + 1) * HALF]
-            for rows, cols in (direct_scores if n < PASSES else turned_scores)(n):
+            count = TURNED[n]
+            ready = turned_scores(n, count) if count else []
+            for j in range(count, 2):
+                ready = ready + direct_scores(n, j)
+            for rows, cols in ready:
                 nc.vector.tensor_tensor(z[n][:, rows, cols], z[n][:, rows, cols], label[:, rows, cols], ALU.subtract)
 
         def pieces(n):
@@ -212,7 +224,7 @@ def tile_attend_gmf_nce_v_kernel(tc, uT, vT, y, us, ts, offs, uoffs, out):
                 nc.vector.tensor_tensor(
                     h[g][:, i0 * PACK : (i0 + width) * PACK].rearrange("p (c i t) -> p c t i", i=4, t=PACK),
                     z[n][:, :, c0 : c0 + width].rearrange("p t (c i) -> p c t i", i=4),
-                    scale[g][:, :, i0 : i0 + width].rearrange("p t (c i) -> p c t i", i=4),
+                    scale[n][:, :, c0 : c0 + width].rearrange("p t (c i) -> p c t i", i=4),
                     ALU.mult,
                 )
 
@@ -241,6 +253,8 @@ def tile_attend_gmf_nce_v_kernel(tc, uT, vT, y, us, ts, offs, uoffs, out):
             for lag, stage_of in enumerate(stages):
                 if 0 <= step - lag < len(steps):
                     stage_of(step - lag)
+                if stage_of is residual and step == PASSES - 1:
+                    scale.append(make_scale(len(steps) - 1, ts_late[:], "v_raw3"))
                 if stage_of is quantise and step - lag == PASSES - 1:
                     early = product(0)
 

@@ -202,7 +202,7 @@ def tile_attend_gmf_nce_v_kernel(tc, uT, vT, y, us, ts, offs, uoffs, out):
                     nc.tensor.transpose(banks[t // share][:, t % share, j * P : (j + 1) * P], turned[:, t * P : (t + 1) * P], ident[:])
             for t in range(PACK):
                 nc.scalar.activation(z[n][:, t, 0 : count * P], banks[t // share][:, t % share, :], ACT.Sigmoid, scale=row_scale[:, g, t : t + 1])
-            return [(slice(share * u, share * (u + 1)), slice(0, count * P)) for u in range(count)]
+            return [(slice(0, PACK), slice(j * P, (j + 1) * P)) for j in range(count)]
 
         def residual(n):
             g, k = steps[n]
@@ -216,7 +216,7 @@ def tile_attend_gmf_nce_v_kernel(tc, uT, vT, y, us, ts, offs, uoffs, out):
 
         def pieces(n):
             g, k = steps[n]
-            width = P if n == len(steps) - 1 else HALF
+            width = P
             return [(g, c0, k * HALF + c0, width) for c0 in range(0, HALF, width)]
 
         def weigh(n):

@@ -22,7 +22,7 @@ PASSES = R // K
 BLOCKS = N // P
 HALF = N // 2
 WINDOWS = 3
-TURNED = (0, 1, 2, 2)
+TURNED = (0, 0, 2, 2)
 PLACED = {"ts_all": 0, "turned_early": 0, "woven0": 4096, "woven1": 8192}
 FLOPS = 2 * 2 * D * R * N
 
@@ -34,7 +34,8 @@ def tile_attend_gmf_nce_v_kernel(tc, uT, vT, y, us, ts, offs, uoffs, out):
         ring = ctx.enter_context(tc.tile_pool(name="ring", bufs=4))
         shared = ctx.enter_context(tc.tile_pool(name="shared", bufs=1))
         psum = ctx.enter_context(tc.psum_pool(name="psum", bufs=2))
-        psum_out = ctx.enter_context(tc.psum_pool(name="psum_out", bufs=4))
+        psum_out = ctx.enter_context(tc.psum_pool(name="psum_out", bufs=2))
+        psum_turn = ctx.enter_context(tc.psum_pool(name="psum_turn", bufs=4))
 
         def kept(shape, dtype, name, tag=None):
             if (tag or name) in PLACED:
@@ -172,7 +173,7 @@ def tile_attend_gmf_nce_v_kernel(tc, uT, vT, y, us, ts, offs, uoffs, out):
         def direct_scores(n, j):
             g, k = steps[n]
             block = slice(k * HALF + j * P, k * HALF + (j + 1) * P)
-            acc = psum.tile([P, PACK, P], F32, name="turn", tag="turn")
+            acc = psum_turn.tile([P, PACK, P], F32, name="turn", tag="turn")
             for t in range(PACK):
                 cols = slice(t * P, (t + 1) * P)
                 nc.tensor.matmul_mx(
@@ -187,7 +188,7 @@ def tile_attend_gmf_nce_v_kernel(tc, uT, vT, y, us, ts, offs, uoffs, out):
         def turned_scores(n, count):
             g, k = steps[n]
             share = PACK // count
-            banks = [psum.tile([P, share, count * P], F32, name="turn", tag="turn") for u in range(count)]
+            banks = [psum_turn.tile([P, share, count * P], F32, name="turn", tag="turn") for u in range(count)]
             for j in range(count):
                 b = 2 * k + j
                 block = slice(b * P, (b + 1) * P)

@@ -23,7 +23,7 @@ BLOCKS = N // P
 HALF = N // 2
 WINDOWS = 3
 TURNED = (0, 0, 2, 2)
-PLACED = {"ts_all": 0, "turned_early": 0, "woven0": 4096, "woven1": 8192}
+PLACED = {"ts_all": 0, "turned_early": 0, "woven0": 4096, "woven1": 8192, "heads1": 12288, "tails0": 12288, "tails1": 14336}
 FLOPS = 2 * 2 * D * R * N
 
 
@@ -143,27 +143,35 @@ def tile_attend_gmf_nce_v_kernel(tc, uT, vT, y, us, ts, offs, uoffs, out):
             nc.vector.quantize_mx(codes[:].bitcast(E4M3), xt_scales[:, planes[0] * plane : planes[0] * plane + width], turned[:])
             return [codes[:, n * plane : (n + 1) * plane] for n in range(len(planes))]
 
-        tails = kept([P, N * PACK], BF16, "tails", "heads1")
-        places = tails[:].rearrange("p (i d) -> p i d", d=PACK)
+        tails = [kept([P, HALF * PACK], BF16, "tails%d" % k) for k in range(2)]
+
+        def weave_tails(pairs, slot, place):
+            k, at = divmod(slot, HALF)
+            nc.scalar.copy(tails[k][:].rearrange("p (i d) -> p i d", d=PACK)[:, at : at + pairs.shape[1], place : place + 2], pairs)
+
         pair = kept([P, 2 * N], BF16, "pair")
         nc.vector.tensor_copy(pair[:, 0:N], v_raw[0][:].indirect(tail_list[:]))
         xt_codes = quantise_turned([0, 1], turned_early, "xt_early", "u_raw3")
         nc.vector.tensor_copy(pair[:, N:], v_raw[1][:].indirect(tail_list[:]))
-        nc.scalar.copy(places[:, :, 0:2], pair[:].rearrange("p (e i) -> p i e", e=2))
-        turned_late = copy_turned([2, 3], "turned_late", "pair")
+        for k in range(2):
+            weave_tails(pair[:].rearrange("p (e i) -> p i e", e=2)[:, k * HALF : (k + 1) * HALF], k * HALF, 0)
         for g in range(PASSES):
             nc.vector.quantize_mx(x_codes[g][:].bitcast(E4M3), x_scales[g][:], woven[g][:])
-        pair = kept([P, 2 * N], BF16, "late_pair", "woven1")
-        nc.vector.tensor_copy(pair[:, 0:N], v_raw[2][:].indirect(tail_list[:]))
         w_codes = kept([P, N], U32, "w_codes")
         w_scales = kept([P, N], U8, "w_scales")
-        parts = [slice(0, P), slice(P, HALF), slice(HALF, N)]
-        for part in parts:
-            nc.vector.tensor_copy(pair[:, N + part.start : N + part.stop], v_raw[3][:].indirect(tail_list[:, part.start // 16 : part.stop // 16]))
-            nc.scalar.copy(places[:, part, 2:4], pair[:].rearrange("p (e i) -> p i e", e=2)[:, part])
-        for part in parts:
-            nc.vector.quantize_mx(w_codes[:, part].bitcast(E4M3), w_scales[:, part], tails[:, part.start * PACK : part.stop * PACK])
-        xt_codes.extend(quantise_turned([2, 3], turned_late, "xt_late", "woven1"))
+        for k, (tag, width) in enumerate([("woven1", P), ("tails0", HALF)]):
+            pair = kept([P, 2 * HALF], BF16, "late_pair%d" % k, tag)
+            nc.vector.tensor_copy(pair[:, 0:HALF], v_raw[2][:].indirect(tail_list[:, 16 * k : 16 * (k + 1)]))
+            for at in range(0, HALF, width):
+                first = k * HALF + at
+                nc.vector.tensor_copy(pair[:, HALF + at : HALF + at + width], v_raw[3][:].indirect(tail_list[:, first // 16 : (first + width) // 16]))
+                weave_tails(pair[:].rearrange("p (e i) -> p i e", e=2)[:, at : at + width], first, 2)
+            for at in range(0, HALF, width):
+                slots = slice(k * HALF + at, k * HALF + at + width)
+                nc.vector.quantize_mx(w_codes[:, slots].bitcast(E4M3), w_scales[:, slots], tails[k][:, at * PACK : (at + width) * PACK])
+            if k == 0:
+                turned_late = copy_turned([2, 3], "turned_late", "woven1")
+        xt_codes.extend(quantise_turned([2, 3], turned_late, "xt_late", "tails0"))
 
         labels = [load(y[0].rearrange("(g p t) i -> g p (t i)", g=PASSES, t=PACK)[g], "labels%d" % g, "u_raw%d" % g) for g in range(PASSES)]
 
@@ -255,7 +263,7 @@ def tile_attend_gmf_nce_v_kernel(tc, uT, vT, y, us, ts, offs, uoffs, out):
                 if 0 <= step - lag < len(steps):
                     stage_of(step - lag)
                 if stage_of is residual and step == PASSES - 1:
-                    scale.append(make_scale(len(steps) - 1, ts_late[:], "v_raw3"))
+                    scale.append(make_scale(len(steps) - 1, ts_late[:], "woven1"))
                 if stage_of is quantise and step - lag == PASSES - 1:
                     early = product(0)
 

@@ -23,7 +23,7 @@ BLOCKS = N // P
 HALF = N // 2
 WINDOWS = 3
 TURNED = (0, 0, 2, 2)
-PLACED = {"ts_all": 0, "turned_early": 0, "woven0": 4096, "woven1": 8192, "heads1": 12288, "tails0": 12288, "tails1": 14336}
+PLACED = {"ts_all": 0, "turned_early": 0, "woven1": 4096, "woven0": 8192, "late_pair0": 8192, "tails1": 8192, "turned_late": 12288, "heads1": 16384, "tails0": 16384}
 FLOPS = 2 * 2 * D * R * N
 
 
@@ -153,24 +153,25 @@ def tile_attend_gmf_nce_v_kernel(tc, uT, vT, y, us, ts, offs, uoffs, out):
         nc.vector.tensor_copy(pair[:, 0:N], v_raw[0][:].indirect(tail_list[:]))
         xt_codes = quantise_turned([0, 1], turned_early, "xt_early", "u_raw3")
         nc.vector.tensor_copy(pair[:, N:], v_raw[1][:].indirect(tail_list[:]))
-        for k in range(2):
-            weave_tails(pair[:].rearrange("p (e i) -> p i e", e=2)[:, k * HALF : (k + 1) * HALF], k * HALF, 0)
+        early_pairs = pair[:].rearrange("p (e i) -> p i e", e=2)
+        weave_tails(early_pairs[:, 0:HALF], 0, 0)
         for g in range(PASSES):
             nc.vector.quantize_mx(x_codes[g][:].bitcast(E4M3), x_scales[g][:], woven[g][:])
         w_codes = kept([P, N], U32, "w_codes")
         w_scales = kept([P, N], U8, "w_scales")
-        for k, (tag, width) in enumerate([("woven1", P), ("tails0", HALF)]):
-            pair = kept([P, 2 * HALF], BF16, "late_pair%d" % k, tag)
+        for k, (tag, width) in enumerate([(None, P), ("tails0", HALF)]):
+            pair = kept([P, (16 if k == 0 else 2) * HALF], BF16, "late_pair%d" % k, tag)
             nc.vector.tensor_copy(pair[:, 0:HALF], v_raw[2][:].indirect(tail_list[:, 16 * k : 16 * (k + 1)]))
             for at in range(0, HALF, width):
                 first = k * HALF + at
                 nc.vector.tensor_copy(pair[:, HALF + at : HALF + at + width], v_raw[3][:].indirect(tail_list[:, first // 16 : (first + width) // 16]))
-                weave_tails(pair[:].rearrange("p (e i) -> p i e", e=2)[:, at : at + width], first, 2)
+                weave_tails(pair[:, 0:N].rearrange("p (e i) -> p i e", e=2)[:, at : at + width], first, 2)
             for at in range(0, HALF, width):
                 slots = slice(k * HALF + at, k * HALF + at + width)
                 nc.vector.quantize_mx(w_codes[:, slots].bitcast(E4M3), w_scales[:, slots], tails[k][:, at * PACK : (at + width) * PACK])
             if k == 0:
-                turned_late = copy_turned([2, 3], "turned_late", "woven1")
+                weave_tails(early_pairs[:, HALF:], HALF, 0)
+                turned_late = copy_turned([2, 3], "turned_late", None)
         xt_codes.extend(quantise_turned([2, 3], turned_late, "xt_late", "tails0"))
 
         labels = [load(y[0].rearrange("(g p t) i -> g p (t i)", g=PASSES, t=PACK)[g], "labels%d" % g, "u_raw%d" % g) for g in range(PASSES)]

@@ -89,18 +89,17 @@ def tile_attend_gmf_nce_v_kernel(tc, uT, vT, y, us, ts, offs, uoffs, out):
         for b in range(BLOCKS):
             nc.tensor.transpose(ts_rows[:, b * P : (b + 1) * P], ts_cols[:, b : b + 1].to_broadcast([P, P]), ident[:])
         ts_all = kept([P, 6 * N], F32, "ts_all")
-        nc.scalar.copy(ts_all[:, 0:N], ts_rows[:])
+        nc.scalar.copy(ts_all[:, 0:HALF], ts_rows[:, 0:HALF])
         ts_late = kept([P, HALF], F32, "ts_late")
         nc.scalar.copy(ts_late[:], ts_rows[:, HALF:])
         steps = [(g, k) for k in range(2) for g in range(PASSES)]
-
-        def make_scale(n, source, tag=None):
-            tile = kept([P, PACK, HALF], F32, "scale%d" % n, tag)
+        scale = [kept([P, PACK, HALF], F32, "scale%d" % n) for n in range(len(steps))]
+        for n, (g, k) in enumerate(steps):
             for t in range(PACK):
-                nc.scalar.activation(tile[:, t, :], source, ACT.Copy, scale=row_scale[:, steps[n][0], t : t + 1])
-            return tile
-
-        scale = [make_scale(n, ts_all[:, steps[n][1] * HALF : (steps[n][1] + 1) * HALF]) for n in range(len(steps) - 1)]
+                if k == 0:
+                    nc.scalar.activation(scale[n][:, t, :], ts_all[:, 0:HALF], ACT.Copy, scale=row_scale[:, g, t : t + 1])
+                else:
+                    nc.gpsimd.tensor_scalar(scale[n][:, t, :], ts_late[:], row_scale[:, g, t : t + 1], 0.0, ALU.mult, ALU.add)
 
         heads = [kept([P, PACK * K], BF16, "heads%d" % g) for g in range(PASSES)]
         plane = PASSES * P
@@ -263,8 +262,6 @@ def tile_attend_gmf_nce_v_kernel(tc, uT, vT, y, us, ts, offs, uoffs, out):
             for lag, stage_of in enumerate(stages):
                 if 0 <= step - lag < len(steps):
                     stage_of(step - lag)
-                if stage_of is residual and step == PASSES - 1:
-                    scale.append(make_scale(len(steps) - 1, ts_late[:], "woven1"))
                 if stage_of is quantise and step - lag == PASSES - 1:
                     early = product(0)
 

@@ -22,8 +22,8 @@ PASSES = R // K
 BLOCKS = N // P
 HALF = N // 2
 WINDOWS = 3
-TURNED = (0, 0, 2, 2)
-PLACED = {"ts_all": 0, "turned_early": 0, "woven1": 4096, "woven0": 8192, "late_pair0": 8192, "tails1": 8192, "turned_late": 12288, "heads1": 16384, "tails0": 16384}
+BANK = 2048
+PLACED = {"ts_all": 20480, "h_codes0": 20480, "h_codes1": 22528, "h_scales0": 24576, "h_scales1": 25088, "ts_first": 0, "turned_early": 0, "woven1": 4096, "woven0": 8192, "late_pair": 7168, "turned_late": 12288, "heads1": 16384, "tails0": 16384, "tails1": 18432}
 FLOPS = 2 * 2 * D * R * N
 
 
@@ -33,9 +33,10 @@ def tile_attend_gmf_nce_v_kernel(tc, uT, vT, y, us, ts, offs, uoffs, out):
         keep = ctx.enter_context(tc.tile_pool(name="keep", bufs=1))
         ring = ctx.enter_context(tc.tile_pool(name="ring", bufs=4))
         shared = ctx.enter_context(tc.tile_pool(name="shared", bufs=1))
-        psum = ctx.enter_context(tc.psum_pool(name="psum", bufs=2))
-        psum_out = ctx.enter_context(tc.psum_pool(name="psum_out", bufs=2))
-        psum_turn = ctx.enter_context(tc.psum_pool(name="psum_turn", bufs=4))
+        psum = ctx.enter_context(tc.psum_pool(name="psum", bufs=1))
+
+        def in_bank(number, shape, name):
+            return psum.tile(shape, F32, name=name, tag=name, offset=number * BANK)
 
         def kept(shape, dtype, name, tag=None):
             if (tag or name) in PLACED:
@@ -54,14 +55,15 @@ def tile_attend_gmf_nce_v_kernel(tc, uT, vT, y, us, ts, offs, uoffs, out):
         make_identity(nc, ident[:])
         ts_window = kept([P, T], F32, "ts_window")
         nc.gpsimd.memset(ts_window[0 : P - 1, :].bitcast(I32), 0)
-        windows = [kept([P, T], F32, "window%d" % w) for w in range(WINDOWS)]
-        for w in range(WINDOWS):
-            nc.gpsimd.memset(windows[w][:].bitcast(I32), 0)
-        h_codes = [kept([P, N], U32, "h_codes%d" % g) for g in range(PASSES)]
-        h_scales = [kept([P, N], U8, "h_scales%d" % g) for g in range(PASSES)]
-        for g in range(PASSES):
-            nc.gpsimd.memset(h_codes[g][:, HALF:], 0)
-            nc.gpsimd.memset(h_scales[g][:, HALF:], 0)
+        windows = []
+
+        def clear_window(tag):
+            window = kept([P, T], F32, "window%d" % len(windows), tag)
+            nc.gpsimd.memset(window[:].bitcast(I32), 0)
+            windows.append(window)
+
+        clear_window(None)
+        clear_window(None)
 
         nc.scalar.dma_start(ts_window[P - 1 : P, :], ts[0:1, :])
         nc.sync.dma_start(tail_list[:], offs)
@@ -81,58 +83,75 @@ def tile_attend_gmf_nce_v_kernel(tc, uT, vT, y, us, ts, offs, uoffs, out):
         ts_cols = kept([P, BLOCKS], F32, "ts_cols")
         ts_picked = kept([P, N], F32, "ts_picked")
         nc.vector.tensor_copy(ts_picked[:], ts_window[:].indirect(tail_list[:]))
-        bank = psum.tile([P, BLOCKS, P], F32, name="score", tag="score")
+        bank = in_bank(0, [P, BLOCKS, P], "ts_turned")
         for b in range(BLOCKS):
             nc.tensor.transpose(bank[:, b, :], ts_picked[:, b * P : (b + 1) * P], ident[:])
         nc.scalar.copy(ts_cols[:], bank[:, :, P - 1])
-        ts_rows = psum.tile([P, N], F32, name="score", tag="score")
+        ts_rows = in_bank(1, [P, N], "ts_rows")
         for b in range(BLOCKS):
             nc.tensor.transpose(ts_rows[:, b * P : (b + 1) * P], ts_cols[:, b : b + 1].to_broadcast([P, P]), ident[:])
-        ts_all = kept([P, 6 * N], F32, "ts_all")
-        nc.scalar.copy(ts_all[:, 0:HALF], ts_rows[:, 0:HALF])
-        ts_late = kept([P, HALF], F32, "ts_late")
-        nc.scalar.copy(ts_late[:], ts_rows[:, HALF:])
+        ts_all = kept([P, 3 * N], F32, "ts_all")
+        ts_first = kept([P, 8 * N], F32, "ts_first")
+        nc.scalar.copy(ts_first[:, 0:N], ts_rows[:])
+        nc.scalar.copy(ts_all[:, 0:N], ts_rows[:])
         steps = [(g, k) for k in range(2) for g in range(PASSES)]
-        scale = [kept([P, PACK, HALF], F32, "scale%d" % n) for n in range(len(steps))]
-        for n, (g, k) in enumerate(steps):
+        scale_of_pass = [kept([P, PACK, N], F32, "scale%d" % g) for g in range(PASSES)]
+        for g in range(PASSES):
             for t in range(PACK):
-                if k == 0:
-                    nc.scalar.activation(scale[n][:, t, :], ts_all[:, 0:HALF], ACT.Copy, scale=row_scale[:, g, t : t + 1])
-                else:
-                    nc.gpsimd.tensor_scalar(scale[n][:, t, :], ts_late[:], row_scale[:, g, t : t + 1], 0.0, ALU.mult, ALU.add)
+                nc.gpsimd.tensor_scalar(scale_of_pass[g][:, t, :], ts_all[:, 0:N] if g + t else ts_first[:, 0:N], row_scale[:, g, t : t + 1], 0.0, ALU.mult, ALU.add)
+        scale = [scale_of_pass[g][:, :, k * HALF : (k + 1) * HALF] for g, k in steps]
 
-        heads = [kept([P, PACK * K], BF16, "heads%d" % g) for g in range(PASSES)]
+        h_codes = [kept([P, N], U32, "h_codes%d" % g) for g in range(PASSES)]
+        h_scales = [kept([P, N], U8, "h_scales%d" % g) for g in range(PASSES)]
+        for g in range(PASSES):
+            nc.gpsimd.memset(h_codes[g][:, HALF:], 0)
+            nc.gpsimd.memset(h_scales[g][:, HALF:], 0)
+
+        heads = [kept([P, 2 * R], BF16, "heads%d" % n) for n in range(2)]
         plane = PASSES * P
         turned_banks = {}
 
         def turn_heads(td):
-            bank = psum.tile([P, PASSES, 2, P], F32, name="score", tag="score")
+            bank = in_bank(td % 2, [P, PASSES, 2, P], "heads_turned%d" % td)
             for g in range(PASSES):
-                words = heads[g][:, td * K : (td + 1) * K].bitcast(F32)
+                first = (td % 2) * R + g * K
+                words = heads[td // 2][:, first : first + K].bitcast(F32)
                 for u in range(2):
                     nc.tensor.transpose(bank[:, g, u, :], words[:, u : K // 2 : 2], ident[:])
             turned_banks[td] = bank
 
-        def copy_turned(planes, name, tag):
-            tile = kept([P, len(planes) * plane * PACK], BF16, name, tag)
-            words = tile[:].bitcast(F32).rearrange("m (d g p u) -> m d g p u", g=PASSES, d=len(planes), u=2)
-            for n, td in enumerate(planes):
-                nc.scalar.copy(words[:, n], turned_banks[td][:].rearrange("m g u p -> m g p u"))
-            return tile
+        turned = [kept([P, 2 * plane * PACK], BF16, name) for name in ("turned_early", "turned_late")]
 
-        for td, g in [(0, 0), (0, 1), (1, 0), (1, 1), (2, 0), (3, 0), (2, 1), (3, 1)]:
-            nc.vector.tensor_copy(heads[g][:, td * K : (td + 1) * K], u_raw[td][:].indirect(head_list[:, 32 * g : 32 * (g + 1)]))
-            if g == PASSES - 1:
-                turn_heads(td)
-            if (td, g) == (1, 1):
-                turned_early = copy_turned([0, 1], "turned_early", None)
-        x_scales = [kept([P, K], U8, "x_scales%d" % g) for g in range(PASSES)]
+        def copy_turned(td):
+            words = turned[td // 2][:].bitcast(F32).rearrange("m (d g p u) -> m d g p u", g=PASSES, d=2, u=2)
+            nc.scalar.copy(words[:, td % 2], turned_banks[td][:].rearrange("m g u p -> m g p u"))
+
         woven = [kept([P, K * PACK], BF16, "woven%d" % g) for g in range(PASSES)]
-        for g in range(PASSES):
-            nc.scalar.copy(
-                woven[g][:].rearrange("p (t c e d) -> p c t e d", t=PACK, e=2, d=PACK),
-                heads[g][:].rearrange("p (d c e t) -> p c t e d", d=PACK, e=2, t=PACK),
-            )
+
+        def weave_heads(n):
+            for g in range(PASSES):
+                nc.scalar.copy(
+                    woven[g][:].rearrange("p (t c e d) -> p c t e d", t=PACK, e=2, d=PACK)[:, :, :, :, 2 * n : 2 * n + 2],
+                    heads[n][:].rearrange("p (d g c e t) -> p g c t e d", d=2, g=PASSES, e=2, t=PACK)[:, g],
+                )
+
+        for td in range(PACK):
+            parts = PASSES if td % 2 else 1
+            for part in range(parts):
+                width = R // parts
+                first = (td % 2) * R + part * width
+                nc.vector.tensor_copy(heads[td // 2][:, first : first + width], u_raw[td][:].indirect(head_list[:, part * width // 16 : (part + 1) * width // 16]))
+            turn_heads(td)
+            if td == 1:
+                weave_heads(0)
+                copy_turned(0)
+                copy_turned(1)
+            if td == 2:
+                copy_turned(2)
+            if td == 3:
+                weave_heads(1)
+                copy_turned(3)
+        x_scales = [kept([P, K], U8, "x_scales%d" % g) for g in range(PASSES)]
         x_codes = [kept([P, K], U32, "x_codes%d" % g) for g in range(PASSES)]
         xt_scales = kept([P, PACK * plane], U8, "xt_scales")
 
@@ -144,44 +163,48 @@ def tile_attend_gmf_nce_v_kernel(tc, uT, vT, y, us, ts, offs, uoffs, out):
 
         tails = [kept([P, HALF * PACK], BF16, "tails%d" % k) for k in range(2)]
 
-        def weave_tails(pairs, slot, place):
-            k, at = divmod(slot, HALF)
-            nc.scalar.copy(tails[k][:].rearrange("p (i d) -> p i d", d=PACK)[:, at : at + pairs.shape[1], place : place + 2], pairs)
+        def weave_tails(pairs, first, count, place):
+            k, at = divmod(first, HALF)
+            nc.scalar.copy(
+                tails[k][:].rearrange("p (i d) -> p i d", d=PACK)[:, at : at + count, place : place + 2],
+                pairs[:].rearrange("p (e i) -> p i e", e=2)[:, first : first + count],
+            )
 
         pair = kept([P, 2 * N], BF16, "pair")
         nc.vector.tensor_copy(pair[:, 0:N], v_raw[0][:].indirect(tail_list[:]))
-        xt_codes = quantise_turned([0, 1], turned_early, "xt_early", "u_raw3")
+        xt_codes = quantise_turned([0, 1], turned[0], "xt_early", "u_raw3")
         nc.vector.tensor_copy(pair[:, N:], v_raw[1][:].indirect(tail_list[:]))
-        early_pairs = pair[:].rearrange("p (e i) -> p i e", e=2)
-        weave_tails(early_pairs[:, 0:HALF], 0, 0)
+        for k in range(2):
+            weave_tails(pair, k * HALF, HALF, 0)
         for g in range(PASSES):
             nc.vector.quantize_mx(x_codes[g][:].bitcast(E4M3), x_scales[g][:], woven[g][:])
         w_codes = kept([P, N], U32, "w_codes")
         w_scales = kept([P, N], U8, "w_scales")
-        for k, (tag, width) in enumerate([(None, P), ("tails0", HALF)]):
-            pair = kept([P, (16 if k == 0 else 2) * HALF], BF16, "late_pair%d" % k, tag)
-            nc.vector.tensor_copy(pair[:, 0:HALF], v_raw[2][:].indirect(tail_list[:, 16 * k : 16 * (k + 1)]))
-            for at in range(0, HALF, width):
-                first = k * HALF + at
-                nc.vector.tensor_copy(pair[:, HALF + at : HALF + at + width], v_raw[3][:].indirect(tail_list[:, first // 16 : (first + width) // 16]))
-                weave_tails(pair[:, 0:N].rearrange("p (e i) -> p i e", e=2)[:, at : at + width], first, 2)
-            for at in range(0, HALF, width):
-                slots = slice(k * HALF + at, k * HALF + at + width)
-                nc.vector.quantize_mx(w_codes[:, slots].bitcast(E4M3), w_scales[:, slots], tails[k][:, at * PACK : (at + width) * PACK])
-            if k == 0:
-                weave_tails(early_pairs[:, HALF:], HALF, 0)
-                turned_late = copy_turned([2, 3], "turned_late", None)
-        xt_codes.extend(quantise_turned([2, 3], turned_late, "xt_late", "tails0"))
+        late_pair = kept([P, 2 * N], BF16, "late_pair")
+        nc.vector.tensor_copy(late_pair[:, 0:N], v_raw[2][:].indirect(tail_list[:]))
+        parts = [(0, P), (P, P), (HALF, HALF)]
+        for first, count in parts:
+            nc.vector.tensor_copy(late_pair[:, N + first : N + first + count], v_raw[3][:].indirect(tail_list[:, first // 16 : (first + count) // 16]))
+            weave_tails(late_pair, first, count, 2)
+        for first, count in parts:
+            k, at = divmod(first, HALF)
+            slots = slice(first, first + count)
+            nc.vector.quantize_mx(w_codes[:, slots].bitcast(E4M3), w_scales[:, slots], tails[k][:, at * PACK : (at + count) * PACK])
+        xt_codes.extend(quantise_turned([2, 3], turned[1], "xt_late", "tails0"))
 
-        labels = [load(y[0].rearrange("(g p t) i -> g p (t i)", g=PASSES, t=PACK)[g], "labels%d" % g, "u_raw%d" % g) for g in range(PASSES)]
+        labels = []
+        for n, (g, k) in enumerate(steps):
+            tile = kept([P, PACK, HALF], F32, "labels%d" % n)
+            nc.sync.dma_start(tile[:], y[0].rearrange("(g p t) i -> g p t i", g=PASSES, t=PACK)[g][:, :, k * HALF : (k + 1) * HALF])
+            labels.append(tile)
 
-        h = [kept([P, N * PACK], BF16, "h%d" % g) for g in range(PASSES)]
+        h = {}
         z = [kept([P, PACK, HALF], F32, "z%d" % n) for n in range(len(steps))]
 
-        def direct_scores(n, j):
+        def direct_scores(n, j, number):
             g, k = steps[n]
             block = slice(k * HALF + j * P, k * HALF + (j + 1) * P)
-            acc = psum_turn.tile([P, PACK, P], F32, name="turn", tag="turn")
+            acc = in_bank(number, [P, PACK, P], "direct%d_%d" % (n, j))
             for t in range(PACK):
                 cols = slice(t * P, (t + 1) * P)
                 nc.tensor.matmul_mx(
@@ -191,47 +214,45 @@ def tile_attend_gmf_nce_v_kernel(tc, uT, vT, y, us, ts, offs, uoffs, out):
             tile = z[n][:, :, j * P : (j + 1) * P]
             nc.vector.tensor_tensor(tile, acc[:], scale[n][:, :, j * P : (j + 1) * P], ALU.mult)
             nc.scalar.activation(tile, tile, ACT.Sigmoid)
-            return [(slice(0, PACK), slice(j * P, (j + 1) * P))]
 
-        def turned_scores(n, count):
+        def turned_scores(n, j, number, targets):
             g, k = steps[n]
-            share = PACK // count
-            banks = [psum_turn.tile([P, share, count * P], F32, name="turn", tag="turn") for u in range(count)]
-            for j in range(count):
-                b = 2 * k + j
-                block = slice(b * P, (b + 1) * P)
-                acc = psum.tile([P, K], F32, name="score", tag="score")
-                nc.tensor.matmul_mx(
-                    out=acc[:], lhsT=w_codes[:, block].bitcast(E4M3), lhsT_scale=w_scales[:, block],
-                    rhs=x_codes[g][:].bitcast(E4M3), rhs_scale=x_scales[g][:], start=True, stop=True,
-                )
-                turned = ring.tile([P, K], F32, name="turned", tag="turned")
-                nc.scalar.activation(turned[:], acc[:], ACT.Copy, scale=ts_cols[:, b : b + 1])
-                for t in range(PACK):
-                    nc.tensor.transpose(banks[t // share][:, t % share, j * P : (j + 1) * P], turned[:, t * P : (t + 1) * P], ident[:])
+            b = 2 * k + j
+            block = slice(b * P, (b + 1) * P)
+            acc = in_bank(number, [P, K], "score%d_%d" % (n, j))
+            nc.tensor.matmul_mx(
+                out=acc[:], lhsT=w_codes[:, block].bitcast(E4M3), lhsT_scale=w_scales[:, block],
+                rhs=x_codes[g][:].bitcast(E4M3), rhs_scale=x_scales[g][:], start=True, stop=True,
+            )
+            turned = ring.tile([P, K], F32, name="turned", tag="turned")
+            nc.scalar.activation(turned[:], acc[:], ACT.Copy, scale=ts_cols[:, b : b + 1])
             for t in range(PACK):
-                nc.scalar.activation(z[n][:, t, 0 : count * P], banks[t // share][:, t % share, :], ACT.Sigmoid, scale=row_scale[:, g, t : t + 1])
-            return [(slice(0, PACK), slice(j * P, (j + 1) * P)) for j in range(count)]
+                nc.tensor.transpose(targets[t], turned[:, t * P : (t + 1) * P], ident[:])
+
+        def close_turned(n, first, width, sources):
+            g, k = steps[n]
+            for t in range(PACK):
+                nc.scalar.activation(z[n][:, t, first : first + width], sources[t], ACT.Sigmoid, scale=row_scale[:, g, t : t + 1])
+
+        def turned_step(n, scores, turns):
+            banks = [in_bank(number, [P, 2, HALF], "turn%d_%d" % (n, u)) for u, number in enumerate(turns)]
+            for j in range(2):
+                turned_scores(n, j, scores[j], [banks[t // 2][:, t % 2, j * P : (j + 1) * P] for t in range(PACK)])
+            close_turned(n, 0, HALF, [banks[t // 2][:, t % 2, :] for t in range(PACK)])
 
         def residual(n):
-            g, k = steps[n]
-            label = labels[g][:].rearrange("p (t i) -> p t i", t=PACK)[:, :, k * HALF : (k + 1) * HALF]
-            count = TURNED[n]
-            ready = turned_scores(n, count) if count else []
-            for j in range(count, 2):
-                ready = ready + direct_scores(n, j)
-            for rows, cols in ready:
-                nc.vector.tensor_tensor(z[n][:, rows, cols], z[n][:, rows, cols], label[:, rows, cols], ALU.subtract)
+            nc.vector.tensor_tensor(z[n][:], z[n][:], labels[n][:], ALU.subtract)
 
         def pieces(n):
             g, k = steps[n]
-            width = P
+            width = HALF
             return [(g, c0, k * HALF + c0, width) for c0 in range(0, HALF, width)]
 
         def weigh(n):
             for g, c0, i0, width in pieces(n):
+                h[n] = kept([P, HALF * PACK], BF16, "h%d" % n, None if g else "labels%d" % (n + 1))
                 nc.vector.tensor_tensor(
-                    h[g][:, i0 * PACK : (i0 + width) * PACK].rearrange("p (c i t) -> p c t i", i=4, t=PACK),
+                    h[n][:].rearrange("p (c i t) -> p c t i", i=4, t=PACK),
                     z[n][:, :, c0 : c0 + width].rearrange("p t (c i) -> p c t i", i=4),
                     scale[n][:, :, c0 : c0 + width].rearrange("p t (c i) -> p c t i", i=4),
                     ALU.mult,
@@ -240,15 +261,16 @@ def tile_attend_gmf_nce_v_kernel(tc, uT, vT, y, us, ts, offs, uoffs, out):
         def quantise(n):
             for g, c0, i0, width in pieces(n):
                 slots = slice(i0, i0 + width)
-                nc.vector.quantize_mx(h_codes[g][:, slots].bitcast(E5M2), h_scales[g][:, slots], h[g][:, i0 * PACK : (i0 + width) * PACK])
+                nc.vector.quantize_mx(h_codes[g][:, slots].bitcast(E5M2), h_scales[g][:, slots], h[n][:])
 
-        def product(td):
-            acc = psum_out.tile([P, N], F32, name="wide", tag="wide")
-            for g in range(PASSES):
+        def product(td, number, name):
+            acc = in_bank(number, [P, N], name)
+            order = range(PASSES) if td == 0 else range(PASSES - 1, -1, -1)
+            for g in order:
                 nc.tensor.matmul_mx(
                     out=acc[:], lhsT=xt_codes[td][:, g * P : (g + 1) * P].bitcast(E4M3),
                     lhsT_scale=xt_scales[:, td * plane + g * P : td * plane + (g + 1) * P],
-                    rhs=h_codes[g][:].bitcast(E5M2), rhs_scale=h_scales[g][:], start=(g == 0), stop=(g == PASSES - 1),
+                    rhs=h_codes[g][:].bitcast(E5M2), rhs_scale=h_scales[g][:], start=(g == order[0]), stop=(g == order[-1]),
                 )
             return acc
 
@@ -257,17 +279,25 @@ def tile_attend_gmf_nce_v_kernel(tc, uT, vT, y, us, ts, offs, uoffs, out):
             nc.scalar.copy(grad[:], acc[:, first : first + count])
             nc.vector.tensor_copy(windows[td % WINDOWS][:].indirect(tail_list[:, first // 16 : (first + count) // 16]), grad[:])
 
-        stages = (residual, weigh, quantise)
-        for step in range(len(steps) + len(stages) - 1):
-            for lag, stage_of in enumerate(stages):
-                if 0 <= step - lag < len(steps):
-                    stage_of(step - lag)
-                if stage_of is quantise and step - lag == PASSES - 1:
-                    early = product(0)
+        for n in range(PASSES):
+            for j in range(2):
+                direct_scores(n, j, 2 + 2 * n + j)
+        turned_step(2, (4, 5), (0, 1))
+        turned_step(3, (4, 5), (2, 3))
+        for k in range(2):
+            for stage_of in (residual, weigh, quantise):
+                for g in range(PASSES):
+                    stage_of(k * PASSES + g)
+                if k == 1 and stage_of is residual:
+                    scatter(1, second, 0, HALF, "grad_early1")
+            if k == 0:
+                second = product(1, 6, "early1")
+                early = product(0, 7, "early0")
 
+        clear_window("h3")
         scatter(0, early, 0, HALF, "grad_early", "z%d" % (len(steps) - 1))
         out_planes = out.rearrange("(p t) c -> t p c", t=PACK)
         for td in range(PACK):
-            first = HALF if td == 0 else 0
-            scatter(td, product(td), first, N - first, "grad%d" % td)
+            first = HALF if td < 2 else 0
+            scatter(td, product(td, (0, 1, 4, 5)[td], "final%d" % td), first, N - first, "grad%d" % td)
             nc.sync.dma_start(out_planes[td], windows[td % WINDOWS][:])

@@ -23,6 +23,7 @@ BLOCKS = N // P
 HALF = N // 2
 WINDOWS = 3
 BANK = 2048
+SEAM = 8
 PLACED = {"ts_all": 20480, "h_codes0": 20480, "h_codes1": 22528, "h_scales0": 24576, "h_scales1": 25088, "ts_first": 0, "turned_early": 0, "woven1": 4096, "woven0": 8192, "late_pair": 7168, "turned_late": 12288, "heads1": 16384, "tails0": 16384, "tails1": 18432}
 FLOPS = 2 * 2 * D * R * N
 
@@ -192,14 +193,25 @@ def tile_attend_gmf_nce_v_kernel(tc, uT, vT, y, us, ts, offs, uoffs, out):
             nc.vector.quantize_mx(w_codes[:, slots].bitcast(E4M3), w_scales[:, slots], tails[k][:, at * PACK : (at + count) * PACK])
         xt_codes.extend(quantise_turned([2, 3], turned[1], "xt_late", "tails0"))
 
+        y_parts = y[0].rearrange("(g p t) i -> g p t i", g=PASSES, t=PACK)
         labels = []
-        for n, (g, k) in enumerate(steps):
-            tile = kept([P, PACK, HALF], F32, "labels%d" % n)
-            nc.sync.dma_start(tile[:], y[0].rearrange("(g p t) i -> g p t i", g=PASSES, t=PACK)[g][:, :, k * HALF : (k + 1) * HALF])
+        for g in range(PASSES):
+            tile = kept([P, PACK, HALF], F32, "labels%d" % g)
+            nc.sync.dma_start(tile[:], y_parts[g][:, :, 0:HALF])
             labels.append(tile)
+        step = PACK * HALF
+        own = step + HALF
+        late_labels = kept([P, own], F32, "late_labels")
+        nc.sync.dma_start(late_labels[:, 0:step].rearrange("p (t i) -> p t i", t=PACK), y_parts[0][:, :, HALF:])
+        nc.sync.dma_start(late_labels[:, step:], y_parts[1][:, 0, HALF:])
+        lent_labels = kept([P, SEAM + 2 * step - own], F32, "lent_labels")
+        nc.gpsimd.memset(lent_labels[:, 0:SEAM], 0.0)
+        nc.sync.dma_start(lent_labels[:, SEAM:].rearrange("p (t i) -> p t i", i=HALF), y_parts[1][:, 1:, HALF:])
 
         h = {}
-        z = [kept([P, PACK, HALF], F32, "z%d" % n) for n in range(len(steps))]
+        z_late = kept([P, 2 * step], F32, "z_late")
+        z = [kept([P, PACK, HALF], F32, "z%d" % n)[:] for n in range(PASSES)]
+        z.extend(z_late[:, g * step : (g + 1) * step].rearrange("p (t i) -> p t i", t=PACK) for g in range(PASSES))
 
         def direct_scores(n, j, number):
             g, k = steps[n]
@@ -241,7 +253,13 @@ def tile_attend_gmf_nce_v_kernel(tc, uT, vT, y, us, ts, offs, uoffs, out):
             close_turned(n, 0, HALF, [banks[t // 2][:, t % 2, :] for t in range(PACK)])
 
         def residual(n):
-            nc.vector.tensor_tensor(z[n][:], z[n][:], labels[n][:], ALU.subtract)
+            if n < PASSES:
+                nc.vector.tensor_tensor(z[n], z[n], labels[n][:], ALU.subtract)
+            elif n == PASSES:
+                for cols in (slice(0, step), slice(step, own)):
+                    nc.vector.tensor_tensor(z_late[:, cols], z_late[:, cols], late_labels[:, cols], ALU.subtract)
+            else:
+                nc.gpsimd.tensor_tensor(z_late[:, own - SEAM :], z_late[:, own - SEAM :], lent_labels[:], ALU.subtract)
 
         def pieces(n):
             g, k = steps[n]
@@ -250,7 +268,7 @@ def tile_attend_gmf_nce_v_kernel(tc, uT, vT, y, us, ts, offs, uoffs, out):
 
         def weigh(n):
             for g, c0, i0, width in pieces(n):
-                h[n] = kept([P, HALF * PACK], BF16, "h%d" % n, None if g else "labels%d" % (n + 1))
+                h[n] = kept([P, HALF * PACK], BF16, "h%d" % n, None if n else "labels1")
                 nc.vector.tensor_tensor(
                     h[n][:].rearrange("p (c i t) -> p c t i", i=4, t=PACK),
                     z[n][:, :, c0 : c0 + width].rearrange("p t (c i) -> p c t i", i=4),
@@ -282,22 +300,22 @@ def tile_attend_gmf_nce_v_kernel(tc, uT, vT, y, us, ts, offs, uoffs, out):
         for n in range(PASSES):
             for j in range(2):
                 direct_scores(n, j, 2 + 2 * n + j)
-        turned_step(2, (4, 5), (0, 1))
-        turned_step(3, (4, 5), (2, 3))
+        turned_step(2, (2, 3), (0, 1))
+        turned_step(3, (4, 5), (6, 7))
         for k in range(2):
             for stage_of in (residual, weigh, quantise):
                 for g in range(PASSES):
                     stage_of(k * PASSES + g)
-                if k == 1 and stage_of is residual:
-                    scatter(1, second, 0, HALF, "grad_early1")
+                    if (k, g) == (1, 0) and stage_of is weigh:
+                        scatter(1, second, 0, HALF, "grad_early1")
             if k == 0:
-                second = product(1, 6, "early1")
-                early = product(0, 7, "early0")
+                second = product(1, 2, "early1")
+                early = product(0, 3, "early0")
 
         clear_window("h3")
-        scatter(0, early, 0, HALF, "grad_early", "z%d" % (len(steps) - 1))
+        scatter(0, early, 0, HALF, "grad_early", "z_late")
         out_planes = out.rearrange("(p t) c -> t p c", t=PACK)
         for td in range(PACK):
             first = HALF if td < 2 else 0
-            scatter(td, product(td, (0, 1, 4, 5)[td], "final%d" % td), first, N - first, "grad%d" % td)
+            scatter(td, product(td, (4, 5, 0, 1)[td], "final%d" % td), first, N - first, "grad%d" % td)
             nc.sync.dma_start(out_planes[td], windows[td % WINDOWS][:])

@@ -24,7 +24,7 @@ HALF = N // 2
 WINDOWS = 3
 BANK = 2048
 SEAM = 8
-PLACED = {"ts_all": 20480, "h_codes0": 20480, "h_codes1": 22528, "h_scales0": 24576, "h_scales1": 25088, "ts_first": 0, "turned_early": 0, "woven1": 4096, "woven0": 8192, "late_pair": 7168, "turned_late": 12288, "heads1": 16384, "tails0": 16384, "tails1": 18432}
+PLACED = {"last_logits": 26112, "by_slot2_0": 26112, "by_slot2_1": 28160, "by_slot3_0": 30208, "by_slot3_1": 32256, "ts_all": 20480, "h_codes0": 20480, "h_codes1": 22528, "h_scales0": 24576, "h_scales1": 25088, "ts_first": 0, "turned_early": 0, "woven": 4096, "late_pair": 7168, "turned_late": 12288, "heads1": 16384, "tails0": 16384, "tails1": 18432}
 FLOPS = 2 * 2 * D * R * N
 
 
@@ -32,7 +32,6 @@ def tile_attend_gmf_nce_v_kernel(tc, uT, vT, y, us, ts, offs, uoffs, out):
     nc = tc.nc
     with ExitStack() as ctx:
         keep = ctx.enter_context(tc.tile_pool(name="keep", bufs=1))
-        ring = ctx.enter_context(tc.tile_pool(name="ring", bufs=4))
         shared = ctx.enter_context(tc.tile_pool(name="shared", bufs=1))
         psum = ctx.enter_context(tc.psum_pool(name="psum", bufs=1))
 
@@ -127,12 +126,13 @@ def tile_attend_gmf_nce_v_kernel(tc, uT, vT, y, us, ts, offs, uoffs, out):
             words = turned[td // 2][:].bitcast(F32).rearrange("m (d g p u) -> m d g p u", g=PASSES, d=2, u=2)
             nc.scalar.copy(words[:, td % 2], turned_banks[td][:].rearrange("m g u p -> m g p u"))
 
-        woven = [kept([P, K * PACK], BF16, "woven%d" % g) for g in range(PASSES)]
+        woven_all = kept([P, R * PACK], BF16, "woven")
+        woven = [woven_all[:, g * K * PACK : (g + 1) * K * PACK] for g in range(PASSES)]
 
         def weave_heads(n):
             for g in range(PASSES):
                 nc.scalar.copy(
-                    woven[g][:].rearrange("p (t c e d) -> p c t e d", t=PACK, e=2, d=PACK)[:, :, :, :, 2 * n : 2 * n + 2],
+                    woven[g].rearrange("p (t c e d) -> p c t e d", t=PACK, e=2, d=PACK)[:, :, :, :, 2 * n : 2 * n + 2],
                     heads[n][:].rearrange("p (d g c e t) -> p g c t e d", d=2, g=PASSES, e=2, t=PACK)[:, g],
                 )
 
@@ -152,8 +152,10 @@ def tile_attend_gmf_nce_v_kernel(tc, uT, vT, y, us, ts, offs, uoffs, out):
             if td == 3:
                 weave_heads(1)
                 copy_turned(3)
-        x_scales = [kept([P, K], U8, "x_scales%d" % g) for g in range(PASSES)]
-        x_codes = [kept([P, K], U32, "x_codes%d" % g) for g in range(PASSES)]
+        x_scales_all = kept([P, R], U8, "x_scales")
+        x_codes_all = kept([P, R], U32, "x_codes")
+        x_scales = [x_scales_all[:, g * K : (g + 1) * K] for g in range(PASSES)]
+        x_codes = [x_codes_all[:, g * K : (g + 1) * K] for g in range(PASSES)]
         xt_scales = kept([P, PACK * plane], U8, "xt_scales")
 
         def quantise_turned(planes, turned, name, tag):
@@ -177,8 +179,7 @@ def tile_attend_gmf_nce_v_kernel(tc, uT, vT, y, us, ts, offs, uoffs, out):
         nc.vector.tensor_copy(pair[:, N:], v_raw[1][:].indirect(tail_list[:]))
         for k in range(2):
             weave_tails(pair, k * HALF, HALF, 0)
-        for g in range(PASSES):
-            nc.vector.quantize_mx(x_codes[g][:].bitcast(E4M3), x_scales[g][:], woven[g][:])
+        nc.vector.quantize_mx(x_codes_all[:].bitcast(E4M3), x_scales_all[:], woven_all[:])
         w_codes = kept([P, N], U32, "w_codes")
         w_scales = kept([P, N], U8, "w_scales")
         late_pair = kept([P, 2 * N], BF16, "late_pair")
@@ -224,8 +225,11 @@ def tile_attend_gmf_nce_v_kernel(tc, uT, vT, y, us, ts, offs, uoffs, out):
                     rhs=w_codes[:, block].bitcast(E4M3), rhs_scale=w_scales[:, block], start=True, stop=True,
                 )
             tile = z[n][:, :, j * P : (j + 1) * P]
-            nc.vector.tensor_tensor(tile, acc[:], scale[n][:, :, j * P : (j + 1) * P], ALU.mult)
-            nc.scalar.activation(tile, tile, ACT.Sigmoid)
+            logits = tile
+            if (n, j) == (PASSES - 1, 1):
+                logits = kept([P, BLOCKS * K], F32, "last_logits")[:, 0:K].rearrange("p (t i) -> p t i", t=PACK)
+            nc.vector.tensor_tensor(logits, acc[:], scale[n][:, :, j * P : (j + 1) * P], ALU.mult)
+            nc.scalar.activation(tile, logits, ACT.Sigmoid)
 
         def turned_scores(n, j, number, targets):
             g, k = steps[n]
@@ -234,9 +238,9 @@ def tile_attend_gmf_nce_v_kernel(tc, uT, vT, y, us, ts, offs, uoffs, out):
             acc = in_bank(number, [P, K], "score%d_%d" % (n, j))
             nc.tensor.matmul_mx(
                 out=acc[:], lhsT=w_codes[:, block].bitcast(E4M3), lhsT_scale=w_scales[:, block],
-                rhs=x_codes[g][:].bitcast(E4M3), rhs_scale=x_scales[g][:], start=True, stop=True,
+                rhs=x_codes[g].bitcast(E4M3), rhs_scale=x_scales[g], start=True, stop=True,
             )
-            turned = ring.tile([P, K], F32, name="turned", tag="turned")
+            turned = kept([P, K], F32, "by_slot%d_%d" % (n, j))
             nc.scalar.activation(turned[:], acc[:], ACT.Copy, scale=ts_cols[:, b : b + 1])
             for t in range(PACK):
                 nc.tensor.transpose(targets[t], turned[:, t * P : (t + 1) * P], ident[:])

@@ -24,7 +24,7 @@ HALF = N // 2
 WINDOWS = 3
 BANK = 2048
 SEAM = 8
-PLACED = {"last_logits": 26112, "by_slot2_0": 26112, "by_slot2_1": 28160, "by_slot3_0": 30208, "by_slot3_1": 32256, "ts_all": 20480, "h_codes0": 20480, "h_codes1": 22528, "h_scales0": 24576, "h_scales1": 25088, "ts_first": 0, "turned_early": 0, "woven": 4096, "late_pair": 7168, "turned_late": 12288, "heads1": 16384, "tails0": 16384, "tails1": 18432}
+PLACED = {"last_logits": 26112, "by_slot2_0": 26112, "by_slot2_1": 28160, "by_slot3_0": 30208, "by_slot3_1": 32256, "h_codes0": 20480, "h_codes1": 22528, "h_scales0": 24576, "h_scales1": 25088, "ts_first": 0, "turned_early": 0, "woven": 4096, "late_pair": 7168, "turned_late": 12288, "heads1": 16384, "tails0": 16384, "tails1": 18432}
 FLOPS = 2 * 2 * D * R * N
 
 
@@ -90,7 +90,7 @@ def tile_attend_gmf_nce_v_kernel(tc, uT, vT, y, us, ts, offs, uoffs, out):
         ts_rows = in_bank(1, [P, N], "ts_rows")
         for b in range(BLOCKS):
             nc.tensor.transpose(ts_rows[:, b * P : (b + 1) * P], ts_cols[:, b : b + 1].to_broadcast([P, P]), ident[:])
-        ts_all = kept([P, 3 * N], F32, "ts_all")
+        ts_all = kept([P, N], F32, "ts_all")
         ts_first = kept([P, 8 * N], F32, "ts_first")
         nc.scalar.copy(ts_first[:, 0:N], ts_rows[:])
         nc.scalar.copy(ts_all[:, 0:N], ts_rows[:])
@@ -100,12 +100,6 @@ def tile_attend_gmf_nce_v_kernel(tc, uT, vT, y, us, ts, offs, uoffs, out):
             for t in range(PACK):
                 nc.gpsimd.tensor_scalar(scale_of_pass[g][:, t, :], ts_all[:, 0:N] if g + t else ts_first[:, 0:N], row_scale[:, g, t : t + 1], 0.0, ALU.mult, ALU.add)
         scale = [scale_of_pass[g][:, :, k * HALF : (k + 1) * HALF] for g, k in steps]
-
-        h_codes = [kept([P, N], U32, "h_codes%d" % g) for g in range(PASSES)]
-        h_scales = [kept([P, N], U8, "h_scales%d" % g) for g in range(PASSES)]
-        for g in range(PASSES):
-            nc.gpsimd.memset(h_codes[g][:, HALF:], 0)
-            nc.gpsimd.memset(h_scales[g][:, HALF:], 0)
 
         heads = [kept([P, 2 * R], BF16, "heads%d" % n) for n in range(2)]
         plane = PASSES * P
@@ -164,12 +158,12 @@ def tile_attend_gmf_nce_v_kernel(tc, uT, vT, y, us, ts, offs, uoffs, out):
             nc.vector.quantize_mx(codes[:].bitcast(E4M3), xt_scales[:, planes[0] * plane : planes[0] * plane + width], turned[:])
             return [codes[:, n * plane : (n + 1) * plane] for n in range(len(planes))]
 
-        tails = [kept([P, HALF * PACK], BF16, "tails%d" % k) for k in range(2)]
+        tails = [kept([P, (14 if k else PACK) * HALF], BF16, "tails%d" % k)[:, 0 : HALF * PACK] for k in range(2)]
 
         def weave_tails(pairs, first, count, place):
             k, at = divmod(first, HALF)
             nc.scalar.copy(
-                tails[k][:].rearrange("p (i d) -> p i d", d=PACK)[:, at : at + count, place : place + 2],
+                tails[k].rearrange("p (i d) -> p i d", d=PACK)[:, at : at + count, place : place + 2],
                 pairs[:].rearrange("p (e i) -> p i e", e=2)[:, first : first + count],
             )
 
@@ -209,6 +203,11 @@ def tile_attend_gmf_nce_v_kernel(tc, uT, vT, y, us, ts, offs, uoffs, out):
         nc.gpsimd.memset(lent_labels[:, 0:SEAM], 0.0)
         nc.sync.dma_start(lent_labels[:, SEAM:].rearrange("p (t i) -> p t i", i=HALF), y_parts[1][:, 1:, HALF:])
 
+        h_codes = [kept([P, N], U32, "h_codes%d" % g) for g in range(PASSES)]
+        h_scales = [kept([P, N], U8, "h_scales%d" % g) for g in range(PASSES)]
+        for g in range(PASSES):
+            nc.gpsimd.memset(h_codes[g][:, HALF:], 0)
+            nc.gpsimd.memset(h_scales[g][:, HALF:], 0)
         h = {}
         z_late = kept([P, 2 * step], F32, "z_late")
         z = [kept([P, PACK, HALF], F32, "z%d" % n)[:] for n in range(PASSES)]

@@ -23,7 +23,6 @@ BLOCKS = N // P
 HALF = N // 2
 WINDOWS = 3
 BANK = 2048
-SEAM = 8
 PLACED = {"last_logits": 26112, "by_slot2_0": 26112, "by_slot2_1": 28160, "by_slot3_0": 30208, "by_slot3_1": 32256, "h_codes0": 20480, "h_codes1": 22528, "h_scales0": 24576, "h_scales1": 25088, "ts_first": 0, "turned_early": 0, "woven": 4096, "late_pair": 7168, "turned_late": 12288, "heads1": 16384, "tails0": 16384, "tails1": 18432}
 FLOPS = 2 * 2 * D * R * N
 
@@ -35,8 +34,8 @@ def tile_attend_gmf_nce_v_kernel(tc, uT, vT, y, us, ts, offs, uoffs, out):
         shared = ctx.enter_context(tc.tile_pool(name="shared", bufs=1))
         psum = ctx.enter_context(tc.psum_pool(name="psum", bufs=1))
 
-        def in_bank(number, shape, name):
-            return psum.tile(shape, F32, name=name, tag=name, offset=number * BANK)
+        def in_bank(number, shape, name, dtype=F32):
+            return psum.tile(shape, dtype, name=name, tag=name, offset=number * BANK)
 
         def kept(shape, dtype, name, tag=None):
             if (tag or name) in PLACED:
@@ -64,6 +63,8 @@ def tile_attend_gmf_nce_v_kernel(tc, uT, vT, y, us, ts, offs, uoffs, out):
 
         clear_window(None)
         clear_window(None)
+        ident_bf = kept([P, P], BF16, "ident_bf")
+        make_identity(nc, ident_bf[:])
 
         nc.scalar.dma_start(ts_window[P - 1 : P, :], ts[0:1, :])
         nc.sync.dma_start(tail_list[:], offs)
@@ -80,26 +81,39 @@ def tile_attend_gmf_nce_v_kernel(tc, uT, vT, y, us, ts, offs, uoffs, out):
         u_raw.extend(load(u_planes[td], "u_raw%d" % td) for td in range(1, PACK))
         v_raw = [load(v_planes[td], "v_raw%d" % td) for td in range(PACK)]
 
-        ts_cols = kept([P, BLOCKS], F32, "ts_cols")
+        ts_cols = kept([P, 2], F32, "ts_cols")
+        ts_minus = kept([P, 2], F32, "ts_minus")
         ts_picked = kept([P, N], F32, "ts_picked")
         nc.vector.tensor_copy(ts_picked[:], ts_window[:].indirect(tail_list[:]))
         bank = in_bank(0, [P, BLOCKS, P], "ts_turned")
         for b in range(BLOCKS):
             nc.tensor.transpose(bank[:, b, :], ts_picked[:, b * P : (b + 1) * P], ident[:])
-        nc.scalar.copy(ts_cols[:], bank[:, :, P - 1])
-        ts_rows = in_bank(1, [P, N], "ts_rows")
-        for b in range(BLOCKS):
+        nc.scalar.copy(ts_cols[:], bank[:, 0:2, P - 1])
+        nc.scalar.activation(ts_minus[:], bank[:, 2:4, P - 1], ACT.Copy, scale=-1.0)
+        ts_rows = in_bank(1, [P, HALF], "ts_rows")
+        for b in range(2):
             nc.tensor.transpose(ts_rows[:, b * P : (b + 1) * P], ts_cols[:, b : b + 1].to_broadcast([P, P]), ident[:])
-        ts_all = kept([P, N], F32, "ts_all")
+        ts_all = kept([P, HALF], F32, "ts_all")
         ts_first = kept([P, 8 * N], F32, "ts_first")
-        nc.scalar.copy(ts_first[:, 0:N], ts_rows[:])
-        nc.scalar.copy(ts_all[:, 0:N], ts_rows[:])
-        steps = [(g, k) for k in range(2) for g in range(PASSES)]
-        scale_of_pass = [kept([P, PACK, N], F32, "scale%d" % g) for g in range(PASSES)]
+        nc.scalar.copy(ts_first[:, 0:HALF], ts_rows[:])
+        nc.scalar.copy(ts_all[:], ts_rows[:])
+        us_rows = [in_bank(2 + g, [P, K], "us_rows%d" % g) for g in range(PASSES)]
         for g in range(PASSES):
             for t in range(PACK):
-                nc.gpsimd.tensor_scalar(scale_of_pass[g][:, t, :], ts_all[:, 0:N] if g + t else ts_first[:, 0:N], row_scale[:, g, t : t + 1], 0.0, ALU.mult, ALU.add)
-        scale = [scale_of_pass[g][:, :, k * HALF : (k + 1) * HALF] for g, k in steps]
+                nc.tensor.transpose(us_rows[g][:, t * P : (t + 1) * P], row_scale[:, g, t : t + 1].to_broadcast([P, P]), ident[:])
+        scale_by_slot = {}
+
+        def spread_by_slot(g, tag):
+            scale_by_slot[g] = kept([P, 2, K], F32, "scale_by_slot%d" % g, tag)
+            for j in range(2):
+                nc.scalar.activation(scale_by_slot[g][:, j, :], us_rows[g][:], ACT.Copy, scale=ts_minus[:, j : j + 1])
+
+        spread_by_slot(0, None)
+        steps = [(g, k) for k in range(2) for g in range(PASSES)]
+        scale = [kept([P, PACK, HALF], F32, "scale%d" % g)[:] for g in range(PASSES)]
+        for g in range(PASSES):
+            for t in range(PACK):
+                nc.gpsimd.tensor_scalar(scale[g][:, t, :], ts_all[:] if g + t else ts_first[:, 0:HALF], row_scale[:, g, t : t + 1], 0.0, ALU.mult, ALU.add)
 
         heads = [kept([P, 2 * R], BF16, "heads%d" % n) for n in range(2)]
         plane = PASSES * P
@@ -173,6 +187,7 @@ def tile_attend_gmf_nce_v_kernel(tc, uT, vT, y, us, ts, offs, uoffs, out):
         nc.vector.tensor_copy(pair[:, N:], v_raw[1][:].indirect(tail_list[:]))
         for k in range(2):
             weave_tails(pair, k * HALF, HALF, 0)
+        spread_by_slot(1, "pair")
         nc.vector.quantize_mx(x_codes_all[:].bitcast(E4M3), x_scales_all[:], woven_all[:])
         w_codes = kept([P, N], U32, "w_codes")
         w_scales = kept([P, N], U8, "w_scales")
@@ -190,18 +205,10 @@ def tile_attend_gmf_nce_v_kernel(tc, uT, vT, y, us, ts, offs, uoffs, out):
 
         y_parts = y[0].rearrange("(g p t) i -> g p t i", g=PASSES, t=PACK)
         labels = []
-        for g in range(PASSES):
-            tile = kept([P, PACK, HALF], F32, "labels%d" % g)
-            nc.sync.dma_start(tile[:], y_parts[g][:, :, 0:HALF])
+        for n, (g, k) in enumerate(steps):
+            tile = kept([P, PACK, HALF], F32, "labels%d" % n)
+            nc.sync.dma_start(tile[:], y_parts[g][:, :, k * HALF : (k + 1) * HALF])
             labels.append(tile)
-        step = PACK * HALF
-        own = step + HALF
-        late_labels = kept([P, own], F32, "late_labels")
-        nc.sync.dma_start(late_labels[:, 0:step].rearrange("p (t i) -> p t i", t=PACK), y_parts[0][:, :, HALF:])
-        nc.sync.dma_start(late_labels[:, step:], y_parts[1][:, 0, HALF:])
-        lent_labels = kept([P, SEAM + 2 * step - own], F32, "lent_labels")
-        nc.gpsimd.memset(lent_labels[:, 0:SEAM], 0.0)
-        nc.sync.dma_start(lent_labels[:, SEAM:].rearrange("p (t i) -> p t i", i=HALF), y_parts[1][:, 1:, HALF:])
 
         h_codes = [kept([P, N], U32, "h_codes%d" % g) for g in range(PASSES)]
         h_scales = [kept([P, N], U8, "h_scales%d" % g) for g in range(PASSES)]
@@ -209,9 +216,7 @@ def tile_attend_gmf_nce_v_kernel(tc, uT, vT, y, us, ts, offs, uoffs, out):
             nc.gpsimd.memset(h_codes[g][:, HALF:], 0)
             nc.gpsimd.memset(h_scales[g][:, HALF:], 0)
         h = {}
-        z_late = kept([P, 2 * step], F32, "z_late")
-        z = [kept([P, PACK, HALF], F32, "z%d" % n)[:] for n in range(PASSES)]
-        z.extend(z_late[:, g * step : (g + 1) * step].rearrange("p (t i) -> p t i", t=PACK) for g in range(PASSES))
+        z = [kept([P, PACK, HALF], F32, "z%d" % n)[:] for n in range(len(steps))]
 
         def direct_scores(n, j, number):
             g, k = steps[n]
@@ -230,7 +235,7 @@ def tile_attend_gmf_nce_v_kernel(tc, uT, vT, y, us, ts, offs, uoffs, out):
             nc.vector.tensor_tensor(logits, acc[:], scale[n][:, :, j * P : (j + 1) * P], ALU.mult)
             nc.scalar.activation(tile, logits, ACT.Sigmoid)
 
-        def turned_scores(n, j, number, targets):
+        def turned_scores(n, j, number):
             g, k = steps[n]
             b = 2 * k + j
             block = slice(b * P, (b + 1) * P)
@@ -240,49 +245,64 @@ def tile_attend_gmf_nce_v_kernel(tc, uT, vT, y, us, ts, offs, uoffs, out):
                 rhs=x_codes[g].bitcast(E4M3), rhs_scale=x_scales[g], start=True, stop=True,
             )
             turned = kept([P, K], F32, "by_slot%d_%d" % (n, j))
-            nc.scalar.activation(turned[:], acc[:], ACT.Copy, scale=ts_cols[:, b : b + 1])
-            for t in range(PACK):
-                nc.tensor.transpose(targets[t], turned[:, t * P : (t + 1) * P], ident[:])
+            nc.scalar.activation(turned[:], acc[:], ACT.Copy, scale=ts_minus[:, j : j + 1])
+            return turned
 
         def close_turned(n, first, width, sources):
             g, k = steps[n]
             for t in range(PACK):
                 nc.scalar.activation(z[n][:, t, first : first + width], sources[t], ACT.Sigmoid, scale=row_scale[:, g, t : t + 1])
 
-        def turned_step(n, scores, turns):
+        def turned_step(n, turns):
             banks = [in_bank(number, [P, 2, HALF], "turn%d_%d" % (n, u)) for u, number in enumerate(turns)]
             for j in range(2):
-                turned_scores(n, j, scores[j], [banks[t // 2][:, t % 2, j * P : (j + 1) * P] for t in range(PACK)])
+                for t in range(PACK):
+                    nc.tensor.transpose(banks[t // 2][:, t % 2, j * P : (j + 1) * P], by_slot[n][j][:, t * P : (t + 1) * P], ident[:])
             close_turned(n, 0, HALF, [banks[t // 2][:, t % 2, :] for t in range(PACK)])
 
         def residual(n):
-            if n < PASSES:
-                nc.vector.tensor_tensor(z[n], z[n], labels[n][:], ALU.subtract)
-            elif n == PASSES:
-                for cols in (slice(0, step), slice(step, own)):
-                    nc.vector.tensor_tensor(z_late[:, cols], z_late[:, cols], late_labels[:, cols], ALU.subtract)
-            else:
-                nc.gpsimd.tensor_tensor(z_late[:, own - SEAM :], z_late[:, own - SEAM :], lent_labels[:], ALU.subtract)
-
-        def pieces(n):
-            g, k = steps[n]
-            width = HALF
-            return [(g, c0, k * HALF + c0, width) for c0 in range(0, HALF, width)]
+            nc.vector.tensor_tensor(z[n], z[n], labels[n][:], ALU.subtract)
 
         def weigh(n):
-            for g, c0, i0, width in pieces(n):
-                h[n] = kept([P, HALF * PACK], BF16, "h%d" % n, None if n else "labels1")
-                nc.vector.tensor_tensor(
-                    h[n][:].rearrange("p (c i t) -> p c t i", i=4, t=PACK),
-                    z[n][:, :, c0 : c0 + width].rearrange("p t (c i) -> p c t i", i=4),
-                    scale[n][:, :, c0 : c0 + width].rearrange("p t (c i) -> p c t i", i=4),
-                    ALU.mult,
+            h[n] = kept([P, HALF * PACK], BF16, "h%d" % n, None if n else "labels1")
+            nc.vector.tensor_tensor(
+                h[n][:].rearrange("p (c i t) -> p c t i", i=4, t=PACK),
+                z[n].rearrange("p t (c i) -> p c t i", i=4),
+                scale[n].rearrange("p t (c i) -> p c t i", i=4),
+                ALU.mult,
+            )
+
+        sums = {}
+
+        def open_sum(n, j, number):
+            sums[n, j] = in_bank(number, [P, PACK, P], "sum%d_%d" % (n, j))
+            for t in range(PACK):
+                nc.tensor.matmul(sums[n, j][:, t, :], labels[n][:, t, j * P : (j + 1) * P], ident[:], start=(t == 0), stop=False, is_transpose=True)
+
+        def close_sums(n):
+            for t in range(PACK):
+                for j in range(2):
+                    nc.tensor.matmul(sums[n, j][:, t, :], z[n][:, t, j * P : (j + 1) * P], ident[:], start=False, stop=(t == PACK - 1), is_transpose=True)
+
+        h_by_slot = {}
+
+        def weigh_by_slot(n, numbers):
+            g, k = steps[n]
+            h_by_slot[n] = kept([P, 2, K], BF16, "h_by_slot%d" % n)
+            h[n] = kept([P, HALF * PACK], BF16, "h%d" % n)
+            for j, number in enumerate(numbers):
+                nc.vector.scalar_tensor_tensor(
+                    h_by_slot[n][:, j, :], sums[n, j][:].rearrange("p t s -> p (t s)"), 1.0, scale_by_slot[g][:, j, :], ALU.subtract, ALU.mult
                 )
+                bank = in_bank(number, [P, PACK, P], "h_turned%d_%d" % (n, j), BF16)
+                for t in range(PACK):
+                    nc.tensor.transpose(bank[:, t, :], h_by_slot[n][:, j, t * P : (t + 1) * P], ident_bf[:])
+                nc.scalar.copy(h[n][:, j * K : (j + 1) * K].rearrange("p (i t) -> p i t", t=PACK), bank[:].rearrange("p t i -> p i t"))
 
         def quantise(n):
-            for g, c0, i0, width in pieces(n):
-                slots = slice(i0, i0 + width)
-                nc.vector.quantize_mx(h_codes[g][:, slots].bitcast(E5M2), h_scales[g][:, slots], h[n][:])
+            g, k = steps[n]
+            slots = slice(k * HALF, (k + 1) * HALF)
+            nc.vector.quantize_mx(h_codes[g][:, slots].bitcast(E5M2), h_scales[g][:, slots], h[n][:])
 
         def product(td, number, name):
             acc = in_bank(number, [P, N], name)
@@ -303,22 +323,30 @@ def tile_attend_gmf_nce_v_kernel(tc, uT, vT, y, us, ts, offs, uoffs, out):
         for n in range(PASSES):
             for j in range(2):
                 direct_scores(n, j, 2 + 2 * n + j)
-        turned_step(2, (2, 3), (0, 1))
-        turned_step(3, (4, 5), (6, 7))
-        for k in range(2):
-            for stage_of in (residual, weigh, quantise):
-                for g in range(PASSES):
-                    stage_of(k * PASSES + g)
-                    if (k, g) == (1, 0) and stage_of is weigh:
-                        scatter(1, second, 0, HALF, "grad_early1")
-            if k == 0:
-                second = product(1, 2, "early1")
-                early = product(0, 3, "early0")
+        by_slot = {n: [turned_scores(n, j, 2 * n - 2 + j) for j in range(2)] for n in (2, 3)}
+        for j in range(2):
+            open_sum(2, j, 6 + j)
+        for j in range(2):
+            open_sum(3, j, j)
+        turned_step(2, (2, 3))
+        turned_step(3, (4, 5))
+        close_sums(2)
+        close_sums(3)
+        for stage_of in (residual, weigh, quantise):
+            for g in range(PASSES):
+                stage_of(g)
+        second = product(1, 2, "early1")
+        weigh_by_slot(2, (4, 5))
+        early = product(0, 3, "early0")
+        weigh_by_slot(3, (6, 7))
+        scatter(1, second, 0, HALF, "grad_early1")
+        quantise(2)
+        quantise(3)
 
         clear_window("h3")
-        scatter(0, early, 0, HALF, "grad_early", "z_late")
+        scatter(0, early, 0, HALF, "grad_early", "h_by_slot3")
         out_planes = out.rearrange("(p t) c -> t p c", t=PACK)
         for td in range(PACK):
             first = HALF if td < 2 else 0
-            scatter(td, product(td, (4, 5, 0, 1)[td], "final%d" % td), first, N - first, "grad%d" % td)
+            scatter(td, product(td, (0, 1, 4, 5)[td], "final%d" % td), first, N - first, "grad%d" % td)
             nc.sync.dma_start(out_planes[td], windows[td % WINDOWS][:])

@@ -63,8 +63,6 @@ def tile_attend_gmf_nce_v_kernel(tc, uT, vT, y, us, ts, offs, uoffs, out):
 
         clear_window(None)
         clear_window(None)
-        ident_bf = kept([P, P], BF16, "ident_bf")
-        make_identity(nc, ident_bf[:])
 
         nc.scalar.dma_start(ts_window[P - 1 : P, :], ts[0:1, :])
         nc.sync.dma_start(tail_list[:], offs)
@@ -106,7 +104,7 @@ def tile_attend_gmf_nce_v_kernel(tc, uT, vT, y, us, ts, offs, uoffs, out):
         def spread_by_slot(g, tag):
             scale_by_slot[g] = kept([P, 2, K], F32, "scale_by_slot%d" % g, tag)
             for j in range(2):
-                nc.scalar.activation(scale_by_slot[g][:, j, :], us_rows[g][:], ACT.Copy, scale=ts_minus[:, j : j + 1])
+                nc.scalar.activation(scale_by_slot[g][:, j, :].rearrange("p (s t) -> p s t", t=PACK), us_rows[g][:].rearrange("p (t s) -> p s t", t=PACK), ACT.Copy, scale=ts_minus[:, j : j + 1])
 
         spread_by_slot(0, None)
         steps = [(g, k) for k in range(2) for g in range(PASSES)]
@@ -292,12 +290,14 @@ def tile_attend_gmf_nce_v_kernel(tc, uT, vT, y, us, ts, offs, uoffs, out):
             h[n] = kept([P, HALF * PACK], BF16, "h%d" % n)
             for j, number in enumerate(numbers):
                 nc.vector.scalar_tensor_tensor(
-                    h_by_slot[n][:, j, :], sums[n, j][:].rearrange("p t s -> p (t s)"), 1.0, scale_by_slot[g][:, j, :], ALU.subtract, ALU.mult
+                    h_by_slot[n][:, j, :].rearrange("p (s t) -> p s t", t=PACK), sums[n, j][:].rearrange("p t s -> p s t"), 1.0,
+                    scale_by_slot[g][:, j, :].rearrange("p (s t) -> p s t", t=PACK), ALU.subtract, ALU.mult,
                 )
-                bank = in_bank(number, [P, PACK, P], "h_turned%d_%d" % (n, j), BF16)
-                for t in range(PACK):
-                    nc.tensor.transpose(bank[:, t, :], h_by_slot[n][:, j, t * P : (t + 1) * P], ident_bf[:])
-                nc.scalar.copy(h[n][:, j * K : (j + 1) * K].rearrange("p (i t) -> p i t", t=PACK), bank[:].rearrange("p t i -> p i t"))
+                bank = in_bank(number, [P, 2, P], "h_turned%d_%d" % (n, j))
+                words = h_by_slot[n][:, j, :].bitcast(F32)
+                for u in range(2):
+                    nc.tensor.transpose(bank[:, u, :], words[:, u : K // 2 : 2], ident[:])
+                nc.scalar.copy(h[n][:, j * K : (j + 1) * K].bitcast(F32).rearrange("p (i u) -> p i u", u=2), bank[:].rearrange("p u i -> p i u"))
 
         def quantise(n):
             g, k = steps[n]
@@ -335,10 +335,10 @@ def tile_attend_gmf_nce_v_kernel(tc, uT, vT, y, us, ts, offs, uoffs, out):
         for stage_of in (residual, weigh, quantise):
             for g in range(PASSES):
                 stage_of(g)
-        second = product(1, 2, "early1")
-        weigh_by_slot(2, (4, 5))
-        early = product(0, 3, "early0")
+        second = product(1, 5, "early1")
+        weigh_by_slot(2, (2, 3))
         weigh_by_slot(3, (6, 7))
+        early = product(0, 0, "early0")
         scatter(1, second, 0, HALF, "grad_early1")
         quantise(2)
         quantise(3)
@@ -348,5 +348,5 @@ def tile_attend_gmf_nce_v_kernel(tc, uT, vT, y, us, ts, offs, uoffs, out):
         out_planes = out.rearrange("(p t) c -> t p c", t=PACK)
         for td in range(PACK):
             first = HALF if td < 2 else 0
-            scatter(td, product(td, (0, 1, 4, 5)[td], "final%d" % td), first, N - first, "grad%d" % td)
+            scatter(td, product(td, (1, 4, 2, 3)[td], "final%d" % td), first, N - first, "grad%d" % td)
             nc.sync.dma_start(out_planes[td], windows[td % WINDOWS][:])

@@ -23,7 +23,7 @@ BLOCKS = N // P
 HALF = N // 2
 WINDOWS = 3
 BANK = 2048
-PLACED = {"last_logits": 26112, "by_slot2_0": 26112, "by_slot2_1": 28160, "by_slot3_0": 30208, "by_slot3_1": 32256, "h_codes0": 20480, "h_codes1": 22528, "h_scales0": 24576, "h_scales1": 25088, "ts_first": 0, "turned_early": 0, "woven": 4096, "late_pair": 7168, "turned_late": 12288, "heads1": 16384, "tails0": 16384, "tails1": 18432}
+PLACED = {"last_logits": 26112, "by_slot2_1": 28160, "by_slot3_0": 30208, "by_slot3_1": 32256, "h_codes0": 20480, "h_codes1": 22528, "h_scales0": 24576, "h_scales1": 25088, "ts_first": 0, "turned_early": 0, "woven": 4096, "late_pair": 7168, "turned_late": 12288, "heads1": 16384, "tails0": 16384, "tails1": 18432}
 FLOPS = 2 * 2 * D * R * N
 
 
@@ -79,21 +79,21 @@ def tile_attend_gmf_nce_v_kernel(tc, uT, vT, y, us, ts, offs, uoffs, out):
         u_raw.extend(load(u_planes[td], "u_raw%d" % td) for td in range(1, PACK))
         v_raw = [load(v_planes[td], "v_raw%d" % td) for td in range(PACK)]
 
-        ts_cols = kept([P, 2], F32, "ts_cols")
+        ts_cols = kept([P, 3], F32, "ts_cols")
         ts_minus = kept([P, 2], F32, "ts_minus")
         ts_picked = kept([P, N], F32, "ts_picked")
         nc.vector.tensor_copy(ts_picked[:], ts_window[:].indirect(tail_list[:]))
         bank = in_bank(0, [P, BLOCKS, P], "ts_turned")
         for b in range(BLOCKS):
             nc.tensor.transpose(bank[:, b, :], ts_picked[:, b * P : (b + 1) * P], ident[:])
-        nc.scalar.copy(ts_cols[:], bank[:, 0:2, P - 1])
+        nc.scalar.copy(ts_cols[:], bank[:, 0:3, P - 1])
         nc.scalar.activation(ts_minus[:], bank[:, 2:4, P - 1], ACT.Copy, scale=-1.0)
-        ts_rows = in_bank(1, [P, HALF], "ts_rows")
-        for b in range(2):
+        ts_rows = in_bank(1, [P, 3 * P], "ts_rows")
+        for b in range(3):
             nc.tensor.transpose(ts_rows[:, b * P : (b + 1) * P], ts_cols[:, b : b + 1].to_broadcast([P, P]), ident[:])
-        ts_all = kept([P, HALF], F32, "ts_all")
+        ts_all = kept([P, 3 * P], F32, "ts_all")
         ts_first = kept([P, 8 * N], F32, "ts_first")
-        nc.scalar.copy(ts_first[:, 0:HALF], ts_rows[:])
+        nc.scalar.copy(ts_first[:, 0 : 3 * P], ts_rows[:])
         nc.scalar.copy(ts_all[:], ts_rows[:])
         us_rows = [in_bank(2 + g, [P, K], "us_rows%d" % g) for g in range(PASSES)]
         for g in range(PASSES):
@@ -108,10 +108,12 @@ def tile_attend_gmf_nce_v_kernel(tc, uT, vT, y, us, ts, offs, uoffs, out):
 
         spread_by_slot(0, None)
         steps = [(g, k) for k in range(2) for g in range(PASSES)]
-        scale = [kept([P, PACK, HALF], F32, "scale%d" % g)[:] for g in range(PASSES)]
+        widths = (3 * P, HALF)
+        scale_of_pass = [kept([P, PACK, widths[g]], F32, "scale%d" % g) for g in range(PASSES)]
+        scale = [scale_of_pass[0][:, :, 0:HALF], scale_of_pass[1][:], scale_of_pass[0][:, :, HALF:]]
         for g in range(PASSES):
             for t in range(PACK):
-                nc.gpsimd.tensor_scalar(scale[g][:, t, :], ts_all[:] if g + t else ts_first[:, 0:HALF], row_scale[:, g, t : t + 1], 0.0, ALU.mult, ALU.add)
+                nc.gpsimd.tensor_scalar(scale_of_pass[g][:, t, :], (ts_all if g + t else ts_first)[:, 0 : widths[g]], row_scale[:, g, t : t + 1], 0.0, ALU.mult, ALU.add)
 
         heads = [kept([P, 2 * R], BF16, "heads%d" % n) for n in range(2)]
         plane = PASSES * P
@@ -228,10 +230,10 @@ def tile_attend_gmf_nce_v_kernel(tc, uT, vT, y, us, ts, offs, uoffs, out):
                 )
             tile = z[n][:, :, j * P : (j + 1) * P]
             logits = tile
-            if (n, j) == (PASSES - 1, 1):
+            if n == PASSES:
                 logits = kept([P, BLOCKS * K], F32, "last_logits")[:, 0:K].rearrange("p (t i) -> p t i", t=PACK)
             nc.vector.tensor_tensor(logits, acc[:], scale[n][:, :, j * P : (j + 1) * P], ALU.mult)
-            nc.scalar.activation(tile, logits, ACT.Sigmoid)
+            nc.scalar.activation(tile, logits, ACT.Sigmoid, scale=-1.0 if k else 1.0)
 
         def turned_scores(n, j, number):
             g, k = steps[n]
@@ -246,20 +248,19 @@ def tile_attend_gmf_nce_v_kernel(tc, uT, vT, y, us, ts, offs, uoffs, out):
             nc.scalar.activation(turned[:], acc[:], ACT.Copy, scale=ts_minus[:, j : j + 1])
             return turned
 
-        def close_turned(n, first, width, sources):
+        def turned_step(n, blocks, turns):
             g, k = steps[n]
-            for t in range(PACK):
-                nc.scalar.activation(z[n][:, t, first : first + width], sources[t], ACT.Sigmoid, scale=row_scale[:, g, t : t + 1])
-
-        def turned_step(n, turns):
-            banks = [in_bank(number, [P, 2, HALF], "turn%d_%d" % (n, u)) for u, number in enumerate(turns)]
-            for j in range(2):
+            share = PACK // len(turns)
+            banks = [in_bank(number, [P, share, len(blocks) * P], "turn%d_%d" % (n, u)) for u, number in enumerate(turns)]
+            for at, j in enumerate(blocks):
                 for t in range(PACK):
-                    nc.tensor.transpose(banks[t // 2][:, t % 2, j * P : (j + 1) * P], by_slot[n][j][:, t * P : (t + 1) * P], ident[:])
-            close_turned(n, 0, HALF, [banks[t // 2][:, t % 2, :] for t in range(PACK)])
+                    nc.tensor.transpose(banks[t // share][:, t % share, at * P : (at + 1) * P], by_slot[n, j][:, t * P : (t + 1) * P], ident[:])
+            for t in range(PACK):
+                nc.scalar.activation(z[n][:, t, blocks[0] * P :], banks[t // share][:, t % share, :], ACT.Sigmoid, scale=row_scale[:, g, t : t + 1])
 
         def residual(n):
-            nc.vector.tensor_tensor(z[n], z[n], labels[n][:], ALU.subtract)
+            first = 0 if n else P
+            nc.vector.tensor_tensor(z[n][:, :, first:], z[n][:, :, first:], labels[n][:, :, first:], ALU.subtract)
 
         def weigh(n):
             h[n] = kept([P, HALF * PACK], BF16, "h%d" % n, None if n else "labels1")
@@ -278,8 +279,8 @@ def tile_attend_gmf_nce_v_kernel(tc, uT, vT, y, us, ts, offs, uoffs, out):
                 nc.tensor.matmul(sums[n, j][:, t, :], labels[n][:, t, j * P : (j + 1) * P], ident[:], start=(t == 0), stop=False, is_transpose=True)
 
         def close_sums(n):
-            for t in range(PACK):
-                for j in range(2):
+            for t, j in [(t, j) for t in range(PACK) for j in range(2)] if n > PASSES else [(t, j) for j in range(2) for t in range(PACK)]:
+                if True:
                     nc.tensor.matmul(sums[n, j][:, t, :], z[n][:, t, j * P : (j + 1) * P], ident[:], start=False, stop=(t == PACK - 1), is_transpose=True)
 
         h_by_slot = {}
@@ -323,13 +324,15 @@ def tile_attend_gmf_nce_v_kernel(tc, uT, vT, y, us, ts, offs, uoffs, out):
         for n in range(PASSES):
             for j in range(2):
                 direct_scores(n, j, 2 + 2 * n + j)
-        by_slot = {n: [turned_scores(n, j, 2 * n - 2 + j) for j in range(2)] for n in (2, 3)}
+        nc.gpsimd.tensor_tensor(z[0][:, :, 0:P], z[0][:, :, 0:P], labels[0][:, :, 0:P], ALU.subtract)
+        direct_scores(2, 0, 2)
+        by_slot = {(n, j): turned_scores(n, j, 2 * n - 2 + j) for n, j in ((2, 1), (3, 0), (3, 1))}
         for j in range(2):
             open_sum(2, j, 6 + j)
         for j in range(2):
             open_sum(3, j, j)
-        turned_step(2, (2, 3))
-        turned_step(3, (4, 5))
+        turned_step(2, [1], [3])
+        turned_step(3, [0, 1], [4, 5])
         close_sums(2)
         close_sums(3)
         for stage_of in (residual, weigh, quantise):

@@ -305,9 +305,9 @@ def tile_attend_gmf_nce_v_kernel(tc, uT, vT, y, us, ts, offs, uoffs, out):
             slots = slice(k * HALF, (k + 1) * HALF)
             nc.vector.quantize_mx(h_codes[g][:, slots].bitcast(E5M2), h_scales[g][:, slots], h[n][:])
 
-        def product(td, number, name):
+        def product(td, number, name, first):
             acc = in_bank(number, [P, N], name)
-            order = range(PASSES) if td == 0 else range(PASSES - 1, -1, -1)
+            order = (first, 1 - first)
             for g in order:
                 nc.tensor.matmul_mx(
                     out=acc[:], lhsT=xt_codes[td][:, g * P : (g + 1) * P].bitcast(E4M3),
@@ -338,10 +338,10 @@ def tile_attend_gmf_nce_v_kernel(tc, uT, vT, y, us, ts, offs, uoffs, out):
         for stage_of in (residual, weigh, quantise):
             for g in range(PASSES):
                 stage_of(g)
-        second = product(1, 5, "early1")
-        weigh_by_slot(2, (2, 3))
+        second = product(1, 2, "early1", 0)
+        weigh_by_slot(2, (3, 5))
         weigh_by_slot(3, (6, 7))
-        early = product(0, 0, "early0")
+        early = product(0, 0, "early0", 0)
         scatter(1, second, 0, HALF, "grad_early1")
         quantise(2)
         quantise(3)
@@ -351,5 +351,5 @@ def tile_attend_gmf_nce_v_kernel(tc, uT, vT, y, us, ts, offs, uoffs, out):
         out_planes = out.rearrange("(p t) c -> t p c", t=PACK)
         for td in range(PACK):
             first = HALF if td < 2 else 0
-            scatter(td, product(td, (1, 4, 2, 3)[td], "final%d" % td), first, N - first, "grad%d" % td)
+            scatter(td, product(td, (1, 4, 2, 3)[td], "final%d" % td, min(td, 1)), first, N - first, "grad%d" % td)
             nc.sync.dma_start(out_planes[td], windows[td % WINDOWS][:])

@@ -21,9 +21,7 @@ K = P * PACK
 PASSES = R // K
 BLOCKS = N // P
 HALF = N // 2
-WINDOWS = 3
 BANK = 2048
-PLACED = {"last_logits": 26112, "by_slot2_1": 28160, "by_slot3_0": 30208, "by_slot3_1": 32256, "h_codes0": 20480, "h_codes1": 22528, "h_scales0": 24576, "h_scales1": 25088, "ts_first": 0, "turned_early": 0, "woven": 4096, "late_pair": 7168, "turned_late": 12288, "heads1": 16384, "tails0": 16384, "tails1": 18432}
 FLOPS = 2 * 2 * D * R * N
 
 
@@ -31,21 +29,19 @@ def tile_attend_gmf_nce_v_kernel(tc, uT, vT, y, us, ts, offs, uoffs, out):
     nc = tc.nc
     with ExitStack() as ctx:
         keep = ctx.enter_context(tc.tile_pool(name="keep", bufs=1))
-        shared = ctx.enter_context(tc.tile_pool(name="shared", bufs=1))
         psum = ctx.enter_context(tc.psum_pool(name="psum", bufs=1))
 
-        def in_bank(number, shape, name, dtype=F32):
-            return psum.tile(shape, dtype, name=name, tag=name, offset=number * BANK)
+        def in_bank(number, shape, name):
+            return psum.tile(shape, F32, name=name, tag=name, offset=number * BANK)
 
         def kept(shape, dtype, name, tag=None):
-            if (tag or name) in PLACED:
-                return shared.tile(shape, dtype, name=name, tag=tag or name, align_bytes=64, offset=PLACED[tag or name])
             return keep.tile(shape, dtype, name=name, tag=tag or name, align_bytes=64)
 
         tail_list = kept([P, N // 16], U16, "tail_list")
         head_list = kept([P, R // 16], U16, "head_list")
-        u_planes = uT.rearrange("(p t) c -> t p c", t=PACK)
-        v_planes = vT.rearrange("(p t) c -> t p c", t=PACK)
+
+        def listed(window, offsets, first, count):
+            return window[:].indirect(offsets[:, first // 16 : (first + count) // 16])
 
         warm = kept([P, 2], F32, "warm")
         nc.gpsimd.memset(warm[:, 0:1], 0.0)
@@ -54,221 +50,154 @@ def tile_attend_gmf_nce_v_kernel(tc, uT, vT, y, us, ts, offs, uoffs, out):
         make_identity(nc, ident[:])
         ts_window = kept([P, T], F32, "ts_window")
         nc.gpsimd.memset(ts_window[0 : P - 1, :].bitcast(I32), 0)
-        windows = []
-
-        def clear_window(tag):
-            window = kept([P, T], F32, "window%d" % len(windows), tag)
+        windows = [kept([P, T], F32, "window%d" % td) for td in range(PACK - 1)]
+        for window in windows:
             nc.gpsimd.memset(window[:].bitcast(I32), 0)
-            windows.append(window)
-
-        clear_window(None)
-        clear_window(None)
 
         nc.scalar.dma_start(ts_window[P - 1 : P, :], ts[0:1, :])
         nc.sync.dma_start(tail_list[:], offs)
         row_scale = kept([P, PASSES, PACK], F32, "row_scale")
         nc.scalar.dma_start(row_scale[:], us[0].rearrange("(g p t) o -> p g (t o)", g=PASSES, t=PACK))
 
-        def load(source, name, tag=None):
-            tile = kept([P, T], F32, name, tag)
-            nc.sync.dma_start(tile[:], source)
+        def load_plane(table, td, name):
+            tile = kept([P, T], F32, name)
+            nc.sync.dma_start(tile[:], table.rearrange("(p t) c -> t p c", t=PACK)[td])
             return tile
 
-        u_raw = [load(u_planes[0], "u_raw0")]
+        u_raw = [load_plane(uT, 0, "u_raw0")]
         nc.sync.dma_start(head_list[:], uoffs)
-        u_raw.extend(load(u_planes[td], "u_raw%d" % td) for td in range(1, PACK))
-        v_raw = [load(v_planes[td], "v_raw%d" % td) for td in range(PACK)]
+        u_raw.extend(load_plane(uT, td, "u_raw%d" % td) for td in range(1, PACK))
+        v_raw = [load_plane(vT, td, "v_raw%d" % td) for td in range(PACK)]
+        steps = [(g, k) for k in range(2) for g in range(PASSES)]
+        y_rows = y[0].rearrange("(g p t) i -> g p t i", g=PASSES, t=PACK)
+        labels = []
+        for n, (g, k) in enumerate(steps):
+            tile = kept([P, PACK, HALF], F32, "labels%d" % n)
+            nc.sync.dma_start(tile[:], y_rows[g][:, :, k * HALF : (k + 1) * HALF])
+            labels.append(tile)
 
-        ts_cols = kept([P, 3], F32, "ts_cols")
-        ts_minus = kept([P, 2], F32, "ts_minus")
         ts_picked = kept([P, N], F32, "ts_picked")
-        nc.vector.tensor_copy(ts_picked[:], ts_window[:].indirect(tail_list[:]))
+        nc.vector.tensor_copy(ts_picked[:], listed(ts_window, tail_list, 0, N))
         bank = in_bank(0, [P, BLOCKS, P], "ts_turned")
         for b in range(BLOCKS):
             nc.tensor.transpose(bank[:, b, :], ts_picked[:, b * P : (b + 1) * P], ident[:])
-        nc.scalar.copy(ts_cols[:], bank[:, 0:3, P - 1])
+        ts_cols = kept([P, BLOCKS], F32, "ts_cols")
+        ts_minus = kept([P, 2], F32, "ts_minus", "heads1")
+        nc.scalar.copy(ts_cols[:], bank[:, :, P - 1])
         nc.scalar.activation(ts_minus[:], bank[:, 2:4, P - 1], ACT.Copy, scale=-1.0)
-        ts_rows = in_bank(1, [P, 3 * P], "ts_rows")
-        for b in range(3):
+        ts_rows = in_bank(1, [P, N], "ts_rows")
+        for b in range(BLOCKS):
             nc.tensor.transpose(ts_rows[:, b * P : (b + 1) * P], ts_cols[:, b : b + 1].to_broadcast([P, P]), ident[:])
-        ts_all = kept([P, 3 * P], F32, "ts_all")
-        ts_first = kept([P, 8 * N], F32, "ts_first")
-        nc.scalar.copy(ts_first[:, 0 : 3 * P], ts_rows[:])
-        nc.scalar.copy(ts_all[:], ts_rows[:])
-        us_rows = [in_bank(2 + g, [P, K], "us_rows%d" % g) for g in range(PASSES)]
+        ts_low = kept([P, HALF], F32, "ts_low")
+        ts_high = kept([P, HALF], F32, "ts_high")
+        nc.scalar.copy(ts_low[:], ts_rows[:, 0:HALF])
+        nc.scalar.activation(ts_high[:], ts_rows[:, HALF:], ACT.Copy, scale=-1.0)
+        scale_by_slot = []
         for g in range(PASSES):
+            us_rows = in_bank(2 + g, [P, PACK, P], "us_rows%d" % g)
             for t in range(PACK):
-                nc.tensor.transpose(us_rows[g][:, t * P : (t + 1) * P], row_scale[:, g, t : t + 1].to_broadcast([P, P]), ident[:])
-        scale_by_slot = {}
-
-        def spread_by_slot(g, tag):
-            scale_by_slot[g] = kept([P, 2, K], F32, "scale_by_slot%d" % g, tag)
+                nc.tensor.transpose(us_rows[:, t, :], row_scale[:, g, t : t + 1].to_broadcast([P, P]), ident[:])
+            tile = kept([P, 2, P, PACK], F32, "scale_by_slot%d" % g)
             for j in range(2):
-                nc.scalar.activation(scale_by_slot[g][:, j, :].rearrange("p (s t) -> p s t", t=PACK), us_rows[g][:].rearrange("p (t s) -> p s t", t=PACK), ACT.Copy, scale=ts_minus[:, j : j + 1])
-
-        spread_by_slot(0, None)
-        steps = [(g, k) for k in range(2) for g in range(PASSES)]
-        widths = (3 * P, HALF)
-        scale_of_pass = [kept([P, PACK, widths[g]], F32, "scale%d" % g) for g in range(PASSES)]
-        scale = [scale_of_pass[0][:, :, 0:HALF], scale_of_pass[1][:], scale_of_pass[0][:, :, HALF:]]
+                nc.scalar.activation(tile[:, j], us_rows[:].rearrange("p t s -> p s t"), ACT.Copy, scale=ts_minus[:, j : j + 1])
+            scale_by_slot.append(tile)
+        scale_by_row = [kept([P, PACK, HALF], F32, "scale_by_row%d" % g) for g in range(PASSES)]
         for g in range(PASSES):
             for t in range(PACK):
-                nc.gpsimd.tensor_scalar(scale_of_pass[g][:, t, :], (ts_all if g + t else ts_first)[:, 0 : widths[g]], row_scale[:, g, t : t + 1], 0.0, ALU.mult, ALU.add)
+                nc.gpsimd.tensor_scalar(scale_by_row[g][:, t, :], ts_low[:], row_scale[:, g, t : t + 1], 0.0, ALU.mult, ALU.add)
 
         heads = [kept([P, 2 * R], BF16, "heads%d" % n) for n in range(2)]
         plane = PASSES * P
-        turned_banks = {}
+        turned = [kept([P, 2 * plane * PACK], BF16, "turned%d" % n) for n in range(2)]
+        woven = kept([P, R * PACK], BF16, "woven")
+
+        def gather(engine, into, window):
+            if engine is nc.vector:
+                nc.vector.tensor_copy(into, window)
+            else:
+                nc.scalar.activation(into, window, ACT.Copy)
+
+        def gather_heads(engine, td, first, count):
+            at = (td % 2) * R + first
+            gather(engine, heads[td // 2][:, at : at + count], listed(u_raw[td], head_list, first, count))
 
         def turn_heads(td):
-            bank = in_bank(td % 2, [P, PASSES, 2, P], "heads_turned%d" % td)
+            bank = in_bank(4 + td, [P, PASSES, 2, P], "heads_turned%d" % td)
             for g in range(PASSES):
                 first = (td % 2) * R + g * K
                 words = heads[td // 2][:, first : first + K].bitcast(F32)
                 for u in range(2):
                     nc.tensor.transpose(bank[:, g, u, :], words[:, u : K // 2 : 2], ident[:])
-            turned_banks[td] = bank
-
-        turned = [kept([P, 2 * plane * PACK], BF16, name) for name in ("turned_early", "turned_late")]
-
-        def copy_turned(td):
             words = turned[td // 2][:].bitcast(F32).rearrange("m (d g p u) -> m d g p u", g=PASSES, d=2, u=2)
-            nc.scalar.copy(words[:, td % 2], turned_banks[td][:].rearrange("m g u p -> m g p u"))
-
-        woven_all = kept([P, R * PACK], BF16, "woven")
-        woven = [woven_all[:, g * K * PACK : (g + 1) * K * PACK] for g in range(PASSES)]
+            nc.scalar.copy(words[:, td % 2], bank[:].rearrange("m g u p -> m g p u"))
 
         def weave_heads(n):
             for g in range(PASSES):
-                nc.scalar.copy(
-                    woven[g].rearrange("p (t c e d) -> p c t e d", t=PACK, e=2, d=PACK)[:, :, :, :, 2 * n : 2 * n + 2],
+                nc.vector.tensor_copy(
+                    woven[:, g * K * PACK : (g + 1) * K * PACK].rearrange("p (t c e d) -> p c t e d", t=PACK, e=2, d=PACK)[:, :, :, :, 2 * n : 2 * n + 2],
                     heads[n][:].rearrange("p (d g c e t) -> p g c t e d", d=2, g=PASSES, e=2, t=PACK)[:, g],
                 )
 
+        gather_heads(nc.vector, 0, 0, R)
+        gather_heads(nc.vector, 1, 0, R)
+        weave_heads(0)
+        gather_heads(nc.scalar, 2, 0, R)
+        gather_heads(nc.vector, 3, 0, K)
+        gather_heads(nc.scalar, 3, K, K)
+        weave_heads(1)
         for td in range(PACK):
-            parts = PASSES if td % 2 else 1
-            for part in range(parts):
-                width = R // parts
-                first = (td % 2) * R + part * width
-                nc.vector.tensor_copy(heads[td // 2][:, first : first + width], u_raw[td][:].indirect(head_list[:, part * width // 16 : (part + 1) * width // 16]))
             turn_heads(td)
-            if td == 1:
-                weave_heads(0)
-                copy_turned(0)
-                copy_turned(1)
-            if td == 2:
-                copy_turned(2)
-            if td == 3:
-                weave_heads(1)
-                copy_turned(3)
-        x_scales_all = kept([P, R], U8, "x_scales")
-        x_codes_all = kept([P, R], U32, "x_codes")
-        x_scales = [x_scales_all[:, g * K : (g + 1) * K] for g in range(PASSES)]
-        x_codes = [x_codes_all[:, g * K : (g + 1) * K] for g in range(PASSES)]
+        x_codes = kept([P, R], U32, "x_codes")
+        x_scales = kept([P, R], U8, "x_scales")
+        nc.vector.quantize_mx(x_codes[:].bitcast(E4M3), x_scales[:], woven[:])
         xt_scales = kept([P, PACK * plane], U8, "xt_scales")
+        xt_codes = []
+        for n in range(2):
+            codes = kept([P, 2 * plane], U32, "xt_codes%d" % n, None if n else "heads1")
+            nc.vector.quantize_mx(codes[:].bitcast(E4M3), xt_scales[:, 2 * n * plane : 2 * (n + 1) * plane], turned[n][:])
+            xt_codes.extend(codes[:, e * plane : (e + 1) * plane] for e in range(2))
+        windows.append(kept([P, T], F32, "window3", "turned1"))
+        nc.gpsimd.memset(windows[3][:].bitcast(I32), 0)
 
-        def quantise_turned(planes, turned, name, tag):
-            codes = kept([P, len(planes) * plane], U32, name, tag)
-            width = len(planes) * plane
-            nc.vector.quantize_mx(codes[:].bitcast(E4M3), xt_scales[:, planes[0] * plane : planes[0] * plane + width], turned[:])
-            return [codes[:, n * plane : (n + 1) * plane] for n in range(len(planes))]
+        tails = [kept([P, HALF * PACK], BF16, "tails%d" % k) for k in range(2)]
+        pairs = [kept([P, 2 * N], BF16, "pair%d" % n, ("u_raw3", "woven")[n]) for n in range(2)]
 
-        tails = [kept([P, (14 if k else PACK) * HALF], BF16, "tails%d" % k)[:, 0 : HALF * PACK] for k in range(2)]
+        def gather_tails(engine, td, first, count):
+            at = (td % 2) * N + first
+            gather(engine, pairs[td // 2][:, at : at + count], listed(v_raw[td], tail_list, first, count))
 
-        def weave_tails(pairs, first, count, place):
+        def weave_tails(copy, n, first, count):
             k, at = divmod(first, HALF)
-            nc.scalar.copy(
-                tails[k].rearrange("p (i d) -> p i d", d=PACK)[:, at : at + count, place : place + 2],
-                pairs[:].rearrange("p (e i) -> p i e", e=2)[:, first : first + count],
+            copy(
+                tails[k][:].rearrange("p (i d) -> p i d", d=PACK)[:, at : at + count, 2 * n : 2 * n + 2],
+                pairs[n][:].rearrange("p (e i) -> p i e", e=2)[:, first : first + count],
             )
 
-        pair = kept([P, 2 * N], BF16, "pair")
-        nc.vector.tensor_copy(pair[:, 0:N], v_raw[0][:].indirect(tail_list[:]))
-        xt_codes = quantise_turned([0, 1], turned[0], "xt_early", "u_raw3")
-        nc.vector.tensor_copy(pair[:, N:], v_raw[1][:].indirect(tail_list[:]))
+        gather_tails(nc.scalar, 0, 0, N)
+        gather_tails(nc.scalar, 1, 0, N)
         for k in range(2):
-            weave_tails(pair, k * HALF, HALF, 0)
-        spread_by_slot(1, "pair")
-        nc.vector.quantize_mx(x_codes_all[:].bitcast(E4M3), x_scales_all[:], woven_all[:])
+            weave_tails(nc.scalar.copy, 0, k * HALF, HALF)
+        gather_tails(nc.vector, 2, 0, N)
+        for b in range(2):
+            gather_tails(nc.vector, 3, b * P, P)
+        gather_tails(nc.scalar, 3, HALF, HALF)
+        weave_tails(nc.scalar.copy, 1, HALF, HALF)
+        for b in range(2):
+            weave_tails(nc.vector.tensor_copy, 1, b * P, P)
         w_codes = kept([P, N], U32, "w_codes")
         w_scales = kept([P, N], U8, "w_scales")
-        late_pair = kept([P, 2 * N], BF16, "late_pair")
-        nc.vector.tensor_copy(late_pair[:, 0:N], v_raw[2][:].indirect(tail_list[:]))
-        parts = [(0, P), (P, P), (HALF, HALF)]
-        for first, count in parts:
-            nc.vector.tensor_copy(late_pair[:, N + first : N + first + count], v_raw[3][:].indirect(tail_list[:, first // 16 : (first + count) // 16]))
-            weave_tails(late_pair, first, count, 2)
-        for first, count in parts:
+        for first, count in ((0, P), (P, P), (HALF, HALF)):
             k, at = divmod(first, HALF)
             slots = slice(first, first + count)
             nc.vector.quantize_mx(w_codes[:, slots].bitcast(E4M3), w_scales[:, slots], tails[k][:, at * PACK : (at + count) * PACK])
-        xt_codes.extend(quantise_turned([2, 3], turned[1], "xt_late", "tails0"))
 
-        y_parts = y[0].rearrange("(g p t) i -> g p t i", g=PASSES, t=PACK)
-        labels = []
-        for n, (g, k) in enumerate(steps):
-            tile = kept([P, PACK, HALF], F32, "labels%d" % n)
-            nc.sync.dma_start(tile[:], y_parts[g][:, :, k * HALF : (k + 1) * HALF])
-            labels.append(tile)
+        z = [kept([P, PACK, HALF], F32, "z%d" % n) for n in range(len(steps))]
 
-        h_codes = [kept([P, N], U32, "h_codes%d" % g) for g in range(PASSES)]
-        h_scales = [kept([P, N], U8, "h_scales%d" % g) for g in range(PASSES)]
-        for g in range(PASSES):
-            nc.gpsimd.memset(h_codes[g][:, HALF:], 0)
-            nc.gpsimd.memset(h_scales[g][:, HALF:], 0)
-        h = {}
-        z = [kept([P, PACK, HALF], F32, "z%d" % n)[:] for n in range(len(steps))]
-
-        def direct_scores(n, j, number):
-            g, k = steps[n]
-            block = slice(k * HALF + j * P, k * HALF + (j + 1) * P)
-            acc = in_bank(number, [P, PACK, P], "direct%d_%d" % (n, j))
-            for t in range(PACK):
-                cols = slice(t * P, (t + 1) * P)
-                nc.tensor.matmul_mx(
-                    out=acc[:, t, :], lhsT=x_codes[g][:, cols].bitcast(E4M3), lhsT_scale=x_scales[g][:, cols],
-                    rhs=w_codes[:, block].bitcast(E4M3), rhs_scale=w_scales[:, block], start=True, stop=True,
-                )
-            tile = z[n][:, :, j * P : (j + 1) * P]
-            logits = tile
-            if n == PASSES:
-                logits = kept([P, BLOCKS * K], F32, "last_logits")[:, 0:K].rearrange("p (t i) -> p t i", t=PACK)
-            nc.vector.tensor_tensor(logits, acc[:], scale[n][:, :, j * P : (j + 1) * P], ALU.mult)
-            nc.scalar.activation(tile, logits, ACT.Sigmoid, scale=-1.0 if k else 1.0)
-
-        def turned_scores(n, j, number):
-            g, k = steps[n]
-            b = 2 * k + j
-            block = slice(b * P, (b + 1) * P)
-            acc = in_bank(number, [P, K], "score%d_%d" % (n, j))
+        def score(acc, g, rows, slots):
+            rows = slice(g * K + rows.start, g * K + rows.stop)
             nc.tensor.matmul_mx(
-                out=acc[:], lhsT=w_codes[:, block].bitcast(E4M3), lhsT_scale=w_scales[:, block],
-                rhs=x_codes[g].bitcast(E4M3), rhs_scale=x_scales[g], start=True, stop=True,
-            )
-            turned = kept([P, K], F32, "by_slot%d_%d" % (n, j))
-            nc.scalar.activation(turned[:], acc[:], ACT.Copy, scale=ts_minus[:, j : j + 1])
-            return turned
-
-        def turned_step(n, blocks, turns):
-            g, k = steps[n]
-            share = PACK // len(turns)
-            banks = [in_bank(number, [P, share, len(blocks) * P], "turn%d_%d" % (n, u)) for u, number in enumerate(turns)]
-            for at, j in enumerate(blocks):
-                for t in range(PACK):
-                    nc.tensor.transpose(banks[t // share][:, t % share, at * P : (at + 1) * P], by_slot[n, j][:, t * P : (t + 1) * P], ident[:])
-            for t in range(PACK):
-                nc.scalar.activation(z[n][:, t, blocks[0] * P :], banks[t // share][:, t % share, :], ACT.Sigmoid, scale=row_scale[:, g, t : t + 1])
-
-        def residual(n):
-            first = 0 if n else P
-            nc.vector.tensor_tensor(z[n][:, :, first:], z[n][:, :, first:], labels[n][:, :, first:], ALU.subtract)
-
-        def weigh(n):
-            h[n] = kept([P, HALF * PACK], BF16, "h%d" % n, None if n else "labels1")
-            nc.vector.tensor_tensor(
-                h[n][:].rearrange("p (c i t) -> p c t i", i=4, t=PACK),
-                z[n].rearrange("p t (c i) -> p c t i", i=4),
-                scale[n].rearrange("p t (c i) -> p c t i", i=4),
-                ALU.mult,
+                out=acc, lhsT=x_codes[:, rows].bitcast(E4M3), lhsT_scale=x_scales[:, rows],
+                rhs=w_codes[:, slots].bitcast(E4M3), rhs_scale=w_scales[:, slots], start=True, stop=True,
             )
 
         sums = {}
@@ -278,78 +207,114 @@ def tile_attend_gmf_nce_v_kernel(tc, uT, vT, y, us, ts, offs, uoffs, out):
             for t in range(PACK):
                 nc.tensor.matmul(sums[n, j][:, t, :], labels[n][:, t, j * P : (j + 1) * P], ident[:], start=(t == 0), stop=False, is_transpose=True)
 
-        def close_sums(n):
-            for t, j in [(t, j) for t in range(PACK) for j in range(2)] if n > PASSES else [(t, j) for j in range(2) for t in range(PACK)]:
-                if True:
-                    nc.tensor.matmul(sums[n, j][:, t, :], z[n][:, t, j * P : (j + 1) * P], ident[:], start=False, stop=(t == PACK - 1), is_transpose=True)
+        def close_sum(n, j):
+            for t in range(PACK):
+                nc.tensor.matmul(sums[n, j][:, t, :], z[n][:, t, j * P : (j + 1) * P], ident[:], start=False, stop=(t == PACK - 1), is_transpose=True)
 
-        h_by_slot = {}
+        for g in range(PASSES):
+            for j in range(2):
+                block = slice(j * P, (j + 1) * P)
+                acc = in_bank(2 * g + j, [P, PACK, P], "low%d_%d" % (g, j))
+                for t in range(PACK):
+                    score(acc[:, t, :], g, slice(t * P, (t + 1) * P), block)
+                tile = z[g][:, :, block]
+                nc.vector.tensor_tensor(tile, acc[:], scale_by_row[g][:, :, block], ALU.mult)
+                nc.scalar.activation(tile, tile, ACT.Sigmoid)
+                nc.gpsimd.tensor_tensor(tile, tile, labels[g][:, :, block], ALU.subtract)
+        for g in range(PASSES):
+            n = PASSES + g
+            for a in range(2):
+                acc = in_bank(4 + 2 * g + a, [P, 2, HALF], "high%d_%d" % (g, a))
+                for e in range(2):
+                    t = 2 * a + e
+                    score(acc[:, e, :], g, slice(t * P, (t + 1) * P), slice(HALF, N))
+                nc.vector.tensor_tensor(z[n][:, 2 * a : 2 * a + 2, :], acc[:], ts_high[:].unsqueeze(1).to_broadcast([P, 2, HALF]), ALU.mult)
+                for t in (2 * a, 2 * a + 1):
+                    nc.scalar.activation(z[n][:, t, :], z[n][:, t, :], ACT.Sigmoid, scale=row_scale[:, g, t : t + 1])
+            for j in range(2):
+                open_sum(n, j, 2 * g + j)
+            for j in range(2):
+                close_sum(n, j)
 
-        def weigh_by_slot(n, numbers):
+        h = {}
+
+        def weigh_by_slot(n, j):
+            by_slot = kept([P, P, PACK], BF16, "h_by_slot%d_%d" % (n, j))
+            nc.vector.scalar_tensor_tensor(by_slot[:], sums[n, j][:].rearrange("p t s -> p s t"), 1.0, scale_by_slot[n - PASSES][:, j], ALU.subtract, ALU.mult)
+            bank = in_bank(4 + 2 * (n - PASSES) + j, [P, 2, P], "h_turned%d_%d" % (n, j))
+            words = by_slot[:].rearrange("p s t -> p (s t)").bitcast(F32)
+            for u in range(2):
+                nc.tensor.transpose(bank[:, u, :], words[:, u : K // 2 : 2], ident[:])
+            nc.scalar.copy(h[n][:, j * K : (j + 1) * K].bitcast(F32).rearrange("p (i u) -> p i u", u=2), bank[:].rearrange("p u i -> p i u"))
+
+        def weigh_by_row(n):
             g, k = steps[n]
-            h_by_slot[n] = kept([P, 2, K], BF16, "h_by_slot%d" % n)
-            h[n] = kept([P, HALF * PACK], BF16, "h%d" % n)
-            for j, number in enumerate(numbers):
-                nc.vector.scalar_tensor_tensor(
-                    h_by_slot[n][:, j, :].rearrange("p (s t) -> p s t", t=PACK), sums[n, j][:].rearrange("p t s -> p s t"), 1.0,
-                    scale_by_slot[g][:, j, :].rearrange("p (s t) -> p s t", t=PACK), ALU.subtract, ALU.mult,
-                )
-                bank = in_bank(number, [P, 2, P], "h_turned%d_%d" % (n, j))
-                words = h_by_slot[n][:, j, :].bitcast(F32)
-                for u in range(2):
-                    nc.tensor.transpose(bank[:, u, :], words[:, u : K // 2 : 2], ident[:])
-                nc.scalar.copy(h[n][:, j * K : (j + 1) * K].bitcast(F32).rearrange("p (i u) -> p i u", u=2), bank[:].rearrange("p u i -> p i u"))
+            h[n] = kept([P, HALF * PACK], BF16, "h%d" % n, "h3" if n else None)
+            nc.vector.tensor_tensor(
+                h[n][:].rearrange("p (c i t) -> p c t i", i=4, t=PACK),
+                z[n][:].rearrange("p t (c i) -> p c t i", i=4),
+                scale_by_row[g][:].rearrange("p t (c i) -> p c t i", i=4),
+                ALU.mult,
+            )
+
+        h_codes = [kept([P, N], U32, "h_codes%d" % g) for g in range(PASSES)]
+        h_scales = [kept([P, N], U8, "h_scales%d" % g) for g in range(PASSES)]
 
         def quantise(n):
             g, k = steps[n]
             slots = slice(k * HALF, (k + 1) * HALF)
             nc.vector.quantize_mx(h_codes[g][:, slots].bitcast(E5M2), h_scales[g][:, slots], h[n][:])
 
-        def product(td, number, name, first):
-            acc = in_bank(number, [P, N], name)
-            order = (first, 1 - first)
-            for g in order:
-                nc.tensor.matmul_mx(
-                    out=acc[:], lhsT=xt_codes[td][:, g * P : (g + 1) * P].bitcast(E4M3),
-                    lhsT_scale=xt_scales[:, td * plane + g * P : td * plane + (g + 1) * P],
-                    rhs=h_codes[g][:].bitcast(E5M2), rhs_scale=h_scales[g][:], start=(g == order[0]), stop=(g == order[-1]),
-                )
-            return acc
-
-        def scatter(td, acc, first, count, name, tag=None):
-            grad = kept([P, count], F32, name, tag)
-            nc.scalar.copy(grad[:], acc[:, first : first + count])
-            nc.vector.tensor_copy(windows[td % WINDOWS][:].indirect(tail_list[:, first // 16 : (first + count) // 16]), grad[:])
-
-        for n in range(PASSES):
-            for j in range(2):
-                direct_scores(n, j, 2 + 2 * n + j)
-        nc.gpsimd.tensor_tensor(z[0][:, :, 0:P], z[0][:, :, 0:P], labels[0][:, :, 0:P], ALU.subtract)
-        direct_scores(2, 0, 2)
-        by_slot = {(n, j): turned_scores(n, j, 2 * n - 2 + j) for n, j in ((2, 1), (3, 0), (3, 1))}
-        for j in range(2):
-            open_sum(2, j, 6 + j)
-        for j in range(2):
-            open_sum(3, j, j)
-        turned_step(2, [1], [3])
-        turned_step(3, [0, 1], [4, 5])
-        close_sums(2)
-        close_sums(3)
-        for stage_of in (residual, weigh, quantise):
+        def product(acc, td, k):
+            slots = slice(k * HALF, (k + 1) * HALF)
             for g in range(PASSES):
-                stage_of(g)
-        second = product(1, 2, "early1", 0)
-        weigh_by_slot(2, (3, 5))
-        weigh_by_slot(3, (6, 7))
-        early = product(0, 0, "early0", 0)
-        scatter(1, second, 0, HALF, "grad_early1")
-        quantise(2)
-        quantise(3)
+                nc.tensor.matmul_mx(
+                    out=acc, lhsT=xt_codes[td][:, g * P : (g + 1) * P].bitcast(E4M3),
+                    lhsT_scale=xt_scales[:, td * plane + g * P : td * plane + (g + 1) * P],
+                    rhs=h_codes[g][:, slots].bitcast(E5M2), rhs_scale=h_scales[g][:, slots], start=(g == 0), stop=(g == PASSES - 1),
+                )
 
-        clear_window("h3")
-        scatter(0, early, 0, HALF, "grad_early", "h_by_slot3")
+        for n in (2, 3):
+            h[n] = kept([P, HALF * PACK], BF16, "h%d" % n)
+            for j in range(2):
+                weigh_by_slot(n, j)
+        quantise(2)
+        weigh_by_row(0)
+        quantise(3)
+        weigh_by_row(1)
+        quantise(0)
+        quantise(1)
+
         out_planes = out.rearrange("(p t) c -> t p c", t=PACK)
-        for td in range(PACK):
-            first = HALF if td < 2 else 0
-            scatter(td, product(td, (1, 4, 2, 3)[td], "final%d" % td, min(td, 1)), first, N - first, "grad%d" % td)
-            nc.sync.dma_start(out_planes[td], windows[td % WINDOWS][:])
+
+        def scatter_on_scalar(td, grad, first):
+            nc.scalar.activation(listed(windows[td], tail_list, first, HALF), grad, ACT.Copy)
+
+        halves = {}
+        for td, k, number in ((0, 1, 0), (1, 1, 1), (0, 0, 4), (1, 0, 5)):
+            halves[td, k] = in_bank(number, [P, HALF], "grad_half%d_%d" % (td, k))
+            product(halves[td, k][:], td, k)
+        wholes = {}
+        for td, number in ((2, 2), (3, 3)):
+            wholes[td] = in_bank(number, [P, N], "grad_whole%d" % td)
+            for k in (1, 0):
+                product(wholes[td][:, k * HALF : (k + 1) * HALF], td, k)
+        for k in (1, 0):
+            grad = kept([P, HALF], F32, "grad0_%d" % k)
+            nc.scalar.copy(grad[:], halves[0, k][:])
+            scatter_on_scalar(0, grad[:], k * HALF)
+        nc.sync.dma_start(out_planes[0], windows[0][:])
+        for k in (1, 0):
+            grad = kept([P, HALF], F32, "grad1_%d" % k, "h3" if k else None)
+            nc.vector.tensor_copy(grad[:], halves[1, k][:])
+            nc.vector.tensor_copy(listed(windows[1], tail_list, k * HALF, HALF), grad[:])
+        nc.sync.dma_start(out_planes[1], windows[1][:])
+        grad = kept([P, N], F32, "grad2")
+        nc.scalar.copy(grad[:], wholes[2][:])
+        for k in range(2):
+            scatter_on_scalar(2, grad[:, k * HALF : (k + 1) * HALF], k * HALF)
+        nc.sync.dma_start(out_planes[2], windows[2][:])
+        grad = kept([P, N], F32, "grad3")
+        nc.vector.tensor_copy(grad[:], wholes[3][:])
+        nc.vector.tensor_copy(listed(windows[3], tail_list, 0, N), grad[:])
+        nc.sync.dma_start(out_planes[3], windows[3][:])

@@ -82,7 +82,7 @@ def tile_attend_gmf_nce_v_kernel(tc, uT, vT, y, us, ts, offs, uoffs, out):
         for b in range(BLOCKS):
             nc.tensor.transpose(bank[:, b, :], ts_picked[:, b * P : (b + 1) * P], ident[:])
         ts_cols = kept([P, BLOCKS], F32, "ts_cols")
-        ts_minus = kept([P, 2], F32, "ts_minus", "heads1")
+        ts_minus = kept([P, 2], F32, "ts_minus")
         nc.scalar.copy(ts_cols[:], bank[:, :, P - 1])
         nc.scalar.activation(ts_minus[:], bank[:, 2:4, P - 1], ACT.Copy, scale=-1.0)
         ts_rows = in_bank(1, [P, N], "ts_rows")
@@ -106,84 +106,66 @@ def tile_attend_gmf_nce_v_kernel(tc, uT, vT, y, us, ts, offs, uoffs, out):
             for t in range(PACK):
                 nc.gpsimd.tensor_scalar(scale_by_row[g][:, t, :], ts_low[:], row_scale[:, g, t : t + 1], 0.0, ALU.mult, ALU.add)
 
-        heads = [kept([P, 2 * R], BF16, "heads%d" % n) for n in range(2)]
+        heads = kept([P, PACK * R], BF16, "heads")
         plane = PASSES * P
         turned = [kept([P, 2 * plane * PACK], BF16, "turned%d" % n) for n in range(2)]
         woven = kept([P, R * PACK], BF16, "woven")
 
-        def gather(engine, into, window):
-            if engine is nc.vector:
-                nc.vector.tensor_copy(into, window)
-            else:
+        def gather(on_scalar, into, window):
+            if on_scalar:
                 nc.scalar.activation(into, window, ACT.Copy)
+            else:
+                nc.vector.tensor_copy(into, window)
 
-        def gather_heads(engine, td, first, count):
-            at = (td % 2) * R + first
-            gather(engine, heads[td // 2][:, at : at + count], listed(u_raw[td], head_list, first, count))
-
-        def turn_heads(td):
+        for td in range(PACK):
+            gather(td == 0, heads[:, td * R : (td + 1) * R], listed(u_raw[td], head_list, 0, R))
             bank = in_bank(4 + td, [P, PASSES, 2, P], "heads_turned%d" % td)
             for g in range(PASSES):
-                first = (td % 2) * R + g * K
-                words = heads[td // 2][:, first : first + K].bitcast(F32)
+                first = td * R + g * K
+                words = heads[:, first : first + K].bitcast(F32)
                 for u in range(2):
                     nc.tensor.transpose(bank[:, g, u, :], words[:, u : K // 2 : 2], ident[:])
             words = turned[td // 2][:].bitcast(F32).rearrange("m (d g p u) -> m d g p u", g=PASSES, d=2, u=2)
             nc.scalar.copy(words[:, td % 2], bank[:].rearrange("m g u p -> m g p u"))
-
-        def weave_heads(n):
-            for g in range(PASSES):
-                nc.vector.tensor_copy(
-                    woven[:, g * K * PACK : (g + 1) * K * PACK].rearrange("p (t c e d) -> p c t e d", t=PACK, e=2, d=PACK)[:, :, :, :, 2 * n : 2 * n + 2],
-                    heads[n][:].rearrange("p (d g c e t) -> p g c t e d", d=2, g=PASSES, e=2, t=PACK)[:, g],
-                )
-
-        gather_heads(nc.vector, 0, 0, R)
-        gather_heads(nc.vector, 1, 0, R)
-        weave_heads(0)
-        gather_heads(nc.scalar, 2, 0, R)
-        gather_heads(nc.vector, 3, 0, K)
-        gather_heads(nc.scalar, 3, K, K)
-        weave_heads(1)
-        for td in range(PACK):
-            turn_heads(td)
+        for g in range(PASSES):
+            nc.vector.tensor_copy(
+                woven[:, g * K * PACK : (g + 1) * K * PACK].rearrange("p (t c e d) -> p c t e d", t=PACK, e=2, d=PACK),
+                heads[:].rearrange("p (d g c e t) -> p g c t e d", d=PACK, g=PASSES, e=2, t=PACK)[:, g],
+            )
         x_codes = kept([P, R], U32, "x_codes")
         x_scales = kept([P, R], U8, "x_scales")
         nc.vector.quantize_mx(x_codes[:].bitcast(E4M3), x_scales[:], woven[:])
         xt_scales = kept([P, PACK * plane], U8, "xt_scales")
         xt_codes = []
         for n in range(2):
-            codes = kept([P, 2 * plane], U32, "xt_codes%d" % n, None if n else "heads1")
+            codes = kept([P, 2 * plane], U32, "xt_codes%d" % n, None if n else "heads")
             nc.vector.quantize_mx(codes[:].bitcast(E4M3), xt_scales[:, 2 * n * plane : 2 * (n + 1) * plane], turned[n][:])
             xt_codes.extend(codes[:, e * plane : (e + 1) * plane] for e in range(2))
-        windows.append(kept([P, T], F32, "window3", "turned1"))
+        windows.append(kept([P, T], F32, "window3", "turned0"))
         nc.gpsimd.memset(windows[3][:].bitcast(I32), 0)
 
         tails = [kept([P, HALF * PACK], BF16, "tails%d" % k) for k in range(2)]
-        pairs = [kept([P, 2 * N], BF16, "pair%d" % n, ("u_raw3", "woven")[n]) for n in range(2)]
+        picked = kept([P, PACK * N], BF16, "picked", "u_raw2")
 
-        def gather_tails(engine, td, first, count):
-            at = (td % 2) * N + first
-            gather(engine, pairs[td // 2][:, at : at + count], listed(v_raw[td], tail_list, first, count))
+        def gather_tails(on_scalar, td, first, count):
+            at = td * N + first
+            gather(on_scalar, picked[:, at : at + count], listed(v_raw[td], tail_list, first, count))
 
-        def weave_tails(copy, n, first, count):
+        def weave_tails(copy, first, count):
             k, at = divmod(first, HALF)
             copy(
-                tails[k][:].rearrange("p (i d) -> p i d", d=PACK)[:, at : at + count, 2 * n : 2 * n + 2],
-                pairs[n][:].rearrange("p (e i) -> p i e", e=2)[:, first : first + count],
+                tails[k][:, at * PACK : (at + count) * PACK].rearrange("p (c i d) -> p c d i", i=4, d=PACK),
+                picked[:].rearrange("p (d c i) -> p c d i", d=PACK, i=4)[:, first // 4 : (first + count) // 4],
             )
 
-        gather_tails(nc.scalar, 0, 0, N)
-        gather_tails(nc.scalar, 1, 0, N)
-        for k in range(2):
-            weave_tails(nc.scalar.copy, 0, k * HALF, HALF)
-        gather_tails(nc.vector, 2, 0, N)
+        for td in range(PACK - 1):
+            gather_tails(True, td, 0, N)
         for b in range(2):
-            gather_tails(nc.vector, 3, b * P, P)
-        gather_tails(nc.scalar, 3, HALF, HALF)
-        weave_tails(nc.scalar.copy, 1, HALF, HALF)
+            gather_tails(False, 3, b * P, P)
+        gather_tails(True, 3, HALF, HALF)
+        weave_tails(nc.scalar.copy, HALF, HALF)
         for b in range(2):
-            weave_tails(nc.vector.tensor_copy, 1, b * P, P)
+            weave_tails(nc.vector.tensor_copy, b * P, P)
         w_codes = kept([P, N], U32, "w_codes")
         w_scales = kept([P, N], U8, "w_scales")
         for first, count in ((0, P), (P, P), (HALF, HALF)):
@@ -212,15 +194,16 @@ def tile_attend_gmf_nce_v_kernel(tc, uT, vT, y, us, ts, offs, uoffs, out):
                 nc.tensor.matmul(sums[n, j][:, t, :], z[n][:, t, j * P : (j + 1) * P], ident[:], start=False, stop=(t == PACK - 1), is_transpose=True)
 
         for g in range(PASSES):
-            for j in range(2):
-                block = slice(j * P, (j + 1) * P)
-                acc = in_bank(2 * g + j, [P, PACK, P], "low%d_%d" % (g, j))
-                for t in range(PACK):
-                    score(acc[:, t, :], g, slice(t * P, (t + 1) * P), block)
-                tile = z[g][:, :, block]
-                nc.vector.tensor_tensor(tile, acc[:], scale_by_row[g][:, :, block], ALU.mult)
+            for a in range(2):
+                acc = in_bank(2 * g + a, [P, 2, HALF], "low%d_%d" % (g, a))
+                rows = slice(2 * a, 2 * a + 2)
+                for e in range(2):
+                    t = 2 * a + e
+                    score(acc[:, e, :], g, slice(t * P, (t + 1) * P), slice(0, HALF))
+                tile = z[g][:, rows, :]
+                nc.vector.tensor_tensor(tile, acc[:], scale_by_row[g][:, rows, :], ALU.mult)
                 nc.scalar.activation(tile, tile, ACT.Sigmoid)
-                nc.gpsimd.tensor_tensor(tile, tile, labels[g][:, :, block], ALU.subtract)
+                nc.gpsimd.tensor_tensor(tile, tile, labels[g][:, rows, :], ALU.subtract)
         for g in range(PASSES):
             n = PASSES + g
             for a in range(2):

@@ -29,6 +29,7 @@ def tile_attend_gmf_nce_v_kernel(tc, uT, vT, y, us, ts, offs, uoffs, out):
     nc = tc.nc
     with ExitStack() as ctx:
         keep = ctx.enter_context(tc.tile_pool(name="keep", bufs=1))
+        shared = ctx.enter_context(tc.tile_pool(name="shared", bufs=1))
         psum = ctx.enter_context(tc.psum_pool(name="psum", bufs=1))
 
         def in_bank(number, shape, name):
@@ -36,6 +37,9 @@ def tile_attend_gmf_nce_v_kernel(tc, uT, vT, y, us, ts, offs, uoffs, out):
 
         def kept(shape, dtype, name, tag=None):
             return keep.tile(shape, dtype, name=name, tag=tag or name, align_bytes=64)
+
+        def placed(shape, dtype, name, offset):
+            return shared.tile(shape, dtype, name=name, tag=name, align_bytes=64, offset=offset)
 
         tail_list = kept([P, N // 16], U16, "tail_list")
         head_list = kept([P, R // 16], U16, "head_list")
@@ -50,9 +54,9 @@ def tile_attend_gmf_nce_v_kernel(tc, uT, vT, y, us, ts, offs, uoffs, out):
         make_identity(nc, ident[:])
         ts_window = kept([P, T], F32, "ts_window")
         nc.gpsimd.memset(ts_window[0 : P - 1, :].bitcast(I32), 0)
-        windows = [kept([P, T], F32, "window%d" % td) for td in range(PACK - 1)]
-        for window in windows:
-            nc.gpsimd.memset(window[:].bitcast(I32), 0)
+        windows = [kept([P, T], F32, "window%d" % td) for td in range(PACK)]
+        for td, window in enumerate(windows):
+            (nc.gpsimd if td < 3 else nc.vector).memset(window[:].bitcast(I32), 0)
 
         nc.scalar.dma_start(ts_window[P - 1 : P, :], ts[0:1, :])
         nc.sync.dma_start(tail_list[:], offs)
@@ -70,11 +74,10 @@ def tile_attend_gmf_nce_v_kernel(tc, uT, vT, y, us, ts, offs, uoffs, out):
         v_raw = [load_plane(vT, td, "v_raw%d" % td) for td in range(PACK)]
         steps = [(g, k) for k in range(2) for g in range(PASSES)]
         y_rows = y[0].rearrange("(g p t) i -> g p t i", g=PASSES, t=PACK)
-        labels = []
-        for n, (g, k) in enumerate(steps):
-            tile = kept([P, PACK, HALF], F32, "labels%d" % n)
-            nc.sync.dma_start(tile[:], y_rows[g][:, :, k * HALF : (k + 1) * HALF])
-            labels.append(tile)
+        labels = [kept([P, PACK, HALF], F32, "labels%d" % n) for n in range(len(steps))]
+        for g in range(PASSES):
+            for k in range(2):
+                nc.sync.dma_start(labels[steps.index((g, k))][:], y_rows[g][:, :, k * HALF : (k + 1) * HALF])
 
         ts_picked = kept([P, N], F32, "ts_picked")
         nc.vector.tensor_copy(ts_picked[:], listed(ts_window, tail_list, 0, N))
@@ -88,10 +91,9 @@ def tile_attend_gmf_nce_v_kernel(tc, uT, vT, y, us, ts, offs, uoffs, out):
         ts_rows = in_bank(1, [P, N], "ts_rows")
         for b in range(BLOCKS):
             nc.tensor.transpose(ts_rows[:, b * P : (b + 1) * P], ts_cols[:, b : b + 1].to_broadcast([P, P]), ident[:])
-        ts_low = kept([P, HALF], F32, "ts_low")
-        ts_high = kept([P, HALF], F32, "ts_high")
-        nc.scalar.copy(ts_low[:], ts_rows[:, 0:HALF])
-        nc.scalar.activation(ts_high[:], ts_rows[:, HALF:], ACT.Copy, scale=-1.0)
+        ts_signed = kept([P, N], F32, "ts_signed")
+        nc.scalar.copy(ts_signed[:, 0:HALF], ts_rows[:, 0:HALF])
+        nc.scalar.activation(ts_signed[:, HALF:], ts_rows[:, HALF:], ACT.Copy, scale=-1.0)
         scale_by_slot = []
         for g in range(PASSES):
             us_rows = in_bank(2 + g, [P, PACK, P], "us_rows%d" % g)
@@ -101,14 +103,14 @@ def tile_attend_gmf_nce_v_kernel(tc, uT, vT, y, us, ts, offs, uoffs, out):
             for j in range(2):
                 nc.scalar.activation(tile[:, j], us_rows[:].rearrange("p t s -> p s t"), ACT.Copy, scale=ts_minus[:, j : j + 1])
             scale_by_slot.append(tile)
-        scale_by_row = [kept([P, PACK, HALF], F32, "scale_by_row%d" % g) for g in range(PASSES)]
+        scale_by_row = [kept([P, PACK, N], F32, "scale_by_row%d" % g) for g in range(PASSES)]
         for g in range(PASSES):
             for t in range(PACK):
-                nc.gpsimd.tensor_scalar(scale_by_row[g][:, t, :], ts_low[:], row_scale[:, g, t : t + 1], 0.0, ALU.mult, ALU.add)
+                nc.gpsimd.tensor_scalar(scale_by_row[g][:, t, :], ts_signed[:], row_scale[:, g, t : t + 1], 0.0, ALU.mult, ALU.add)
 
-        heads = kept([P, PACK * R], BF16, "heads")
+        heads = placed([P, PACK * R], BF16, "heads", 20480)
         plane = PASSES * P
-        turned = [kept([P, 2 * plane * PACK], BF16, "turned%d" % n) for n in range(2)]
+        turned = [kept([P, 2 * plane * PACK], BF16, "turned0"), placed([P, 2 * plane * PACK], BF16, "turned1", 16384)]
         woven = kept([P, R * PACK], BF16, "woven")
 
         def gather(on_scalar, into, window):
@@ -138,40 +140,33 @@ def tile_attend_gmf_nce_v_kernel(tc, uT, vT, y, us, ts, offs, uoffs, out):
         xt_scales = kept([P, PACK * plane], U8, "xt_scales")
         xt_codes = []
         for n in range(2):
-            codes = kept([P, 2 * plane], U32, "xt_codes%d" % n, None if n else "heads")
+            codes = placed([P, 2 * plane], U32, "xt_codes%d" % n, 20480 + 2048 * n)
             nc.vector.quantize_mx(codes[:].bitcast(E4M3), xt_scales[:, 2 * n * plane : 2 * (n + 1) * plane], turned[n][:])
             xt_codes.extend(codes[:, e * plane : (e + 1) * plane] for e in range(2))
-        windows.append(kept([P, T], F32, "window3", "turned0"))
-        nc.gpsimd.memset(windows[3][:].bitcast(I32), 0)
 
-        tails = [kept([P, HALF * PACK], BF16, "tails%d" % k) for k in range(2)]
-        picked = kept([P, PACK * N], BF16, "picked", "u_raw2")
+        tails = [placed([P, HALF, PACK], BF16, "tails0", 16384), kept([P, HALF, PACK], BF16, "tails1")]
 
-        def gather_tails(on_scalar, td, first, count):
-            at = td * N + first
-            gather(on_scalar, picked[:, at : at + count], listed(v_raw[td], tail_list, first, count))
-
-        def weave_tails(copy, first, count):
-            k, at = divmod(first, HALF)
-            copy(
-                tails[k][:, at * PACK : (at + count) * PACK].rearrange("p (c i d) -> p c d i", i=4, d=PACK),
-                picked[:].rearrange("p (d c i) -> p c d i", d=PACK, i=4)[:, first // 4 : (first + count) // 4],
+        def weave_pair(k, n, pair):
+            nc.scalar.copy(
+                tails[k][:, :, 2 * n : 2 * n + 2].rearrange("p (c i) d -> p c d i", i=4),
+                pair.rearrange("p d (c i) -> p c d i", i=4),
             )
 
-        for td in range(PACK - 1):
-            gather_tails(True, td, 0, N)
-        for b in range(2):
-            gather_tails(False, 3, b * P, P)
-        gather_tails(True, 3, HALF, HALF)
-        weave_tails(nc.scalar.copy, HALF, HALF)
-        for b in range(2):
-            weave_tails(nc.vector.tensor_copy, b * P, P)
+        early_pair = kept([P, 2, N], BF16, "early_pair", "u_raw2")
+        for td in range(2):
+            gather(True, early_pair[:, td, :], listed(v_raw[td], tail_list, 0, N))
+        for k in (1, 0):
+            weave_pair(k, 0, early_pair[:, :, k * HALF : (k + 1) * HALF])
+        late_pair = kept([P, 2, HALF], BF16, "late_pair", "u_raw2")
+        for td in (2, 3):
+            nc.vector.tensor_copy(tails[0][:, :, td], listed(v_raw[td], tail_list, 0, HALF))
+            gather(True, late_pair[:, td - 2, :], listed(v_raw[td], tail_list, HALF, HALF))
+        weave_pair(1, 1, late_pair[:])
         w_codes = kept([P, N], U32, "w_codes")
         w_scales = kept([P, N], U8, "w_scales")
-        for first, count in ((0, P), (P, P), (HALF, HALF)):
-            k, at = divmod(first, HALF)
-            slots = slice(first, first + count)
-            nc.vector.quantize_mx(w_codes[:, slots].bitcast(E4M3), w_scales[:, slots], tails[k][:, at * PACK : (at + count) * PACK])
+        for k in range(2):
+            slots = slice(k * HALF, (k + 1) * HALF)
+            nc.vector.quantize_mx(w_codes[:, slots].bitcast(E4M3), w_scales[:, slots], tails[k][:].rearrange("p i d -> p (i d)"))
 
         z = [kept([P, PACK, HALF], F32, "z%d" % n) for n in range(len(steps))]
 
@@ -189,54 +184,50 @@ def tile_attend_gmf_nce_v_kernel(tc, uT, vT, y, us, ts, offs, uoffs, out):
             for t in range(PACK):
                 nc.tensor.matmul(sums[n, j][:, t, :], labels[n][:, t, j * P : (j + 1) * P], ident[:], start=(t == 0), stop=False, is_transpose=True)
 
-        def close_sum(n, j):
-            for t in range(PACK):
-                nc.tensor.matmul(sums[n, j][:, t, :], z[n][:, t, j * P : (j + 1) * P], ident[:], start=False, stop=(t == PACK - 1), is_transpose=True)
+        def close_sums(n, places):
+            for t in places:
+                for j in range(2):
+                    nc.tensor.matmul(sums[n, j][:, t, :], z[n][:, t, j * P : (j + 1) * P], ident[:], start=False, stop=(t == PACK - 1), is_transpose=True)
 
+        score_banks = ((4, 0), (2, 6))
         for g in range(PASSES):
-            for a in range(2):
-                acc = in_bank(2 * g + a, [P, 2, HALF], "low%d_%d" % (g, a))
-                rows = slice(2 * a, 2 * a + 2)
-                for e in range(2):
-                    t = 2 * a + e
-                    score(acc[:, e, :], g, slice(t * P, (t + 1) * P), slice(0, HALF))
-                tile = z[g][:, rows, :]
-                nc.vector.tensor_tensor(tile, acc[:], scale_by_row[g][:, rows, :], ALU.mult)
-                nc.scalar.activation(tile, tile, ACT.Sigmoid)
-                nc.gpsimd.tensor_tensor(tile, tile, labels[g][:, rows, :], ALU.subtract)
-        for g in range(PASSES):
-            n = PASSES + g
-            for a in range(2):
-                acc = in_bank(4 + 2 * g + a, [P, 2, HALF], "high%d_%d" % (g, a))
-                for e in range(2):
-                    t = 2 * a + e
-                    score(acc[:, e, :], g, slice(t * P, (t + 1) * P), slice(HALF, N))
-                nc.vector.tensor_tensor(z[n][:, 2 * a : 2 * a + 2, :], acc[:], ts_high[:].unsqueeze(1).to_broadcast([P, 2, HALF]), ALU.mult)
-                for t in (2 * a, 2 * a + 1):
-                    nc.scalar.activation(z[n][:, t, :], z[n][:, t, :], ACT.Sigmoid, scale=row_scale[:, g, t : t + 1])
-            for j in range(2):
-                open_sum(n, j, 2 * g + j)
-            for j in range(2):
-                close_sum(n, j)
+            for k in range(2):
+                n = steps.index((g, k))
+                for a in range(2):
+                    acc = in_bank(score_banks[g][k] + a, [P, 2, HALF], "score%d_%d" % (n, a))
+                    rows = slice(2 * a, 2 * a + 2)
+                    for e in range(2):
+                        t = 2 * a + e
+                        score(acc[:, e, :], g, slice(t * P, (t + 1) * P), slice(k * HALF, (k + 1) * HALF))
+                    if k and not a:
+                        for j in range(2):
+                            open_sum(n, j, score_banks[0][g] + j)
+                    tile = z[n][:, rows, :]
+                    if k:
+                        nc.vector.tensor_tensor(tile, acc[:], scale_by_row[g][:, rows, HALF:], ALU.mult)
+                        nc.scalar.activation(tile, tile, ACT.Sigmoid)
+                        close_sums(n, (2 * a, 2 * a + 1))
+                    else:
+                        nc.vector.tensor_tensor(tile, acc[:], scale_by_row[g][:, rows, 0:HALF], ALU.mult)
+                        nc.scalar.activation(tile, tile, ACT.Sigmoid)
+                        nc.gpsimd.tensor_tensor(tile, tile, labels[n][:, rows, :], ALU.subtract)
 
         h = {}
 
         def weigh_by_slot(n, j):
-            by_slot = kept([P, P, PACK], BF16, "h_by_slot%d_%d" % (n, j))
+            by_slot = placed([P, P, PACK], BF16, "h_by_slot%d_%d" % (n, j), 1024 * (2 * (n - PASSES) + j))
             nc.vector.scalar_tensor_tensor(by_slot[:], sums[n, j][:].rearrange("p t s -> p s t"), 1.0, scale_by_slot[n - PASSES][:, j], ALU.subtract, ALU.mult)
-            bank = in_bank(4 + 2 * (n - PASSES) + j, [P, 2, P], "h_turned%d_%d" % (n, j))
+            bank = in_bank(score_banks[1][n - PASSES] + j, [P, 2, P], "h_turned%d_%d" % (n, j))
             words = by_slot[:].rearrange("p s t -> p (s t)").bitcast(F32)
             for u in range(2):
                 nc.tensor.transpose(bank[:, u, :], words[:, u : K // 2 : 2], ident[:])
             nc.scalar.copy(h[n][:, j * K : (j + 1) * K].bitcast(F32).rearrange("p (i u) -> p i u", u=2), bank[:].rearrange("p u i -> p i u"))
 
-        def weigh_by_row(n):
-            g, k = steps[n]
-            h[n] = kept([P, HALF * PACK], BF16, "h%d" % n, "h3" if n else None)
+        def weigh_by_row(n, first, count):
             nc.vector.tensor_tensor(
-                h[n][:].rearrange("p (c i t) -> p c t i", i=4, t=PACK),
-                z[n][:].rearrange("p t (c i) -> p c t i", i=4),
-                scale_by_row[g][:].rearrange("p t (c i) -> p c t i", i=4),
+                h[n][:, first * PACK : (first + count) * PACK].rearrange("p (c i t) -> p c t i", i=4, t=PACK),
+                z[n][:, :, first : first + count].rearrange("p t (c i) -> p c t i", i=4),
+                scale_by_row[n][:, :, first : first + count].rearrange("p t (c i) -> p c t i", i=4),
                 ALU.mult,
             )
 
@@ -261,10 +252,13 @@ def tile_attend_gmf_nce_v_kernel(tc, uT, vT, y, us, ts, offs, uoffs, out):
             h[n] = kept([P, HALF * PACK], BF16, "h%d" % n)
             for j in range(2):
                 weigh_by_slot(n, j)
+        h[0] = kept([P, HALF * PACK], BF16, "h0", "scale_by_slot1")
         quantise(2)
-        weigh_by_row(0)
+        weigh_by_row(0, 0, P)
         quantise(3)
-        weigh_by_row(1)
+        weigh_by_row(0, P, P)
+        h[1] = kept([P, HALF * PACK], BF16, "h1", "h3")
+        weigh_by_row(1, 0, HALF)
         quantise(0)
         quantise(1)
 
@@ -274,11 +268,11 @@ def tile_attend_gmf_nce_v_kernel(tc, uT, vT, y, us, ts, offs, uoffs, out):
             nc.scalar.activation(listed(windows[td], tail_list, first, HALF), grad, ACT.Copy)
 
         halves = {}
-        for td, k, number in ((0, 1, 0), (1, 1, 1), (0, 0, 4), (1, 0, 5)):
+        for td, k, number in ((0, 1, 4), (1, 1, 5), (0, 0, 2), (1, 0, 3)):
             halves[td, k] = in_bank(number, [P, HALF], "grad_half%d_%d" % (td, k))
             product(halves[td, k][:], td, k)
         wholes = {}
-        for td, number in ((2, 2), (3, 3)):
+        for td, number in ((2, 0), (3, 1)):
             wholes[td] = in_bank(number, [P, N], "grad_whole%d" % td)
             for k in (1, 0):
                 product(wholes[td][:, k * HALF : (k + 1) * HALF], td, k)

@@ -91,7 +91,7 @@ def tile_attend_gmf_nce_v_kernel(tc, uT, vT, y, us, ts, offs, uoffs, out):
         ts_rows = in_bank(1, [P, N], "ts_rows")
         for b in range(BLOCKS):
             nc.tensor.transpose(ts_rows[:, b * P : (b + 1) * P], ts_cols[:, b : b + 1].to_broadcast([P, P]), ident[:])
-        ts_signed = kept([P, N], F32, "ts_signed")
+        ts_signed = placed([P, N], F32, "ts_signed", 0)
         nc.scalar.copy(ts_signed[:, 0:HALF], ts_rows[:, 0:HALF])
         nc.scalar.activation(ts_signed[:, HALF:], ts_rows[:, HALF:], ACT.Copy, scale=-1.0)
         scale_by_slot = []
@@ -99,9 +99,9 @@ def tile_attend_gmf_nce_v_kernel(tc, uT, vT, y, us, ts, offs, uoffs, out):
             us_rows = in_bank(2 + g, [P, PACK, P], "us_rows%d" % g)
             for t in range(PACK):
                 nc.tensor.transpose(us_rows[:, t, :], row_scale[:, g, t : t + 1].to_broadcast([P, P]), ident[:])
-            tile = kept([P, 2, P, PACK], F32, "scale_by_slot%d" % g)
+            tile = kept([P, 2, 2, P, 2], F32, "scale_by_slot%d" % g)
             for j in range(2):
-                nc.scalar.activation(tile[:, j], us_rows[:].rearrange("p t s -> p s t"), ACT.Copy, scale=ts_minus[:, j : j + 1])
+                nc.scalar.activation(tile[:, j], us_rows[:].rearrange("p (u e) s -> p u s e", e=2), ACT.Copy, scale=ts_minus[:, j : j + 1])
             scale_by_slot.append(tile)
         scale_by_row = [kept([P, PACK, N], F32, "scale_by_row%d" % g) for g in range(PASSES)]
         for g in range(PASSES):
@@ -162,19 +162,18 @@ def tile_attend_gmf_nce_v_kernel(tc, uT, vT, y, us, ts, offs, uoffs, out):
             nc.vector.tensor_copy(tails[0][:, :, td], listed(v_raw[td], tail_list, 0, HALF))
             gather(True, late_pair[:, td - 2, :], listed(v_raw[td], tail_list, HALF, HALF))
         weave_pair(1, 1, late_pair[:])
-        w_codes = kept([P, N], U32, "w_codes")
-        w_scales = kept([P, N], U8, "w_scales")
+        w_codes = [kept([P, HALF], U32, "w_codes0"), placed([P, HALF], U32, "w_codes1", 0)]
+        w_scales = [kept([P, HALF], U8, "w_scales%d" % k) for k in range(2)]
         for k in range(2):
-            slots = slice(k * HALF, (k + 1) * HALF)
-            nc.vector.quantize_mx(w_codes[:, slots].bitcast(E4M3), w_scales[:, slots], tails[k][:].rearrange("p i d -> p (i d)"))
+            nc.vector.quantize_mx(w_codes[k][:].bitcast(E4M3), w_scales[k][:], tails[k][:].rearrange("p i d -> p (i d)"))
 
         z = [kept([P, PACK, HALF], F32, "z%d" % n) for n in range(len(steps))]
 
-        def score(acc, g, rows, slots):
-            rows = slice(g * K + rows.start, g * K + rows.stop)
+        def score(acc, g, t, k):
+            rows = slice(g * K + t * P, g * K + (t + 1) * P)
             nc.tensor.matmul_mx(
                 out=acc, lhsT=x_codes[:, rows].bitcast(E4M3), lhsT_scale=x_scales[:, rows],
-                rhs=w_codes[:, slots].bitcast(E4M3), rhs_scale=w_scales[:, slots], start=True, stop=True,
+                rhs=w_codes[k][:].bitcast(E4M3), rhs_scale=w_scales[k][:], start=True, stop=True,
             )
 
         sums = {}
@@ -189,38 +188,46 @@ def tile_attend_gmf_nce_v_kernel(tc, uT, vT, y, us, ts, offs, uoffs, out):
                 for j in range(2):
                     nc.tensor.matmul(sums[n, j][:, t, :], z[n][:, t, j * P : (j + 1) * P], ident[:], start=False, stop=(t == PACK - 1), is_transpose=True)
 
-        score_banks = ((4, 0), (2, 6))
-        for g in range(PASSES):
-            for k in range(2):
-                n = steps.index((g, k))
-                for a in range(2):
-                    acc = in_bank(score_banks[g][k] + a, [P, 2, HALF], "score%d_%d" % (n, a))
-                    rows = slice(2 * a, 2 * a + 2)
-                    for e in range(2):
-                        t = 2 * a + e
-                        score(acc[:, e, :], g, slice(t * P, (t + 1) * P), slice(k * HALF, (k + 1) * HALF))
-                    if k and not a:
-                        for j in range(2):
-                            open_sum(n, j, score_banks[0][g] + j)
-                    tile = z[n][:, rows, :]
-                    if k:
-                        nc.vector.tensor_tensor(tile, acc[:], scale_by_row[g][:, rows, HALF:], ALU.mult)
-                        nc.scalar.activation(tile, tile, ACT.Sigmoid)
-                        close_sums(n, (2 * a, 2 * a + 1))
-                    else:
-                        nc.vector.tensor_tensor(tile, acc[:], scale_by_row[g][:, rows, 0:HALF], ALU.mult)
-                        nc.scalar.activation(tile, tile, ACT.Sigmoid)
-                        nc.gpsimd.tensor_tensor(tile, tile, labels[n][:, rows, :], ALU.subtract)
+        sum_banks = ((5, 0), (1, 2))
+        back_banks = ((3, 6), (7, 4))
+
+        def score_pair(g, k, a, number):
+            n = steps.index((g, k))
+            acc = in_bank(number, [P, 2, HALF], "score%d_%d" % (n, a))
+            rows = slice(2 * a, 2 * a + 2)
+            for e in range(2):
+                score(acc[:, e, :], g, 2 * a + e, k)
+            if k and not a:
+                for j in range(2):
+                    open_sum(n, j, sum_banks[g][j])
+            tile = z[n][:, rows, :]
+            nc.vector.tensor_tensor(tile, acc[:], scale_by_row[g][:, rows, k * HALF : (k + 1) * HALF], ALU.mult)
+            nc.scalar.activation(tile, tile, ACT.Sigmoid)
+            if k:
+                close_sums(n, (2 * a, 2 * a + 1))
+            else:
+                nc.gpsimd.tensor_tensor(tile, tile, labels[n][:, rows, :], ALU.subtract)
+
+        for t in range(2):
+            acc = in_bank(4 + t, [P, HALF], "first%d" % t)
+            score(acc[:], 0, t, 0)
+            nc.vector.tensor_tensor(z[0][:, t, :], acc[:], ts_signed[:, 0:HALF], ALU.mult)
+            nc.scalar.activation(z[0][:, t, :], z[0][:, t, :], ACT.Sigmoid, scale=row_scale[:, 0, t : t + 1])
+        nc.gpsimd.tensor_tensor(z[0][:, 0:2, :], z[0][:, 0:2, :], labels[0][:, 0:2, :], ALU.subtract)
+        for g, k, a, number in ((0, 0, 1, 0), (1, 0, 0, 1), (1, 0, 1, 2), (0, 1, 0, 3), (0, 1, 1, 6), (1, 1, 0, 7), (1, 1, 1, 4)):
+            score_pair(g, k, a, number)
 
         h = {}
 
         def weigh_by_slot(n, j):
-            by_slot = placed([P, P, PACK], BF16, "h_by_slot%d_%d" % (n, j), 1024 * (2 * (n - PASSES) + j))
-            nc.vector.scalar_tensor_tensor(by_slot[:], sums[n, j][:].rearrange("p t s -> p s t"), 1.0, scale_by_slot[n - PASSES][:, j], ALU.subtract, ALU.mult)
-            bank = in_bank(score_banks[1][n - PASSES] + j, [P, 2, P], "h_turned%d_%d" % (n, j))
-            words = by_slot[:].rearrange("p s t -> p (s t)").bitcast(F32)
+            bank = in_bank(back_banks[n - PASSES][j], [P, 2, P], "h_turned%d_%d" % (n, j))
             for u in range(2):
-                nc.tensor.transpose(bank[:, u, :], words[:, u : K // 2 : 2], ident[:])
+                by_slot = kept([P, P, 2], BF16, "h_by_slot%d_%d_%d" % (n, j, u))
+                nc.vector.scalar_tensor_tensor(
+                    by_slot[:], sums[n, j][:, 2 * u : 2 * u + 2, :].rearrange("p e s -> p s e"), 1.0,
+                    scale_by_slot[n - PASSES][:, j, u], ALU.subtract, ALU.mult,
+                )
+                nc.tensor.transpose(bank[:, u, :], by_slot[:].rearrange("p s e -> p (s e)").bitcast(F32), ident[:])
             nc.scalar.copy(h[n][:, j * K : (j + 1) * K].bitcast(F32).rearrange("p (i u) -> p i u", u=2), bank[:].rearrange("p u i -> p i u"))
 
         def weigh_by_row(n, first, count):
@@ -264,34 +271,36 @@ def tile_attend_gmf_nce_v_kernel(tc, uT, vT, y, us, ts, offs, uoffs, out):
 
         out_planes = out.rearrange("(p t) c -> t p c", t=PACK)
 
-        def scatter_on_scalar(td, grad, first):
-            nc.scalar.activation(listed(windows[td], tail_list, first, HALF), grad, ACT.Copy)
+        def scatter(on_scalar, td, grad, first, count):
+            window = listed(windows[td], tail_list, first, count)
+            if on_scalar:
+                nc.scalar.activation(window, grad, ACT.Copy)
+            else:
+                nc.vector.tensor_copy(window, grad)
+
+        def copied(on_scalar, acc, name, tag=None):
+            grad = kept(list(acc.shape), F32, name, tag)
+            (nc.scalar.copy if on_scalar else nc.vector.tensor_copy)(grad[:], acc)
+            return grad[:]
 
         halves = {}
-        for td, k, number in ((0, 1, 4), (1, 1, 5), (0, 0, 2), (1, 0, 3)):
-            halves[td, k] = in_bank(number, [P, HALF], "grad_half%d_%d" % (td, k))
-            product(halves[td, k][:], td, k)
-        wholes = {}
-        for td, number in ((2, 0), (3, 1)):
-            wholes[td] = in_bank(number, [P, N], "grad_whole%d" % td)
+        for td, k, number in ((0, 1, 5), (1, 1, 0), (0, 0, 3), (1, 0, 6)):
+            halves[td, k] = in_bank(number, [P, HALF], "grad_half%d_%d" % (td, k))[:]
+            product(halves[td, k], td, k)
+        wholes = {td: in_bank(td - 1, [P, N], "grad_whole%d" % td)[:] for td in (2, 3)}
+        for td in (2, 3):
             for k in (1, 0):
                 product(wholes[td][:, k * HALF : (k + 1) * HALF], td, k)
-        for k in (1, 0):
-            grad = kept([P, HALF], F32, "grad0_%d" % k)
-            nc.scalar.copy(grad[:], halves[0, k][:])
-            scatter_on_scalar(0, grad[:], k * HALF)
+        scatter(True, 0, copied(True, halves[0, 1], "grad0_1"), HALF, HALF)
+        scatter(True, 1, copied(False, halves[1, 1], "grad1_1", "h3"), HALF, HALF)
+        scatter(False, 0, copied(False, halves[0, 0], "grad0_0"), 0, HALF)
         nc.sync.dma_start(out_planes[0], windows[0][:])
-        for k in (1, 0):
-            grad = kept([P, HALF], F32, "grad1_%d" % k, "h3" if k else None)
-            nc.vector.tensor_copy(grad[:], halves[1, k][:])
-            nc.vector.tensor_copy(listed(windows[1], tail_list, k * HALF, HALF), grad[:])
+        late = copied(True, halves[1, 0], "grad1_0")
+        last = copied(True, wholes[3], "grad3")
+        scatter(True, 1, late, 0, HALF)
         nc.sync.dma_start(out_planes[1], windows[1][:])
-        grad = kept([P, N], F32, "grad2")
-        nc.scalar.copy(grad[:], wholes[2][:])
-        for k in range(2):
-            scatter_on_scalar(2, grad[:, k * HALF : (k + 1) * HALF], k * HALF)
+        scatter(False, 2, copied(False, wholes[2], "grad2", "grad0_0"), 0, N)
         nc.sync.dma_start(out_planes[2], windows[2][:])
-        grad = kept([P, N], F32, "grad3")
-        nc.vector.tensor_copy(grad[:], wholes[3][:])
-        nc.vector.tensor_copy(listed(windows[3], tail_list, 0, N), grad[:])
+        scatter(True, 3, last[:, HALF:], HALF, HALF)
+        scatter(False, 3, last[:, 0:HALF], 0, HALF)
         nc.sync.dma_start(out_planes[3], windows[3][:])

@@ -284,23 +284,16 @@ def tile_attend_gmf_nce_v_kernel(tc, uT, vT, y, us, ts, offs, uoffs, out):
             return grad[:]
 
         halves = {}
-        for td, k, number in ((0, 1, 5), (1, 1, 0), (0, 0, 3), (1, 0, 6)):
-            halves[td, k] = in_bank(number, [P, HALF], "grad_half%d_%d" % (td, k))[:]
-            product(halves[td, k], td, k)
-        wholes = {td: in_bank(td - 1, [P, N], "grad_whole%d" % td)[:] for td in (2, 3)}
-        for td in (2, 3):
-            for k in (1, 0):
-                product(wholes[td][:, k * HALF : (k + 1) * HALF], td, k)
-        scatter(True, 0, copied(True, halves[0, 1], "grad0_1"), HALF, HALF)
-        scatter(True, 1, copied(False, halves[1, 1], "grad1_1", "h3"), HALF, HALF)
-        scatter(False, 0, copied(False, halves[0, 0], "grad0_0"), 0, HALF)
-        nc.sync.dma_start(out_planes[0], windows[0][:])
-        late = copied(True, halves[1, 0], "grad1_0")
-        last = copied(True, wholes[3], "grad3")
-        scatter(True, 1, late, 0, HALF)
-        nc.sync.dma_start(out_planes[1], windows[1][:])
-        scatter(False, 2, copied(False, wholes[2], "grad2", "grad0_0"), 0, N)
-        nc.sync.dma_start(out_planes[2], windows[2][:])
-        scatter(True, 3, last[:, HALF:], HALF, HALF)
-        scatter(False, 3, last[:, 0:HALF], 0, HALF)
-        nc.sync.dma_start(out_planes[3], windows[3][:])
+        for k, numbers in ((1, (5, 0, 1, 2)), (0, (3, 6, 7, 4))):
+            for td, number in enumerate(numbers):
+                halves[td, k] = in_bank(number, [P, HALF], "grad_half%d_%d" % (td, k))[:]
+                product(halves[td, k], td, k)
+        ahead = copied(True, halves[0, 1], "grad0_1")
+        for td in range(PACK):
+            grad = ahead
+            if td + 1 < PACK:
+                ahead = copied(True, halves[td + 1, 1], "grad%d_1" % (td + 1))
+            scatter(True, td, grad, HALF, HALF)
+        for td in range(PACK):
+            scatter(False, td, copied(False, halves[td, 0], "grad%d_0" % td), 0, HALF)
+            nc.sync.dma_start(out_planes[td], windows[td][:])

@@ -60,8 +60,9 @@ def tile_attend_gmf_nce_v_kernel(tc, uT, vT, y, us, ts, offs, uoffs, out):
 
         nc.scalar.dma_start(ts_window[P - 1 : P, :], ts[0:1, :])
         nc.sync.dma_start(tail_list[:], offs)
-        row_scale = kept([P, PASSES, PACK], F32, "row_scale")
-        nc.scalar.dma_start(row_scale[:], us[0].rearrange("(g p t) o -> p g (t o)", g=PASSES, t=PACK))
+        us_line = kept([P, R], F32, "us_line")
+        nc.vector.memset(us_line[0 : P - 1, :].bitcast(I32), 0)
+        nc.scalar.dma_start(us_line[P - 1 : P, :], us[0].rearrange("r o -> o r"))
 
         def load_plane(table, td, name):
             tile = kept([P, T], F32, name)
@@ -79,6 +80,12 @@ def tile_attend_gmf_nce_v_kernel(tc, uT, vT, y, us, ts, offs, uoffs, out):
             for k in range(2):
                 nc.sync.dma_start(labels[steps.index((g, k))][:], y_rows[g][:, :, k * HALF : (k + 1) * HALF])
 
+        row_scale = kept([P, PASSES, PACK], F32, "row_scale")
+        for g in range(PASSES):
+            bank = in_bank(6 + g, [P, PACK, P], "us_turned%d" % g)
+            for t in range(PACK):
+                nc.tensor.transpose(bank[:, t, :], us_line[:, g * K + t : (g + 1) * K : PACK], ident[:])
+            nc.scalar.copy(row_scale[:, g, :], bank[:, :, P - 1])
         ts_picked = kept([P, N], F32, "ts_picked")
         nc.vector.tensor_copy(ts_picked[:], listed(ts_window, tail_list, 0, N))
         bank = in_bank(0, [P, BLOCKS, P], "ts_turned")
@@ -202,6 +209,11 @@ def tile_attend_gmf_nce_v_kernel(tc, uT, vT, y, us, ts, offs, uoffs, out):
                     open_sum(n, j, sum_banks[g][j])
             tile = z[n][:, rows, :]
             nc.vector.tensor_tensor(tile, acc[:], scale_by_row[g][:, rows, k * HALF : (k + 1) * HALF], ALU.mult)
+            if (g, k, a) == (1, 1, 1):
+                for t in (2, 3):
+                    nc.scalar.activation(z[n][:, t, :], z[n][:, t, :], ACT.Sigmoid)
+                    close_sums(n, (t,))
+                return
             nc.scalar.activation(tile, tile, ACT.Sigmoid)
             if k:
                 close_sums(n, (2 * a, 2 * a + 1))
@@ -248,11 +260,12 @@ def tile_attend_gmf_nce_v_kernel(tc, uT, vT, y, us, ts, offs, uoffs, out):
 
         def product(acc, td, k):
             slots = slice(k * HALF, (k + 1) * HALF)
-            for g in range(PASSES):
+            order = (1, 0) if td and not k else (0, 1)
+            for g in order:
                 nc.tensor.matmul_mx(
                     out=acc, lhsT=xt_codes[td][:, g * P : (g + 1) * P].bitcast(E4M3),
                     lhsT_scale=xt_scales[:, td * plane + g * P : td * plane + (g + 1) * P],
-                    rhs=h_codes[g][:, slots].bitcast(E5M2), rhs_scale=h_scales[g][:, slots], start=(g == 0), stop=(g == PASSES - 1),
+                    rhs=h_codes[g][:, slots].bitcast(E5M2), rhs_scale=h_scales[g][:, slots], start=(g == order[0]), stop=(g == order[1]),
                 )
 
         for n in (2, 3):
@@ -283,17 +296,18 @@ def tile_attend_gmf_nce_v_kernel(tc, uT, vT, y, us, ts, offs, uoffs, out):
             (nc.scalar.copy if on_scalar else nc.vector.tensor_copy)(grad[:], acc)
             return grad[:]
 
-        halves = {}
-        for k, numbers in ((1, (5, 0, 1, 2)), (0, (3, 6, 7, 4))):
-            for td, number in enumerate(numbers):
-                halves[td, k] = in_bank(number, [P, HALF], "grad_half%d_%d" % (td, k))[:]
-                product(halves[td, k], td, k)
-        ahead = copied(True, halves[0, 1], "grad0_1")
+        early = [in_bank(5, [P, HALF], "early0")[:], in_bank(0, [P, HALF], "early1")[:]]
+        both = in_bank(1, [P, 2, HALF], "early23")
+        early.extend(both[:, e, :] for e in range(2))
+        late = [in_bank(number, [P, HALF], "late%d" % td)[:] for td, number in enumerate((3, 6, 7, 4))]
+        for k, banks in ((1, early), (0, late)):
+            for td in range(PACK):
+                product(banks[td], td, k)
+        grads = [copied(True, early[td], "grad_early%d" % td) for td in range(2)]
+        last_two = copied(False, both[:], "grad_early23", "h3")
+        grads.extend(last_two[:, e, :] for e in range(2))
         for td in range(PACK):
-            grad = ahead
-            if td + 1 < PACK:
-                ahead = copied(True, halves[td + 1, 1], "grad%d_1" % (td + 1))
-            scatter(True, td, grad, HALF, HALF)
+            scatter(True, td, grads[td], HALF, HALF)
         for td in range(PACK):
-            scatter(False, td, copied(False, halves[td, 0], "grad%d_0" % td), 0, HALF)
+            scatter(False, td, copied(False, late[td], "grad_late%d" % td), 0, HALF)
             nc.sync.dma_start(out_planes[td], windows[td][:])

@@ -22,6 +22,7 @@ PASSES = R // K
 BLOCKS = N // P
 HALF = N // 2
 BANK = 2048
+LAST_H = 36864
 FLOPS = 2 * 2 * D * R * N
 
 
@@ -54,9 +55,9 @@ def tile_attend_gmf_nce_v_kernel(tc, uT, vT, y, us, ts, offs, uoffs, out):
         make_identity(nc, ident[:])
         ts_window = kept([P, T], F32, "ts_window")
         nc.gpsimd.memset(ts_window[0 : P - 1, :].bitcast(I32), 0)
-        windows = [kept([P, T], F32, "window%d" % td) for td in range(PACK)]
-        for td, window in enumerate(windows):
-            (nc.gpsimd if td < 3 else nc.vector).memset(window[:].bitcast(I32), 0)
+        windows = [kept([P, T], F32, "window%d" % td) for td in range(2)]
+        for window in windows:
+            nc.gpsimd.memset(window[:].bitcast(I32), 0)
 
         nc.scalar.dma_start(ts_window[P - 1 : P, :], ts[0:1, :])
         nc.sync.dma_start(tail_list[:], offs)
@@ -80,18 +81,12 @@ def tile_attend_gmf_nce_v_kernel(tc, uT, vT, y, us, ts, offs, uoffs, out):
             for k in range(2):
                 nc.sync.dma_start(labels[steps.index((g, k))][:], y_rows[g][:, :, k * HALF : (k + 1) * HALF])
 
-        row_scale = kept([P, PASSES, PACK], F32, "row_scale")
-        for g in range(PASSES):
-            bank = in_bank(6 + g, [P, PACK, P], "us_turned%d" % g)
-            for t in range(PACK):
-                nc.tensor.transpose(bank[:, t, :], us_line[:, g * K + t : (g + 1) * K : PACK], ident[:])
-            nc.scalar.copy(row_scale[:, g, :], bank[:, :, P - 1])
         ts_picked = kept([P, N], F32, "ts_picked")
         nc.vector.tensor_copy(ts_picked[:], listed(ts_window, tail_list, 0, N))
         bank = in_bank(0, [P, BLOCKS, P], "ts_turned")
         for b in range(BLOCKS):
             nc.tensor.transpose(bank[:, b, :], ts_picked[:, b * P : (b + 1) * P], ident[:])
-        ts_cols = kept([P, BLOCKS], F32, "ts_cols")
+        ts_cols = placed([P, BLOCKS], F32, "ts_cols", 20480)
         ts_minus = kept([P, 2], F32, "ts_minus")
         nc.scalar.copy(ts_cols[:], bank[:, :, P - 1])
         nc.scalar.activation(ts_minus[:], bank[:, 2:4, P - 1], ACT.Copy, scale=-1.0)
@@ -101,6 +96,12 @@ def tile_attend_gmf_nce_v_kernel(tc, uT, vT, y, us, ts, offs, uoffs, out):
         ts_signed = placed([P, N], F32, "ts_signed", 0)
         nc.scalar.copy(ts_signed[:, 0:HALF], ts_rows[:, 0:HALF])
         nc.scalar.activation(ts_signed[:, HALF:], ts_rows[:, HALF:], ACT.Copy, scale=-1.0)
+        row_scale = kept([P, PASSES, PACK], F32, "row_scale")
+        for g in range(PASSES):
+            bank = in_bank(6 + g, [P, PACK, P], "us_turned%d" % g)
+            for t in range(PACK):
+                nc.tensor.transpose(bank[:, t, :], us_line[:, g * K + t : (g + 1) * K : PACK], ident[:])
+            nc.scalar.copy(row_scale[:, g, :], bank[:, :, P - 1])
         scale_by_slot = []
         for g in range(PASSES):
             us_rows = in_bank(2 + g, [P, PACK, P], "us_rows%d" % g)
@@ -269,7 +270,7 @@ def tile_attend_gmf_nce_v_kernel(tc, uT, vT, y, us, ts, offs, uoffs, out):
                 )
 
         for n in (2, 3):
-            h[n] = kept([P, HALF * PACK], BF16, "h%d" % n)
+            h[n] = kept([P, HALF * PACK], BF16, "h2") if n == 2 else placed([P, HALF * PACK], BF16, "h3", LAST_H)
             for j in range(2):
                 weigh_by_slot(n, j)
         h[0] = kept([P, HALF * PACK], BF16, "h0", "scale_by_slot1")
@@ -277,11 +278,14 @@ def tile_attend_gmf_nce_v_kernel(tc, uT, vT, y, us, ts, offs, uoffs, out):
         weigh_by_row(0, 0, P)
         quantise(3)
         weigh_by_row(0, P, P)
-        h[1] = kept([P, HALF * PACK], BF16, "h1", "h3")
+        h[1] = placed([P, HALF * PACK], BF16, "h1", LAST_H)
         weigh_by_row(1, 0, HALF)
         quantise(0)
         quantise(1)
 
+        for td, offset in ((2, LAST_H + 1024 - 4 * T), (3, LAST_H + 1024)):
+            windows.append(placed([P, T], F32, "window%d" % td, offset))
+            nc.gpsimd.memset(windows[td][:].bitcast(I32), 0)
         out_planes = out.rearrange("(p t) c -> t p c", t=PACK)
 
         def scatter(on_scalar, td, grad, first, count):
@@ -304,7 +308,7 @@ def tile_attend_gmf_nce_v_kernel(tc, uT, vT, y, us, ts, offs, uoffs, out):
             for td in range(PACK):
                 product(banks[td], td, k)
         grads = [copied(True, early[td], "grad_early%d" % td) for td in range(2)]
-        last_two = copied(False, both[:], "grad_early23", "h3")
+        last_two = copied(False, both[:], "grad_early23", "scale_by_slot1")
         grads.extend(last_two[:, e, :] for e in range(2))
         for td in range(PACK):
             scatter(True, td, grads[td], HALF, HALF)

@@ -76,10 +76,10 @@ def tile_attend_gmf_nce_v_kernel(tc, uT, vT, y, us, ts, offs, uoffs, out):
         v_raw = [load_plane(vT, td, "v_raw%d" % td) for td in range(PACK)]
         steps = [(g, k) for k in range(2) for g in range(PASSES)]
         y_rows = y[0].rearrange("(g p t) i -> g p t i", g=PASSES, t=PACK)
-        labels = [kept([P, PACK, HALF], F32, "labels%d" % n) for n in range(len(steps))]
+        whole_rows = [kept([P, PACK, N], F32, "labels%d" % g) for g in range(PASSES)]
         for g in range(PASSES):
-            for k in range(2):
-                nc.sync.dma_start(labels[steps.index((g, k))][:], y_rows[g][:, :, k * HALF : (k + 1) * HALF])
+            nc.sync.dma_start(whole_rows[g][:], y_rows[g])
+        labels = [whole_rows[g][:, :, k * HALF : (k + 1) * HALF] for g, k in steps]
 
         ts_picked = kept([P, N], F32, "ts_picked")
         nc.vector.tensor_copy(ts_picked[:], listed(ts_window, tail_list, 0, N))
@@ -118,7 +118,7 @@ def tile_attend_gmf_nce_v_kernel(tc, uT, vT, y, us, ts, offs, uoffs, out):
 
         heads = placed([P, PACK * R], BF16, "heads", 20480)
         plane = PASSES * P
-        turned = [kept([P, 2 * plane * PACK], BF16, "turned0"), placed([P, 2 * plane * PACK], BF16, "turned1", 16384)]
+        turned = [placed([P, 2 * plane * PACK], BF16, "turned0", 16384), kept([P, 2 * plane * PACK], BF16, "turned1")]
         woven = kept([P, R * PACK], BF16, "woven")
 
         def gather(on_scalar, into, window):
@@ -128,7 +128,11 @@ def tile_attend_gmf_nce_v_kernel(tc, uT, vT, y, us, ts, offs, uoffs, out):
                 nc.vector.tensor_copy(into, window)
 
         for td in range(PACK):
-            gather(td == 0, heads[:, td * R : (td + 1) * R], listed(u_raw[td], head_list, 0, R))
+            if td < PACK - 1:
+                gather(td == 0, heads[:, td * R : (td + 1) * R], listed(u_raw[td], head_list, 0, R))
+            else:
+                for g in range(PASSES):
+                    gather(g == 1, heads[:, td * R + g * K : td * R + (g + 1) * K], listed(u_raw[td], head_list, g * K, K))
             bank = in_bank(4 + td, [P, PASSES, 2, P], "heads_turned%d" % td)
             for g in range(PASSES):
                 first = td * R + g * K
@@ -147,10 +151,13 @@ def tile_attend_gmf_nce_v_kernel(tc, uT, vT, y, us, ts, offs, uoffs, out):
         nc.vector.quantize_mx(x_codes[:].bitcast(E4M3), x_scales[:], woven[:])
         xt_scales = kept([P, PACK * plane], U8, "xt_scales")
         xt_codes = []
-        for n in range(2):
-            codes = placed([P, 2 * plane], U32, "xt_codes%d" % n, 20480 + 2048 * n)
+
+        def quantise_turned(n, offset):
+            codes = placed([P, 2 * plane], U32, "xt_codes%d" % n, offset)
             nc.vector.quantize_mx(codes[:].bitcast(E4M3), xt_scales[:, 2 * n * plane : 2 * (n + 1) * plane], turned[n][:])
             xt_codes.extend(codes[:, e * plane : (e + 1) * plane] for e in range(2))
+
+        quantise_turned(0, 20480)
 
         tails = [placed([P, HALF, PACK], BF16, "tails0", 16384), kept([P, HALF, PACK], BF16, "tails1")]
 
@@ -174,6 +181,8 @@ def tile_attend_gmf_nce_v_kernel(tc, uT, vT, y, us, ts, offs, uoffs, out):
         w_scales = [kept([P, HALF], U8, "w_scales%d" % k) for k in range(2)]
         for k in range(2):
             nc.vector.quantize_mx(w_codes[k][:].bitcast(E4M3), w_scales[k][:], tails[k][:].rearrange("p i d -> p (i d)"))
+            if k == 0:
+                quantise_turned(1, 16384)
 
         z = [kept([P, PACK, HALF], F32, "z%d" % n) for n in range(len(steps))]
 

@@ -103,7 +103,8 @@ def tile_attend_gmf_nce_v_kernel(tc, uT, vT, y, us, ts, offs, uoffs, out):
                 nc.tensor.transpose(bank[:, t, :], us_line[:, g * K + t : (g + 1) * K : PACK], ident[:])
             nc.scalar.copy(row_scale[:, g, :], bank[:, :, P - 1])
         scale_by_slot = []
-        for g in range(PASSES):
+
+        def spread_by_slot(g):
             us_rows = in_bank(2 + g, [P, PACK, P], "us_rows%d" % g)
             for t in range(PACK):
                 nc.tensor.transpose(us_rows[:, t, :], row_scale[:, g, t : t + 1].to_broadcast([P, P]), ident[:])
@@ -111,6 +112,7 @@ def tile_attend_gmf_nce_v_kernel(tc, uT, vT, y, us, ts, offs, uoffs, out):
             for j in range(2):
                 nc.scalar.activation(tile[:, j], us_rows[:].rearrange("p (u e) s -> p u s e", e=2), ACT.Copy, scale=ts_minus[:, j : j + 1])
             scale_by_slot.append(tile)
+
         scale_by_row = [kept([P, PACK, N], F32, "scale_by_row%d" % g) for g in range(PASSES)]
         for g in range(PASSES):
             for t in range(PACK):
@@ -127,12 +129,10 @@ def tile_attend_gmf_nce_v_kernel(tc, uT, vT, y, us, ts, offs, uoffs, out):
             else:
                 nc.vector.tensor_copy(into, window)
 
-        for td in range(PACK):
-            if td < PACK - 1:
-                gather(td == 0, heads[:, td * R : (td + 1) * R], listed(u_raw[td], head_list, 0, R))
-            else:
-                for g in range(PASSES):
-                    gather(g == 1, heads[:, td * R + g * K : td * R + (g + 1) * K], listed(u_raw[td], head_list, g * K, K))
+        def gather_heads(on_scalar, td, first, count):
+            gather(on_scalar, heads[:, td * R + first : td * R + first + count], listed(u_raw[td], head_list, first, count))
+
+        def turn_heads(td):
             bank = in_bank(4 + td, [P, PASSES, 2, P], "heads_turned%d" % td)
             for g in range(PASSES):
                 first = td * R + g * K
@@ -141,6 +141,17 @@ def tile_attend_gmf_nce_v_kernel(tc, uT, vT, y, us, ts, offs, uoffs, out):
                     nc.tensor.transpose(bank[:, g, u, :], words[:, u : K // 2 : 2], ident[:])
             words = turned[td // 2][:].bitcast(F32).rearrange("m (d g p u) -> m d g p u", g=PASSES, d=2, u=2)
             nc.scalar.copy(words[:, td % 2], bank[:].rearrange("m g u p -> m g p u"))
+
+        gather_heads(True, 0, 0, R)
+        spread_by_slot(0)
+        turn_heads(0)
+        gather_heads(False, 1, 0, R)
+        gather_heads(False, 2, 0, R)
+        gather_heads(False, 3, 0, K)
+        gather_heads(True, 3, K, K)
+        for td in range(1, PACK):
+            turn_heads(td)
+        spread_by_slot(1)
         for g in range(PASSES):
             nc.vector.tensor_copy(
                 woven[:, g * K * PACK : (g + 1) * K * PACK].rearrange("p (t c e d) -> p c t e d", t=PACK, e=2, d=PACK),
@@ -161,22 +172,16 @@ def tile_attend_gmf_nce_v_kernel(tc, uT, vT, y, us, ts, offs, uoffs, out):
 
         tails = [placed([P, HALF, PACK], BF16, "tails0", 16384), kept([P, HALF, PACK], BF16, "tails1")]
 
-        def weave_pair(k, n, pair):
+        for n in range(2):
+            pair = kept([P, 2, HALF], BF16, "pair%d" % n, "u_raw2")
+            for e in range(2):
+                td = 2 * n + e
+                nc.vector.tensor_copy(tails[0][:, :, td], listed(v_raw[td], tail_list, 0, HALF))
+                gather(True, pair[:, e, :], listed(v_raw[td], tail_list, HALF, HALF))
             nc.scalar.copy(
-                tails[k][:, :, 2 * n : 2 * n + 2].rearrange("p (c i) d -> p c d i", i=4),
-                pair.rearrange("p d (c i) -> p c d i", i=4),
+                tails[1][:, :, 2 * n : 2 * n + 2].rearrange("p (c i) d -> p c d i", i=4),
+                pair[:].rearrange("p d (c i) -> p c d i", i=4),
             )
-
-        early_pair = kept([P, 2, N], BF16, "early_pair", "u_raw2")
-        for td in range(2):
-            gather(True, early_pair[:, td, :], listed(v_raw[td], tail_list, 0, N))
-        for k in (1, 0):
-            weave_pair(k, 0, early_pair[:, :, k * HALF : (k + 1) * HALF])
-        late_pair = kept([P, 2, HALF], BF16, "late_pair", "u_raw2")
-        for td in (2, 3):
-            nc.vector.tensor_copy(tails[0][:, :, td], listed(v_raw[td], tail_list, 0, HALF))
-            gather(True, late_pair[:, td - 2, :], listed(v_raw[td], tail_list, HALF, HALF))
-        weave_pair(1, 1, late_pair[:])
         w_codes = [kept([P, HALF], U32, "w_codes0"), placed([P, HALF], U32, "w_codes1", 0)]
         w_scales = [kept([P, HALF], U8, "w_scales%d" % k) for k in range(2)]
         for k in range(2):

@@ -93,9 +93,11 @@ def tile_attend_gmf_nce_v_kernel(tc, uT, vT, y, us, ts, offs, uoffs, out):
         ts_rows = in_bank(1, [P, N], "ts_rows")
         for b in range(BLOCKS):
             nc.tensor.transpose(ts_rows[:, b * P : (b + 1) * P], ts_cols[:, b : b + 1].to_broadcast([P, P]), ident[:])
-        ts_signed = placed([P, N], F32, "ts_signed", 0)
+        ts_signed = kept([P, N], F32, "ts_signed")
         nc.scalar.copy(ts_signed[:, 0:HALF], ts_rows[:, 0:HALF])
         nc.scalar.activation(ts_signed[:, HALF:], ts_rows[:, HALF:], ACT.Copy, scale=-1.0)
+        ts_low = placed([P, HALF], F32, "ts_low", 0)
+        nc.scalar.copy(ts_low[:], ts_rows[:, 0:HALF])
         row_scale = kept([P, PASSES, PACK], F32, "row_scale")
         for g in range(PASSES):
             bank = in_bank(6 + g, [P, PACK, P], "us_turned%d" % g)
@@ -108,15 +110,15 @@ def tile_attend_gmf_nce_v_kernel(tc, uT, vT, y, us, ts, offs, uoffs, out):
             us_rows = in_bank(2 + g, [P, PACK, P], "us_rows%d" % g)
             for t in range(PACK):
                 nc.tensor.transpose(us_rows[:, t, :], row_scale[:, g, t : t + 1].to_broadcast([P, P]), ident[:])
-            tile = kept([P, 2, 2, P, 2], F32, "scale_by_slot%d" % g)
+            tile = kept([P, 2, 2, P, 2], F32, "scale_by_slot%d" % g, "v_raw1" if g else None)
             for j in range(2):
                 nc.scalar.activation(tile[:, j], us_rows[:].rearrange("p (u e) s -> p u s e", e=2), ACT.Copy, scale=ts_minus[:, j : j + 1])
             scale_by_slot.append(tile)
 
-        scale_by_row = [kept([P, PACK, N], F32, "scale_by_row%d" % g) for g in range(PASSES)]
-        for g in range(PASSES):
+        scale_by_row = [kept([P, PACK, width], F32, "scale_by_row%d" % g) for g, width in enumerate((N, HALF))]
+        for g, spread in enumerate((ts_signed, ts_low)):
             for t in range(PACK):
-                nc.gpsimd.tensor_scalar(scale_by_row[g][:, t, :], ts_signed[:], row_scale[:, g, t : t + 1], 0.0, ALU.mult, ALU.add)
+                nc.gpsimd.tensor_scalar(scale_by_row[g][:, t, :], spread[:], row_scale[:, g, t : t + 1], 0.0, ALU.mult, ALU.add)
 
         heads = placed([P, PACK * R], BF16, "heads", 20480)
         plane = PASSES * P
@@ -151,7 +153,6 @@ def tile_attend_gmf_nce_v_kernel(tc, uT, vT, y, us, ts, offs, uoffs, out):
         gather_heads(True, 3, K, K)
         for td in range(1, PACK):
             turn_heads(td)
-        spread_by_slot(1)
         for g in range(PASSES):
             nc.vector.tensor_copy(
                 woven[:, g * K * PACK : (g + 1) * K * PACK].rearrange("p (t c e d) -> p c t e d", t=PACK, e=2, d=PACK),
@@ -172,16 +173,24 @@ def tile_attend_gmf_nce_v_kernel(tc, uT, vT, y, us, ts, offs, uoffs, out):
 
         tails = [placed([P, HALF, PACK], BF16, "tails0", 16384), kept([P, HALF, PACK], BF16, "tails1")]
 
-        for n in range(2):
-            pair = kept([P, 2, HALF], BF16, "pair%d" % n, "u_raw2")
-            for e in range(2):
-                td = 2 * n + e
-                nc.vector.tensor_copy(tails[0][:, :, td], listed(v_raw[td], tail_list, 0, HALF))
-                gather(True, pair[:, e, :], listed(v_raw[td], tail_list, HALF, HALF))
-            nc.scalar.copy(
-                tails[1][:, :, 2 * n : 2 * n + 2].rearrange("p (c i) d -> p c d i", i=4),
-                pair[:].rearrange("p d (c i) -> p c d i", i=4),
+        def weave_pair(copy, k, n, pair):
+            copy(
+                tails[k][:, :, 2 * n : 2 * n + 2].rearrange("p (c i) d -> p c d i", i=4),
+                pair.rearrange("p d (c i) -> p c d i", i=4),
             )
+
+        early_pair = kept([P, 2, N], BF16, "early_pair", "u_raw2")
+        for td in range(2):
+            gather(True, early_pair[:, td, :], listed(v_raw[td], tail_list, 0, N))
+        spread_by_slot(1)
+        nc.vector.tensor_copy(tails[0][:, :, 2], listed(v_raw[2], tail_list, 0, HALF))
+        weave_pair(nc.vector.tensor_copy, 0, 0, early_pair[:, :, 0:HALF])
+        weave_pair(nc.vector.tensor_copy, 1, 0, early_pair[:, :, HALF:])
+        late_pair = kept([P, 2, HALF], BF16, "late_pair", "v_raw0")
+        nc.vector.tensor_copy(tails[0][:, :, 3], listed(v_raw[3], tail_list, 0, HALF))
+        for td in (2, 3):
+            gather(True, late_pair[:, td - 2, :], listed(v_raw[td], tail_list, HALF, HALF))
+        weave_pair(nc.scalar.copy, 1, 1, late_pair[:])
         w_codes = [kept([P, HALF], U32, "w_codes0"), placed([P, HALF], U32, "w_codes1", 0)]
         w_scales = [kept([P, HALF], U8, "w_scales%d" % k) for k in range(2)]
         for k in range(2):
@@ -223,12 +232,13 @@ def tile_attend_gmf_nce_v_kernel(tc, uT, vT, y, us, ts, offs, uoffs, out):
                 for j in range(2):
                     open_sum(n, j, sum_banks[g][j])
             tile = z[n][:, rows, :]
-            nc.vector.tensor_tensor(tile, acc[:], scale_by_row[g][:, rows, k * HALF : (k + 1) * HALF], ALU.mult)
-            if (g, k, a) == (1, 1, 1):
-                for t in (2, 3):
-                    nc.scalar.activation(z[n][:, t, :], z[n][:, t, :], ACT.Sigmoid)
+            if (g, k) == (1, 1):
+                nc.vector.tensor_tensor(tile, acc[:], ts_signed[:, HALF:].unsqueeze(1).to_broadcast([P, 2, HALF]), ALU.mult)
+                for t in (2 * a, 2 * a + 1):
+                    nc.scalar.activation(z[n][:, t, :], z[n][:, t, :], ACT.Sigmoid, scale=row_scale[:, g, t : t + 1])
                     close_sums(n, (t,))
                 return
+            nc.vector.tensor_tensor(tile, acc[:], scale_by_row[g][:, rows, k * HALF : (k + 1) * HALF], ALU.mult)
             nc.scalar.activation(tile, tile, ACT.Sigmoid)
             if k:
                 close_sums(n, (2 * a, 2 * a + 1))
@@ -238,7 +248,7 @@ def tile_attend_gmf_nce_v_kernel(tc, uT, vT, y, us, ts, offs, uoffs, out):
         for t in range(2):
             acc = in_bank(4 + t, [P, HALF], "first%d" % t)
             score(acc[:], 0, t, 0)
-            nc.vector.tensor_tensor(z[0][:, t, :], acc[:], ts_signed[:, 0:HALF], ALU.mult)
+            nc.vector.tensor_tensor(z[0][:, t, :], acc[:], ts_low[:], ALU.mult)
             nc.scalar.activation(z[0][:, t, :], z[0][:, t, :], ACT.Sigmoid, scale=row_scale[:, 0, t : t + 1])
         nc.gpsimd.tensor_tensor(z[0][:, 0:2, :], z[0][:, 0:2, :], labels[0][:, 0:2, :], ALU.subtract)
         for g, k, a, number in ((0, 0, 1, 0), (1, 0, 0, 1), (1, 0, 1, 2), (0, 1, 0, 3), (0, 1, 1, 6), (1, 1, 0, 7), (1, 1, 1, 4)):
@@ -287,7 +297,7 @@ def tile_attend_gmf_nce_v_kernel(tc, uT, vT, y, us, ts, offs, uoffs, out):
             h[n] = kept([P, HALF * PACK], BF16, "h2") if n == 2 else placed([P, HALF * PACK], BF16, "h3", LAST_H)
             for j in range(2):
                 weigh_by_slot(n, j)
-        h[0] = kept([P, HALF * PACK], BF16, "h0", "scale_by_slot1")
+        h[0] = kept([P, HALF * PACK], BF16, "h0", "v_raw1")
         quantise(2)
         weigh_by_row(0, 0, P)
         quantise(3)
@@ -322,7 +332,7 @@ def tile_attend_gmf_nce_v_kernel(tc, uT, vT, y, us, ts, offs, uoffs, out):
             for td in range(PACK):
                 product(banks[td], td, k)
         grads = [copied(True, early[td], "grad_early%d" % td) for td in range(2)]
-        last_two = copied(False, both[:], "grad_early23", "scale_by_slot1")
+        last_two = copied(False, both[:], "grad_early23", "v_raw1")
         grads.extend(last_two[:, e, :] for e in range(2))
         for td in range(PACK):
             scatter(True, td, grads[td], HALF, HALF)

@@ -22,7 +22,7 @@ PASSES = R // K
 BLOCKS = N // P
 HALF = N // 2
 BANK = 2048
-LAST_H = 36864
+PLANE = 4 * T
 FLOPS = 2 * 2 * D * R * N
 
 
@@ -36,8 +36,8 @@ def tile_attend_gmf_nce_v_kernel(tc, uT, vT, y, us, ts, offs, uoffs, out):
         def in_bank(number, shape, name):
             return psum.tile(shape, F32, name=name, tag=name, offset=number * BANK)
 
-        def kept(shape, dtype, name, tag=None):
-            return keep.tile(shape, dtype, name=name, tag=tag or name, align_bytes=64)
+        def kept(shape, dtype, name):
+            return keep.tile(shape, dtype, name=name, tag=name, align_bytes=64)
 
         def placed(shape, dtype, name, offset):
             return shared.tile(shape, dtype, name=name, tag=name, align_bytes=64, offset=offset)
@@ -53,51 +53,52 @@ def tile_attend_gmf_nce_v_kernel(tc, uT, vT, y, us, ts, offs, uoffs, out):
         nc.scalar.activation(warm[:, 1:2], warm[:, 0:1], ACT.Sigmoid)
         ident = kept([P, P], F32, "ident")
         make_identity(nc, ident[:])
-        ts_window = kept([P, T], F32, "ts_window")
+        ts_window = placed([P, T], F32, "ts_window", 4 * PLANE)
+        us_line = placed([P, R], F32, "us_line", 5 * PLANE)
         nc.gpsimd.memset(ts_window[0 : P - 1, :].bitcast(I32), 0)
-        windows = [kept([P, T], F32, "window%d" % td) for td in range(2)]
+        zeros = placed([P, P], F32, "zeros", 8 * PLANE)
+        nc.vector.memset(zeros[:], 0.0)
+        nc.vector.memset(us_line[0 : P - 1, :].bitcast(I32), 0)
+        windows = [kept([P, T], F32, "window%d" % td) for td in range(3)]
         for window in windows:
             nc.gpsimd.memset(window[:].bitcast(I32), 0)
 
         nc.scalar.dma_start(ts_window[P - 1 : P, :], ts[0:1, :])
-        nc.sync.dma_start(tail_list[:], offs)
-        us_line = kept([P, R], F32, "us_line")
-        nc.vector.memset(us_line[0 : P - 1, :].bitcast(I32), 0)
         nc.scalar.dma_start(us_line[P - 1 : P, :], us[0].rearrange("r o -> o r"))
+        nc.sync.dma_start(tail_list[:], offs)
 
-        def load_plane(table, td, name):
-            tile = kept([P, T], F32, name)
+        def load_plane(tile, table, td):
             nc.sync.dma_start(tile[:], table.rearrange("(p t) c -> t p c", t=PACK)[td])
             return tile
 
-        u_raw = [load_plane(uT, 0, "u_raw0")]
-        nc.sync.dma_start(head_list[:], uoffs)
-        u_raw.extend(load_plane(uT, td, "u_raw%d" % td) for td in range(1, PACK))
-        v_raw = [load_plane(vT, td, "v_raw%d" % td) for td in range(PACK)]
-        steps = [(g, k) for k in range(2) for g in range(PASSES)]
+        u_raw = []
+        for td in range(PACK):
+            u_raw.append(load_plane(placed([P, T], F32, "u_raw%d" % td, td * PLANE), uT, td))
+            if td == 0:
+                nc.sync.dma_start(head_list[:], uoffs)
+        v_raw = [load_plane(kept([P, T], F32, "v_raw%d" % td), vT, td) for td in range(PACK)]
         y_rows = y[0].rearrange("(g p t) i -> g p t i", g=PASSES, t=PACK)
-        whole_rows = [kept([P, PACK, N], F32, "labels%d" % g) for g in range(PASSES)]
+        labels = [kept([P, PACK, N], F32, "labels%d" % g) for g in range(PASSES)]
         for g in range(PASSES):
-            nc.sync.dma_start(whole_rows[g][:], y_rows[g])
-        labels = [whole_rows[g][:, :, k * HALF : (k + 1) * HALF] for g, k in steps]
+            nc.sync.dma_start(labels[g][:], y_rows[g])
 
+        heads = kept([P, PACK * R], BF16, "heads")
+        late_heads = heads[:, PACK * R - K :].bitcast(F32)
+        ts_cols = late_heads[:, 0:BLOCKS]
+        ts_minus = late_heads[:, 8:10]
         ts_picked = kept([P, N], F32, "ts_picked")
         nc.vector.tensor_copy(ts_picked[:], listed(ts_window, tail_list, 0, N))
         bank = in_bank(0, [P, BLOCKS, P], "ts_turned")
         for b in range(BLOCKS):
             nc.tensor.transpose(bank[:, b, :], ts_picked[:, b * P : (b + 1) * P], ident[:])
-        ts_cols = placed([P, BLOCKS], F32, "ts_cols", 20480)
-        ts_minus = kept([P, 2], F32, "ts_minus")
-        nc.scalar.copy(ts_cols[:], bank[:, :, P - 1])
-        nc.scalar.activation(ts_minus[:], bank[:, 2:4, P - 1], ACT.Copy, scale=-1.0)
+        nc.scalar.copy(ts_cols, bank[:, :, P - 1])
+        nc.scalar.activation(ts_minus, bank[:, 2:4, P - 1], ACT.Copy, scale=-1.0)
         ts_rows = in_bank(1, [P, N], "ts_rows")
         for b in range(BLOCKS):
             nc.tensor.transpose(ts_rows[:, b * P : (b + 1) * P], ts_cols[:, b : b + 1].to_broadcast([P, P]), ident[:])
         ts_signed = kept([P, N], F32, "ts_signed")
         nc.scalar.copy(ts_signed[:, 0:HALF], ts_rows[:, 0:HALF])
         nc.scalar.activation(ts_signed[:, HALF:], ts_rows[:, HALF:], ACT.Copy, scale=-1.0)
-        ts_low = placed([P, HALF], F32, "ts_low", 0)
-        nc.scalar.copy(ts_low[:], ts_rows[:, 0:HALF])
         row_scale = kept([P, PASSES, PACK], F32, "row_scale")
         for g in range(PASSES):
             bank = in_bank(6 + g, [P, PACK, P], "us_turned%d" % g)
@@ -105,34 +106,22 @@ def tile_attend_gmf_nce_v_kernel(tc, uT, vT, y, us, ts, offs, uoffs, out):
                 nc.tensor.transpose(bank[:, t, :], us_line[:, g * K + t : (g + 1) * K : PACK], ident[:])
             nc.scalar.copy(row_scale[:, g, :], bank[:, :, P - 1])
         scale_by_slot = []
-
-        def spread_by_slot(g):
+        for g in range(PASSES):
             us_rows = in_bank(2 + g, [P, PACK, P], "us_rows%d" % g)
             for t in range(PACK):
                 nc.tensor.transpose(us_rows[:, t, :], row_scale[:, g, t : t + 1].to_broadcast([P, P]), ident[:])
-            tile = kept([P, 2, 2, P, 2], F32, "scale_by_slot%d" % g, "v_raw1" if g else None)
+            tile = kept([P, 2, 2, P, 2], F32, "scale_by_slot%d" % g)
             for j in range(2):
                 nc.scalar.activation(tile[:, j], us_rows[:].rearrange("p (u e) s -> p u s e", e=2), ACT.Copy, scale=ts_minus[:, j : j + 1])
             scale_by_slot.append(tile)
 
-        scale_by_row = [kept([P, PACK, width], F32, "scale_by_row%d" % g) for g, width in enumerate((N, HALF))]
-        for g, spread in enumerate((ts_signed, ts_low)):
-            for t in range(PACK):
-                nc.gpsimd.tensor_scalar(scale_by_row[g][:, t, :], spread[:], row_scale[:, g, t : t + 1], 0.0, ALU.mult, ALU.add)
+        scale_by_row = [kept([P, PACK, N], F32, "scale_by_row%d" % g) for g in range(PASSES)]
+        for t in range(PACK):
+            nc.gpsimd.tensor_scalar(scale_by_row[0][:, t, :], ts_signed[:], row_scale[:, 0, t : t + 1], 0.0, ALU.mult, ALU.add)
 
-        heads = placed([P, PACK * R], BF16, "heads", 20480)
         plane = PASSES * P
-        turned = [placed([P, 2 * plane * PACK], BF16, "turned0", 16384), kept([P, 2 * plane * PACK], BF16, "turned1")]
+        turned = [kept([P, 2 * plane * PACK], BF16, "turned%d" % n) for n in range(2)]
         woven = kept([P, R * PACK], BF16, "woven")
-
-        def gather(on_scalar, into, window):
-            if on_scalar:
-                nc.scalar.activation(into, window, ACT.Copy)
-            else:
-                nc.vector.tensor_copy(into, window)
-
-        def gather_heads(on_scalar, td, first, count):
-            gather(on_scalar, heads[:, td * R + first : td * R + first + count], listed(u_raw[td], head_list, first, count))
 
         def turn_heads(td):
             bank = in_bank(4 + td, [P, PASSES, 2, P], "heads_turned%d" % td)
@@ -144,14 +133,13 @@ def tile_attend_gmf_nce_v_kernel(tc, uT, vT, y, us, ts, offs, uoffs, out):
             words = turned[td // 2][:].bitcast(F32).rearrange("m (d g p u) -> m d g p u", g=PASSES, d=2, u=2)
             nc.scalar.copy(words[:, td % 2], bank[:].rearrange("m g u p -> m g p u"))
 
-        gather_heads(True, 0, 0, R)
-        spread_by_slot(0)
-        turn_heads(0)
-        gather_heads(False, 1, 0, R)
-        gather_heads(False, 2, 0, R)
-        gather_heads(False, 3, 0, K)
-        gather_heads(True, 3, K, K)
-        for td in range(1, PACK):
+        for td in range(PACK - 1):
+            nc.vector.tensor_copy(heads[:, td * R : (td + 1) * R], listed(u_raw[td], head_list, 0, R))
+        nc.vector.tensor_copy(heads[:, 3 * R : 3 * R + K], listed(u_raw[3], head_list, 0, K))
+        for td in range(2):
+            turn_heads(td)
+        nc.scalar.activation(heads[:, 3 * R + K :], listed(u_raw[3], head_list, K, K), ACT.Copy)
+        for td in range(2, PACK):
             turn_heads(td)
         for g in range(PASSES):
             nc.vector.tensor_copy(
@@ -163,179 +151,145 @@ def tile_attend_gmf_nce_v_kernel(tc, uT, vT, y, us, ts, offs, uoffs, out):
         nc.vector.quantize_mx(x_codes[:].bitcast(E4M3), x_scales[:], woven[:])
         xt_scales = kept([P, PACK * plane], U8, "xt_scales")
         xt_codes = []
-
-        def quantise_turned(n, offset):
-            codes = placed([P, 2 * plane], U32, "xt_codes%d" % n, offset)
+        for n in range(2):
+            codes = kept([P, 2 * plane], U32, "xt_codes%d" % n)
             nc.vector.quantize_mx(codes[:].bitcast(E4M3), xt_scales[:, 2 * n * plane : 2 * (n + 1) * plane], turned[n][:])
             xt_codes.extend(codes[:, e * plane : (e + 1) * plane] for e in range(2))
+        for t in range(PACK):
+            nc.vector.tensor_scalar(scale_by_row[1][:, t, :], ts_signed[:], row_scale[:, 1, t : t + 1], None, ALU.mult)
 
-        quantise_turned(0, 20480)
+        parts = ((0, P), (P, P), (HALF, HALF))
+        tails = [placed([P, count, PACK], BF16, "tails%d" % first, 3 * PLANE + 8 * first) for first, count in parts]
+        for td in range(PACK):
+            for tile, (first, count) in zip(tails, parts):
+                nc.scalar.activation(tile[:, :, td], listed(v_raw[td], tail_list, first, count), ACT.Copy)
+        w_codes, w_scales = [], []
 
-        tails = [placed([P, HALF, PACK], BF16, "tails0", 16384), kept([P, HALF, PACK], BF16, "tails1")]
+        def quantise_tails(n):
+            first, count = parts[n]
+            codes = kept([P, count], U32, "w_codes%d" % n)
+            scales = kept([P, count], U8, "w_scales%d" % n)
+            nc.vector.quantize_mx(codes[:].bitcast(E4M3), scales[:], tails[n][:].rearrange("p i d -> p (i d)"))
+            for at in range(0, count, P):
+                w_codes.append(codes[:, at : at + P])
+                w_scales.append(scales[:, at : at + P])
 
-        def weave_pair(copy, k, n, pair):
-            copy(
-                tails[k][:, :, 2 * n : 2 * n + 2].rearrange("p (c i) d -> p c d i", i=4),
-                pair.rearrange("p d (c i) -> p c d i", i=4),
-            )
+        for n in range(len(parts)):
+            quantise_tails(n)
 
-        early_pair = kept([P, 2, N], BF16, "early_pair", "u_raw2")
-        for td in range(2):
-            gather(True, early_pair[:, td, :], listed(v_raw[td], tail_list, 0, N))
-        spread_by_slot(1)
-        nc.vector.tensor_copy(tails[0][:, :, 2], listed(v_raw[2], tail_list, 0, HALF))
-        weave_pair(nc.vector.tensor_copy, 0, 0, early_pair[:, :, 0:HALF])
-        weave_pair(nc.vector.tensor_copy, 1, 0, early_pair[:, :, HALF:])
-        late_pair = kept([P, 2, HALF], BF16, "late_pair", "v_raw0")
-        nc.vector.tensor_copy(tails[0][:, :, 3], listed(v_raw[3], tail_list, 0, HALF))
-        for td in (2, 3):
-            gather(True, late_pair[:, td - 2, :], listed(v_raw[td], tail_list, HALF, HALF))
-        weave_pair(nc.scalar.copy, 1, 1, late_pair[:])
-        w_codes = [kept([P, HALF], U32, "w_codes0"), placed([P, HALF], U32, "w_codes1", 0)]
-        w_scales = [kept([P, HALF], U8, "w_scales%d" % k) for k in range(2)]
-        for k in range(2):
-            nc.vector.quantize_mx(w_codes[k][:].bitcast(E4M3), w_scales[k][:], tails[k][:].rearrange("p i d -> p (i d)"))
-            if k == 0:
-                quantise_turned(1, 16384)
-
-        z = [kept([P, PACK, HALF], F32, "z%d" % n) for n in range(len(steps))]
-
-        def score(acc, g, t, k):
-            rows = slice(g * K + t * P, g * K + (t + 1) * P)
-            nc.tensor.matmul_mx(
-                out=acc, lhsT=x_codes[:, rows].bitcast(E4M3), lhsT_scale=x_scales[:, rows],
-                rhs=w_codes[k][:].bitcast(E4M3), rhs_scale=w_scales[k][:], start=True, stop=True,
-            )
-
-        sums = {}
-
-        def open_sum(n, j, number):
-            sums[n, j] = in_bank(number, [P, PACK, P], "sum%d_%d" % (n, j))
+        units = [(0, 0), (1, 0), (2, 0), (3, 0), (2, 1), (3, 1), (0, 1), (1, 1)]
+        z = {}
+        for n, (b, g) in enumerate(units):
+            acc = in_bank(n, [P, PACK, P], "score%d" % n)
             for t in range(PACK):
-                nc.tensor.matmul(sums[n, j][:, t, :], labels[n][:, t, j * P : (j + 1) * P], ident[:], start=(t == 0), stop=False, is_transpose=True)
+                rows = slice(g * K + t * P, g * K + (t + 1) * P)
+                nc.tensor.matmul_mx(
+                    out=acc[:, t, :], lhsT=x_codes[:, rows].bitcast(E4M3), lhsT_scale=x_scales[:, rows],
+                    rhs=w_codes[b].bitcast(E4M3), rhs_scale=w_scales[b], start=True, stop=True,
+                )
+            slots = slice(b * P, (b + 1) * P)
+            z[b, g] = placed([P, PACK, P], F32, "z%d" % n, n * BANK)
+            nc.vector.tensor_tensor(z[b, g][:], acc[:], scale_by_row[g][:, :, slots], ALU.mult)
+            nc.scalar.activation(z[b, g][:], z[b, g][:], ACT.Sigmoid)
+            if b < 2:
+                nc.gpsimd.tensor_tensor(z[b, g][:], z[b, g][:], labels[g][:, :, slots], ALU.subtract)
 
-        def close_sums(n, places):
-            for t in places:
-                for j in range(2):
-                    nc.tensor.matmul(sums[n, j][:, t, :], z[n][:, t, j * P : (j + 1) * P], ident[:], start=False, stop=(t == PACK - 1), is_transpose=True)
+        summed = [(b, g) for b, g in units if b >= 2]
+        sums = {}
+        for n, (b, g) in enumerate(summed):
+            sums[b, g] = in_bank(n, [P, PACK, P], "sum%d" % n)
+            for t in range(PACK):
+                nc.tensor.matmul(sums[b, g][:, t, :], labels[g][:, t, b * P : (b + 1) * P], ident[:], start=(t == 0), stop=False, is_transpose=True)
+            for t in range(PACK):
+                nc.tensor.matmul(sums[b, g][:, t, :], z[b, g][:, t, :], ident[:], start=False, stop=(t == PACK - 1), is_transpose=True)
 
-        sum_banks = ((5, 0), (1, 2))
-        back_banks = ((3, 6), (7, 4))
-
-        def score_pair(g, k, a, number):
-            n = steps.index((g, k))
-            acc = in_bank(number, [P, 2, HALF], "score%d_%d" % (n, a))
-            rows = slice(2 * a, 2 * a + 2)
-            for e in range(2):
-                score(acc[:, e, :], g, 2 * a + e, k)
-            if k and not a:
-                for j in range(2):
-                    open_sum(n, j, sum_banks[g][j])
-            tile = z[n][:, rows, :]
-            if (g, k) == (1, 1):
-                nc.vector.tensor_tensor(tile, acc[:], ts_signed[:, HALF:].unsqueeze(1).to_broadcast([P, 2, HALF]), ALU.mult)
-                for t in (2 * a, 2 * a + 1):
-                    nc.scalar.activation(z[n][:, t, :], z[n][:, t, :], ACT.Sigmoid, scale=row_scale[:, g, t : t + 1])
-                    close_sums(n, (t,))
-                return
-            nc.vector.tensor_tensor(tile, acc[:], scale_by_row[g][:, rows, k * HALF : (k + 1) * HALF], ALU.mult)
-            nc.scalar.activation(tile, tile, ACT.Sigmoid)
-            if k:
-                close_sums(n, (2 * a, 2 * a + 1))
-            else:
-                nc.gpsimd.tensor_tensor(tile, tile, labels[n][:, rows, :], ALU.subtract)
-
-        for t in range(2):
-            acc = in_bank(4 + t, [P, HALF], "first%d" % t)
-            score(acc[:], 0, t, 0)
-            nc.vector.tensor_tensor(z[0][:, t, :], acc[:], ts_low[:], ALU.mult)
-            nc.scalar.activation(z[0][:, t, :], z[0][:, t, :], ACT.Sigmoid, scale=row_scale[:, 0, t : t + 1])
-        nc.gpsimd.tensor_tensor(z[0][:, 0:2, :], z[0][:, 0:2, :], labels[0][:, 0:2, :], ALU.subtract)
-        for g, k, a, number in ((0, 0, 1, 0), (1, 0, 0, 1), (1, 0, 1, 2), (0, 1, 0, 3), (0, 1, 1, 6), (1, 1, 0, 7), (1, 1, 1, 4)):
-            score_pair(g, k, a, number)
-
-        h = {}
-
-        def weigh_by_slot(n, j):
-            bank = in_bank(back_banks[n - PASSES][j], [P, 2, P], "h_turned%d_%d" % (n, j))
+        early_h = [kept([P, HALF * PACK], BF16, "early_h0"), placed([P, HALF * PACK], BF16, "early_h1", 6 * PLANE)]
+        for n, (b, g) in enumerate(summed):
+            j = b - 2
+            bank = in_bank(4 + n, [P, 2, P], "h_turned%d" % n)
             for u in range(2):
-                by_slot = kept([P, P, 2], BF16, "h_by_slot%d_%d_%d" % (n, j, u))
+                by_slot = kept([P, P, 2], BF16, "h_by_slot%d_%d" % (n, u))
                 nc.vector.scalar_tensor_tensor(
-                    by_slot[:], sums[n, j][:, 2 * u : 2 * u + 2, :].rearrange("p e s -> p s e"), 1.0,
-                    scale_by_slot[n - PASSES][:, j, u], ALU.subtract, ALU.mult,
+                    by_slot[:], sums[b, g][:, 2 * u : 2 * u + 2, :].rearrange("p e s -> p s e"), 1.0,
+                    scale_by_slot[g][:, j, u], ALU.subtract, ALU.mult,
                 )
                 nc.tensor.transpose(bank[:, u, :], by_slot[:].rearrange("p s e -> p (s e)").bitcast(F32), ident[:])
-            nc.scalar.copy(h[n][:, j * K : (j + 1) * K].bitcast(F32).rearrange("p (i u) -> p i u", u=2), bank[:].rearrange("p u i -> p i u"))
+            nc.scalar.copy(early_h[g][:, j * K : (j + 1) * K].bitcast(F32).rearrange("p (i u) -> p i u", u=2), bank[:].rearrange("p u i -> p i u"))
 
-        def weigh_by_row(n, first, count):
+        late_h = {(0, 0): kept([P, K], BF16, "late_h00")}
+        for at, unit in enumerate(((0, 1), (1, 0), (1, 1))):
+            late_h[unit] = placed([P, K], BF16, "late_h%d%d" % unit, 6 * PLANE - 960 + 1024 * at)
+
+        def weigh_by_row(b, g):
             nc.vector.tensor_tensor(
-                h[n][:, first * PACK : (first + count) * PACK].rearrange("p (c i t) -> p c t i", i=4, t=PACK),
-                z[n][:, :, first : first + count].rearrange("p t (c i) -> p c t i", i=4),
-                scale_by_row[n][:, :, first : first + count].rearrange("p t (c i) -> p c t i", i=4),
+                late_h[b, g][:].rearrange("p (c i t) -> p c t i", i=4, t=PACK),
+                z[b, g][:].rearrange("p t (c i) -> p c t i", i=4),
+                scale_by_row[g][:, :, b * P : (b + 1) * P].rearrange("p t (c i) -> p c t i", i=4),
                 ALU.mult,
             )
 
-        h_codes = [kept([P, N], U32, "h_codes%d" % g) for g in range(PASSES)]
-        h_scales = [kept([P, N], U8, "h_scales%d" % g) for g in range(PASSES)]
+        def quantised(values, name):
+            width = values.shape[1] // PACK
+            codes = kept([P, width], U32, name + "_codes")
+            scales = kept([P, width], U8, name + "_scales")
+            nc.vector.quantize_mx(codes[:].bitcast(E5M2), scales[:], values[:])
+            return codes, scales
 
-        def quantise(n):
-            g, k = steps[n]
-            slots = slice(k * HALF, (k + 1) * HALF)
-            nc.vector.quantize_mx(h_codes[g][:, slots].bitcast(E5M2), h_scales[g][:, slots], h[n][:])
-
-        def product(acc, td, k):
-            slots = slice(k * HALF, (k + 1) * HALF)
-            order = (1, 0) if td and not k else (0, 1)
-            for g in order:
+        def product(acc, td, moving):
+            for g in range(PASSES):
+                codes, scales = moving[g]
                 nc.tensor.matmul_mx(
                     out=acc, lhsT=xt_codes[td][:, g * P : (g + 1) * P].bitcast(E4M3),
                     lhsT_scale=xt_scales[:, td * plane + g * P : td * plane + (g + 1) * P],
-                    rhs=h_codes[g][:, slots].bitcast(E5M2), rhs_scale=h_scales[g][:, slots], start=(g == order[0]), stop=(g == order[1]),
+                    rhs=codes.bitcast(E5M2), rhs_scale=scales, start=(g == 0), stop=(g == PASSES - 1),
                 )
 
-        for n in (2, 3):
-            h[n] = kept([P, HALF * PACK], BF16, "h2") if n == 2 else placed([P, HALF * PACK], BF16, "h3", LAST_H)
-            for j in range(2):
-                weigh_by_slot(n, j)
-        h[0] = kept([P, HALF * PACK], BF16, "h0", "v_raw1")
-        quantise(2)
-        weigh_by_row(0, 0, P)
-        quantise(3)
-        weigh_by_row(0, P, P)
-        h[1] = placed([P, HALF * PACK], BF16, "h1", LAST_H)
-        weigh_by_row(1, 0, HALF)
-        quantise(0)
-        quantise(1)
+        early = [quantised(early_h[0], "early0")]
+        weigh_by_row(0, 0)
+        early.append(quantised(early_h[1], "early1"))
+        late = {(0, 0): quantised(late_h[0, 0], "late00")}
+        weigh_by_row(0, 1)
+        weigh_by_row(1, 0)
+        late[0, 1] = quantised(late_h[0, 1], "late01")
+        weigh_by_row(1, 1)
+        for g in range(PASSES):
+            late[1, g] = quantised(late_h[1, g], "late1%d" % g)
 
-        for td, offset in ((2, LAST_H + 1024 - 4 * T), (3, LAST_H + 1024)):
-            windows.append(placed([P, T], F32, "window%d" % td, offset))
-            nc.gpsimd.memset(windows[td][:].bitcast(I32), 0)
+        windows.append(placed([P, T], F32, "window3", 6 * PLANE + 1088))
+        nc.gpsimd.memset(windows[3][:].bitcast(I32), 0)
         out_planes = out.rearrange("(p t) c -> t p c", t=PACK)
+        early_grads = placed([P, PACK, HALF], F32, "early_grads", 2 * PLANE)
+        first_grads = placed([P, 2, P], F32, "first_grads", 2 * PLANE + 4096)
 
-        def scatter(on_scalar, td, grad, first, count):
-            window = listed(windows[td], tail_list, first, count)
-            if on_scalar:
-                nc.scalar.activation(window, grad, ACT.Copy)
-            else:
-                nc.vector.tensor_copy(window, grad)
+        def whole(pairs):
+            return [(codes[:], scales[:]) for codes, scales in pairs]
 
-        def copied(on_scalar, acc, name, tag=None):
-            grad = kept(list(acc.shape), F32, name, tag)
-            (nc.scalar.copy if on_scalar else nc.vector.tensor_copy)(grad[:], acc)
-            return grad[:]
+        early_banks = [in_bank(0, [P, 1, HALF], "early0"), in_bank(1, [P, 1, HALF], "early1"), in_bank(2, [P, 2, HALF], "early23")]
+        closing = [in_bank(3 + b, [P, P], "late_first%d" % b) for b in range(2)]
+        others = [in_bank(5, [P, 2, P], "late_plane1"), in_bank(6, [P, 2, HALF], "late_planes23")]
+        product(early_banks[0][:, 0, :], 0, whole(early))
+        for b in range(2):
+            product(closing[b][:], 0, whole([late[b, g] for g in range(PASSES)]))
+        for td in range(1, PACK):
+            product(early_banks[min(td, 2)][:, max(td - 2, 0), :], td, whole(early))
+        for td in range(1, PACK):
+            for b in range(2):
+                product(others[0][:, b, :] if td == 1 else others[1][:, td - 2, b * P : (b + 1) * P], td, whole([late[b, g] for g in range(PASSES)]))
 
-        early = [in_bank(5, [P, HALF], "early0")[:], in_bank(0, [P, HALF], "early1")[:]]
-        both = in_bank(1, [P, 2, HALF], "early23")
-        early.extend(both[:, e, :] for e in range(2))
-        late = [in_bank(number, [P, HALF], "late%d" % td)[:] for td, number in enumerate((3, 6, 7, 4))]
-        for k, banks in ((1, early), (0, late)):
-            for td in range(PACK):
-                product(banks[td], td, k)
-        grads = [copied(True, early[td], "grad_early%d" % td) for td in range(2)]
-        last_two = copied(False, both[:], "grad_early23", "v_raw1")
-        grads.extend(last_two[:, e, :] for e in range(2))
         for td in range(PACK):
-            scatter(True, td, grads[td], HALF, HALF)
-        for td in range(PACK):
-            scatter(False, td, copied(False, late[td], "grad_late%d" % td), 0, HALF)
+            if td < 3:
+                nc.scalar.copy(early_grads[:, td : td + 1 + td // 2, :], early_banks[td][:])
+            nc.scalar.activation(listed(windows[td], tail_list, HALF, HALF), early_grads[:, td, :], ACT.Copy)
+        for b in range(2):
+            nc.vector.tensor_copy(first_grads[:, b, :], closing[b][:])
+            nc.vector.tensor_tensor(listed(windows[0], tail_list, b * P, P), first_grads[:, b, :], zeros[:], ALU.add)
+        nc.sync.dma_start(out_planes[0], windows[0][:])
+        second_grads = kept([P, HALF], F32, "second_grads")
+        nc.vector.tensor_copy(second_grads[:], others[0][:].rearrange("p b i -> p (b i)"))
+        nc.vector.tensor_copy(listed(windows[1], tail_list, 0, HALF), second_grads[:])
+        nc.sync.dma_start(out_planes[1], windows[1][:])
+        late_grads = placed([P, 2, HALF], F32, "late_grads", 8 * PLANE)
+        nc.vector.tensor_copy(late_grads[:], others[1][:])
+        for td in range(2, PACK):
+            nc.vector.tensor_copy(listed(windows[td], tail_list, 0, HALF), late_grads[:, td - 2, :])
             nc.sync.dma_start(out_planes[td], windows[td][:])

@@ -110,7 +110,7 @@ def tile_attend_gmf_nce_v_kernel(tc, uT, vT, y, us, ts, offs, uoffs, out):
             us_rows = in_bank(2 + g, [P, PACK, P], "us_rows%d" % g)
             for t in range(PACK):
                 nc.tensor.transpose(us_rows[:, t, :], row_scale[:, g, t : t + 1].to_broadcast([P, P]), ident[:])
-            tile = kept([P, 2, 2, P, 2], F32, "scale_by_slot%d" % g)
+            tile = placed([P, 2, 2, P, 2], F32, "scale_by_slot%d" % g, 9 * PLANE + 4096 * g)
             for j in range(2):
                 nc.scalar.activation(tile[:, j], us_rows[:].rearrange("p (u e) s -> p u s e", e=2), ACT.Copy, scale=ts_minus[:, j : j + 1])
             scale_by_slot.append(tile)
@@ -177,10 +177,10 @@ def tile_attend_gmf_nce_v_kernel(tc, uT, vT, y, us, ts, offs, uoffs, out):
         for n in range(len(parts)):
             quantise_tails(n)
 
-        units = [(0, 0), (1, 0), (2, 0), (3, 0), (2, 1), (3, 1), (0, 1), (1, 1)]
+        units = [(0, 0), (1, 0), (0, 1), (2, 0), (3, 0), (2, 1), (3, 1), (1, 1)]
         z = {}
         for n, (b, g) in enumerate(units):
-            acc = in_bank(n, [P, PACK, P], "score%d" % n)
+            acc = in_bank(n if n < 6 else n - 2, [P, PACK, P], "score%d" % n)
             for t in range(PACK):
                 rows = slice(g * K + t * P, g * K + (t + 1) * P)
                 nc.tensor.matmul_mx(
@@ -206,7 +206,7 @@ def tile_attend_gmf_nce_v_kernel(tc, uT, vT, y, us, ts, offs, uoffs, out):
         early_h = [kept([P, HALF * PACK], BF16, "early_h0"), placed([P, HALF * PACK], BF16, "early_h1", 6 * PLANE)]
         for n, (b, g) in enumerate(summed):
             j = b - 2
-            bank = in_bank(4 + n, [P, 2, P], "h_turned%d" % n)
+            bank = in_bank((6, 7, 4, 5)[n], [P, 2, P], "h_turned%d" % n)
             for u in range(2):
                 by_slot = kept([P, P, 2], BF16, "h_by_slot%d_%d" % (n, u))
                 nc.vector.scalar_tensor_tensor(
@@ -216,7 +216,7 @@ def tile_attend_gmf_nce_v_kernel(tc, uT, vT, y, us, ts, offs, uoffs, out):
                 nc.tensor.transpose(bank[:, u, :], by_slot[:].rearrange("p s e -> p (s e)").bitcast(F32), ident[:])
             nc.scalar.copy(early_h[g][:, j * K : (j + 1) * K].bitcast(F32).rearrange("p (i u) -> p i u", u=2), bank[:].rearrange("p u i -> p i u"))
 
-        late_h = {(0, 0): kept([P, K], BF16, "late_h00")}
+        late_h = {(0, 0): placed([P, K], BF16, "late_h00", 9 * PLANE + 4096)}
         for at, unit in enumerate(((0, 1), (1, 0), (1, 1))):
             late_h[unit] = placed([P, K], BF16, "late_h%d%d" % unit, 6 * PLANE - 960 + 1024 * at)
 
@@ -228,9 +228,9 @@ def tile_attend_gmf_nce_v_kernel(tc, uT, vT, y, us, ts, offs, uoffs, out):
                 ALU.mult,
             )
 
-        def quantised(values, name):
+        def quantised(values, name, offset=None):
             width = values.shape[1] // PACK
-            codes = kept([P, width], U32, name + "_codes")
+            codes = placed([P, width], U32, name + "_codes", offset) if offset else kept([P, width], U32, name + "_codes")
             scales = kept([P, width], U8, name + "_scales")
             nc.vector.quantize_mx(codes[:].bitcast(E5M2), scales[:], values[:])
             return codes, scales
@@ -244,7 +244,7 @@ def tile_attend_gmf_nce_v_kernel(tc, uT, vT, y, us, ts, offs, uoffs, out):
                     rhs=codes.bitcast(E5M2), rhs_scale=scales, start=(g == 0), stop=(g == PASSES - 1),
                 )
 
-        early = [quantised(early_h[0], "early0")]
+        early = [quantised(early_h[0], "early0", 9 * PLANE + 6144)]
         weigh_by_row(0, 0)
         early.append(quantised(early_h[1], "early1"))
         late = {(0, 0): quantised(late_h[0, 0], "late00")}

@@ -36,11 +36,11 @@ def tile_attend_gmf_nce_v_kernel(tc, uT, vT, y, us, ts, offs, uoffs, out):
         def in_bank(number, shape, name):
             return psum.tile(shape, F32, name=name, tag=name, offset=number * BANK)
 
-        def kept(shape, dtype, name):
-            return keep.tile(shape, dtype, name=name, tag=name, align_bytes=64)
+        def kept(shape, dtype, name, align=64):
+            return keep.tile(shape, dtype, name=name, tag=name, align_bytes=align)
 
-        def placed(shape, dtype, name, offset):
-            return shared.tile(shape, dtype, name=name, tag=name, align_bytes=64, offset=offset)
+        def placed(shape, dtype, name, offset, align=64):
+            return shared.tile(shape, dtype, name=name, tag=name, align_bytes=align, offset=offset)
 
         tail_list = kept([P, N // 16], U16, "tail_list")
         head_list = kept([P, R // 16], U16, "head_list")
@@ -59,7 +59,7 @@ def tile_attend_gmf_nce_v_kernel(tc, uT, vT, y, us, ts, offs, uoffs, out):
         zeros = placed([P, P], F32, "zeros", 8 * PLANE)
         nc.vector.memset(zeros[:], 0.0)
         nc.vector.memset(us_line[0 : P - 1, :].bitcast(I32), 0)
-        windows = [kept([P, T], F32, "window%d" % td) for td in range(3)]
+        windows = [kept([P, T], F32, "window%d" % td, 256) for td in range(3)]
         for window in windows:
             nc.gpsimd.memset(window[:].bitcast(I32), 0)
 
@@ -73,12 +73,12 @@ def tile_attend_gmf_nce_v_kernel(tc, uT, vT, y, us, ts, offs, uoffs, out):
 
         u_raw = []
         for td in range(PACK):
-            u_raw.append(load_plane(placed([P, T], F32, "u_raw%d" % td, td * PLANE), uT, td))
+            u_raw.append(load_plane(placed([P, T], F32, "u_raw%d" % td, td * PLANE, 256), uT, td))
             if td == 0:
                 nc.sync.dma_start(head_list[:], uoffs)
-        v_raw = [load_plane(kept([P, T], F32, "v_raw%d" % td), vT, td) for td in range(PACK)]
+        v_raw = [load_plane(kept([P, T], F32, "v_raw%d" % td, 256), vT, td) for td in range(PACK)]
         y_rows = y[0].rearrange("(g p t) i -> g p t i", g=PASSES, t=PACK)
-        labels = [kept([P, PACK, N], F32, "labels%d" % g) for g in range(PASSES)]
+        labels = [kept([P, PACK, N], F32, "labels%d" % g, 256) for g in range(PASSES)]
         for g in range(PASSES):
             nc.sync.dma_start(labels[g][:], y_rows[g])
 
@@ -115,12 +115,12 @@ def tile_attend_gmf_nce_v_kernel(tc, uT, vT, y, us, ts, offs, uoffs, out):
                 nc.scalar.activation(tile[:, j], us_rows[:].rearrange("p (u e) s -> p u s e", e=2), ACT.Copy, scale=ts_minus[:, j : j + 1])
             scale_by_slot.append(tile)
 
-        scale_by_row = [kept([P, PACK, N], F32, "scale_by_row%d" % g) for g in range(PASSES)]
+        scale_by_row = [kept([P, PACK, N], F32, "scale_by_row0")]
         for t in range(PACK):
             nc.gpsimd.tensor_scalar(scale_by_row[0][:, t, :], ts_signed[:], row_scale[:, 0, t : t + 1], 0.0, ALU.mult, ALU.add)
 
         plane = PASSES * P
-        turned = [kept([P, 2 * plane * PACK], BF16, "turned%d" % n) for n in range(2)]
+        turned = [placed([P, 2 * plane * PACK], BF16, "turned%d" % n, (11 * PLANE + 4096, 10 * PLANE)[n]) for n in range(2)]
         woven = kept([P, R * PACK], BF16, "woven")
 
         def turn_heads(td):
@@ -155,6 +155,7 @@ def tile_attend_gmf_nce_v_kernel(tc, uT, vT, y, us, ts, offs, uoffs, out):
             codes = kept([P, 2 * plane], U32, "xt_codes%d" % n)
             nc.vector.quantize_mx(codes[:].bitcast(E4M3), xt_scales[:, 2 * n * plane : 2 * (n + 1) * plane], turned[n][:])
             xt_codes.extend(codes[:, e * plane : (e + 1) * plane] for e in range(2))
+        scale_by_row.append(placed([P, PACK, N], F32, "scale_by_row1", 11 * PLANE))
         for t in range(PACK):
             nc.vector.tensor_scalar(scale_by_row[1][:, t, :], ts_signed[:], row_scale[:, 1, t : t + 1], None, ALU.mult)
 
@@ -180,16 +181,18 @@ def tile_attend_gmf_nce_v_kernel(tc, uT, vT, y, us, ts, offs, uoffs, out):
         units = [(0, 0), (1, 0), (0, 1), (2, 0), (3, 0), (2, 1), (3, 1), (1, 1)]
         z = {}
         for n, (b, g) in enumerate(units):
-            acc = in_bank(n if n < 6 else n - 2, [P, PACK, P], "score%d" % n)
-            for t in range(PACK):
-                rows = slice(g * K + t * P, g * K + (t + 1) * P)
-                nc.tensor.matmul_mx(
-                    out=acc[:, t, :], lhsT=x_codes[:, rows].bitcast(E4M3), lhsT_scale=x_scales[:, rows],
-                    rhs=w_codes[b].bitcast(E4M3), rhs_scale=w_scales[b], start=True, stop=True,
-                )
             slots = slice(b * P, (b + 1) * P)
             z[b, g] = placed([P, PACK, P], F32, "z%d" % n, n * BANK)
-            nc.vector.tensor_tensor(z[b, g][:], acc[:], scale_by_row[g][:, :, slots], ALU.mult)
+            for number, first, count in ((n if n < 6 else n - 2, 0, PACK),) if n else ((7, 0, 2), (0, 2, 2)):
+                acc = in_bank(number, [P, count, P], "score%d_%d" % (n, first))
+                for t in range(first, first + count):
+                    rows = slice(g * K + t * P, g * K + (t + 1) * P)
+                    nc.tensor.matmul_mx(
+                        out=acc[:, t - first, :], lhsT=x_codes[:, rows].bitcast(E4M3), lhsT_scale=x_scales[:, rows],
+                        rhs=w_codes[b].bitcast(E4M3), rhs_scale=w_scales[b], start=True, stop=True,
+                    )
+                places = slice(first, first + count)
+                nc.vector.tensor_tensor(z[b, g][:, places, :], acc[:], scale_by_row[g][:, places, slots], ALU.mult)
             nc.scalar.activation(z[b, g][:], z[b, g][:], ACT.Sigmoid)
             if b < 2:
                 nc.gpsimd.tensor_tensor(z[b, g][:], z[b, g][:], labels[g][:, :, slots], ALU.subtract)
@@ -255,8 +258,6 @@ def tile_attend_gmf_nce_v_kernel(tc, uT, vT, y, us, ts, offs, uoffs, out):
         for g in range(PASSES):
             late[1, g] = quantised(late_h[1, g], "late1%d" % g)
 
-        windows.append(placed([P, T], F32, "window3", 6 * PLANE + 1088))
-        nc.gpsimd.memset(windows[3][:].bitcast(I32), 0)
         out_planes = out.rearrange("(p t) c -> t p c", t=PACK)
         early_grads = placed([P, PACK, HALF], F32, "early_grads", 2 * PLANE)
         first_grads = placed([P, 2, P], F32, "first_grads", 2 * PLANE + 4096)
@@ -264,31 +265,43 @@ def tile_attend_gmf_nce_v_kernel(tc, uT, vT, y, us, ts, offs, uoffs, out):
         def whole(pairs):
             return [(codes[:], scales[:]) for codes, scales in pairs]
 
-        early_banks = [in_bank(0, [P, 1, HALF], "early0"), in_bank(1, [P, 1, HALF], "early1"), in_bank(2, [P, 2, HALF], "early23")]
-        closing = [in_bank(3 + b, [P, P], "late_first%d" % b) for b in range(2)]
-        others = [in_bank(5, [P, 2, P], "late_plane1"), in_bank(6, [P, 2, HALF], "late_planes23")]
-        product(early_banks[0][:, 0, :], 0, whole(early))
-        for b in range(2):
-            product(closing[b][:], 0, whole([late[b, g] for g in range(PASSES)]))
-        for td in range(1, PACK):
-            product(early_banks[min(td, 2)][:, max(td - 2, 0), :], td, whole(early))
-        for td in range(1, PACK):
-            for b in range(2):
-                product(others[0][:, b, :] if td == 1 else others[1][:, td - 2, b * P : (b + 1) * P], td, whole([late[b, g] for g in range(PASSES)]))
+        def multiply(acc, td, b):
+            product(acc, td, whole([late[b, g] for g in range(PASSES)]))
 
-        for td in range(PACK):
-            if td < 3:
-                nc.scalar.copy(early_grads[:, td : td + 1 + td // 2, :], early_banks[td][:])
+        def scatter_early(td):
             nc.scalar.activation(listed(windows[td], tail_list, HALF, HALF), early_grads[:, td, :], ACT.Copy)
+
+        for td in range(2):
+            bank = in_bank(td, [P, HALF], "early%d" % td)
+            product(bank[:], td, whole(early))
+            nc.scalar.copy(early_grads[:, td, :], bank[:])
+            scatter_early(td)
+        closing = [in_bank(3 + b, [P, P], "late_first%d" % b) for b in range(2)]
         for b in range(2):
+            multiply(closing[b][:], 0, b)
             nc.vector.tensor_copy(first_grads[:, b, :], closing[b][:])
             nc.vector.tensor_tensor(listed(windows[0], tail_list, b * P, P), first_grads[:, b, :], zeros[:], ALU.add)
         nc.sync.dma_start(out_planes[0], windows[0][:])
+        windows.append(placed([P, T], F32, "window3", 7 * PLANE + 256, 256))
+        nc.gpsimd.memset(windows[3][:].bitcast(I32), 0)
+        others = [in_bank(3, [P, 2, P], "late_plane1")]
+        for b in range(2):
+            multiply(others[0][:, b, :], 1, b)
+        bank = in_bank(1, [P, 2, HALF], "early23")
+        for td in (2, 3):
+            product(bank[:, td - 2, :], td, whole(early))
+        nc.scalar.copy(early_grads[:, 2:, :], bank[:])
+        for td in (2, 3):
+            scatter_early(td)
+        others.append(in_bank(4, [P, 2, HALF], "late_planes23"))
+        for td in (2, 3):
+            for b in range(2):
+                multiply(others[1][:, td - 2, b * P : (b + 1) * P], td, b)
         second_grads = kept([P, HALF], F32, "second_grads")
         nc.vector.tensor_copy(second_grads[:], others[0][:].rearrange("p b i -> p (b i)"))
         nc.vector.tensor_copy(listed(windows[1], tail_list, 0, HALF), second_grads[:])
         nc.sync.dma_start(out_planes[1], windows[1][:])
-        late_grads = placed([P, 2, HALF], F32, "late_grads", 8 * PLANE)
+        late_grads = placed([P, 2, HALF], F32, "late_grads", 8 * PLANE + 256)
         nc.vector.tensor_copy(late_grads[:], others[1][:])
         for td in range(2, PACK):
             nc.vector.tensor_copy(listed(windows[td], tail_list, 0, HALF), late_grads[:, td - 2, :])

@@ -83,9 +83,9 @@ def tile_attend_gmf_nce_v_kernel(tc, uT, vT, y, us, ts, offs, uoffs, out):
             nc.sync.dma_start(labels[g][:], y_rows[g])
 
         heads = kept([P, PACK * R], BF16, "heads")
-        late_heads = heads[:, PACK * R - K :].bitcast(F32)
+        late_heads = heads[:, 3 * R + K - 16 : 3 * R + K + 16].bitcast(F32)
         ts_cols = late_heads[:, 0:BLOCKS]
-        ts_minus = late_heads[:, 8:10]
+        ts_minus = late_heads[:, 7:9]
         ts_picked = kept([P, N], F32, "ts_picked")
         nc.vector.tensor_copy(ts_picked[:], listed(ts_window, tail_list, 0, N))
         bank = in_bank(0, [P, BLOCKS, P], "ts_turned")
@@ -135,10 +135,11 @@ def tile_attend_gmf_nce_v_kernel(tc, uT, vT, y, us, ts, offs, uoffs, out):
 
         for td in range(PACK - 1):
             nc.vector.tensor_copy(heads[:, td * R : (td + 1) * R], listed(u_raw[td], head_list, 0, R))
-        nc.vector.tensor_copy(heads[:, 3 * R : 3 * R + K], listed(u_raw[3], head_list, 0, K))
+        nc.vector.tensor_copy(heads[:, 3 * R : 3 * R + HALF], listed(u_raw[3], head_list, 0, HALF))
         for td in range(2):
             turn_heads(td)
-        nc.scalar.activation(heads[:, 3 * R + K :], listed(u_raw[3], head_list, K, K), ACT.Copy)
+        for first, count in ((HALF, HALF), (K, K)):
+            nc.scalar.activation(heads[:, 3 * R + first : 3 * R + first + count], listed(u_raw[3], head_list, first, count), ACT.Copy)
         for td in range(2, PACK):
             turn_heads(td)
         for g in range(PASSES):
@@ -160,8 +161,16 @@ def tile_attend_gmf_nce_v_kernel(tc, uT, vT, y, us, ts, offs, uoffs, out):
             nc.vector.tensor_scalar(scale_by_row[1][:, t, :], ts_signed[:], row_scale[:, 1, t : t + 1], None, ALU.mult)
 
         parts = ((0, P), (P, P), (HALF, HALF))
-        tails = [placed([P, count, PACK], BF16, "tails%d" % first, 3 * PLANE + 8 * first) for first, count in parts]
-        for td in range(PACK):
+        pair = placed([P, 2, N], BF16, "pair", 3 * PLANE)
+        for td in range(2):
+            nc.scalar.activation(pair[:, td, :], listed(v_raw[td], tail_list, 0, N), ACT.Copy)
+        tails = [placed([P, count, PACK], BF16, "tails%d" % first, 3 * PLANE + 2048 + 8 * first) for first, count in parts]
+        for tile, (first, count) in zip(tails, parts):
+            nc.vector.tensor_copy(
+                tile[:, :, 0:2].rearrange("p (c i) d -> p c d i", i=4),
+                pair[:, :, first : first + count].rearrange("p d (c i) -> p c d i", i=4),
+            )
+        for td in (2, 3):
             for tile, (first, count) in zip(tails, parts):
                 nc.scalar.activation(tile[:, :, td], listed(v_raw[td], tail_list, first, count), ACT.Copy)
         w_codes, w_scales = [], []
@@ -178,7 +187,7 @@ def tile_attend_gmf_nce_v_kernel(tc, uT, vT, y, us, ts, offs, uoffs, out):
         for n in range(len(parts)):
             quantise_tails(n)
 
-        units = [(0, 0), (1, 0), (0, 1), (2, 0), (3, 0), (2, 1), (3, 1), (1, 1)]
+        units = [(0, 0), (0, 1), (1, 0), (2, 0), (3, 0), (2, 1), (3, 1), (1, 1)]
         z = {}
         for n, (b, g) in enumerate(units):
             slots = slice(b * P, (b + 1) * P)
@@ -194,8 +203,9 @@ def tile_attend_gmf_nce_v_kernel(tc, uT, vT, y, us, ts, offs, uoffs, out):
                 places = slice(first, first + count)
                 nc.vector.tensor_tensor(z[b, g][:, places, :], acc[:], scale_by_row[g][:, places, slots], ALU.mult)
             nc.scalar.activation(z[b, g][:], z[b, g][:], ACT.Sigmoid)
-            if b < 2:
-                nc.gpsimd.tensor_tensor(z[b, g][:], z[b, g][:], labels[g][:, :, slots], ALU.subtract)
+        for g in range(PASSES):
+            for b in range(2):
+                nc.gpsimd.tensor_tensor(z[b, g][:], z[b, g][:], labels[g][:, :, b * P : (b + 1) * P], ALU.subtract)
 
         summed = [(b, g) for b, g in units if b >= 2]
         sums = {}

@@ -105,15 +105,15 @@ def tile_attend_gmf_nce_v_kernel(tc, uT, vT, y, us, ts, offs, uoffs, out):
             for t in range(PACK):
                 nc.tensor.transpose(bank[:, t, :], us_line[:, g * K + t : (g + 1) * K : PACK], ident[:])
             nc.scalar.copy(row_scale[:, g, :], bank[:, :, P - 1])
-        scale_by_slot = []
+        scale_by_slot = {}
         for g in range(PASSES):
             us_rows = in_bank(2 + g, [P, PACK, P], "us_rows%d" % g)
             for t in range(PACK):
                 nc.tensor.transpose(us_rows[:, t, :], row_scale[:, g, t : t + 1].to_broadcast([P, P]), ident[:])
-            tile = placed([P, 2, 2, P, 2], F32, "scale_by_slot%d" % g, 9 * PLANE + 4096 * g)
-            for j in range(2):
-                nc.scalar.activation(tile[:, j], us_rows[:].rearrange("p (u e) s -> p u s e", e=2), ACT.Copy, scale=ts_minus[:, j : j + 1])
-            scale_by_slot.append(tile)
+            for b in (2, 3):
+                tile = placed([P, 2, P, 2], F32, "scale_by_slot%d_%d" % (b, g), 9 * PLANE + BANK * len(scale_by_slot))
+                nc.scalar.activation(tile[:], us_rows[:].rearrange("p (u e) s -> p u s e", e=2), ACT.Copy, scale=ts_minus[:, b - 2 : b - 1])
+                scale_by_slot[b, g] = tile
 
         scale_by_row = [kept([P, PACK, N], F32, "scale_by_row0")]
         for t in range(PACK):
@@ -160,6 +160,9 @@ def tile_attend_gmf_nce_v_kernel(tc, uT, vT, y, us, ts, offs, uoffs, out):
         for t in range(PACK):
             nc.vector.tensor_scalar(scale_by_row[1][:, t, :], ts_signed[:], row_scale[:, 1, t : t + 1], None, ALU.mult)
 
+        first_scale = placed([P, 2, P], F32, "first_scale", 8 * PLANE + 2048)
+        nc.scalar.copy(first_scale[:], scale_by_row[0][:, 0:2, 0:P])
+
         parts = ((0, P), (P, P), (HALF, HALF))
         pair = placed([P, 2, N], BF16, "pair", 3 * PLANE)
         for td in range(2):
@@ -177,14 +180,14 @@ def tile_attend_gmf_nce_v_kernel(tc, uT, vT, y, us, ts, offs, uoffs, out):
 
         def quantise_tails(n):
             first, count = parts[n]
-            codes = kept([P, count], U32, "w_codes%d" % n)
+            codes = placed([P, count], U32, "w_codes2", 8 * PLANE + 2048) if n == 2 else kept([P, count], U32, "w_codes%d" % n)
             scales = kept([P, count], U8, "w_scales%d" % n)
             nc.vector.quantize_mx(codes[:].bitcast(E4M3), scales[:], tails[n][:].rearrange("p i d -> p (i d)"))
             for at in range(0, count, P):
                 w_codes.append(codes[:, at : at + P])
                 w_scales.append(scales[:, at : at + P])
 
-        for n in range(len(parts)):
+        for n in range(2):
             quantise_tails(n)
 
         units = [(0, 0), (0, 1), (1, 0), (2, 0), (3, 0), (2, 1), (3, 1), (1, 1)]
@@ -201,7 +204,10 @@ def tile_attend_gmf_nce_v_kernel(tc, uT, vT, y, us, ts, offs, uoffs, out):
                         rhs=w_codes[b].bitcast(E4M3), rhs_scale=w_scales[b], start=True, stop=True,
                     )
                 places = slice(first, first + count)
-                nc.vector.tensor_tensor(z[b, g][:, places, :], acc[:], scale_by_row[g][:, places, slots], ALU.mult)
+                scale = scale_by_row[g][:, places, slots] if n or first else first_scale[:]
+                nc.vector.tensor_tensor(z[b, g][:, places, :], acc[:], scale, ALU.mult)
+            if n == 0:
+                quantise_tails(2)
             nc.scalar.activation(z[b, g][:], z[b, g][:], ACT.Sigmoid)
         for g in range(PASSES):
             for b in range(2):
@@ -224,18 +230,21 @@ def tile_attend_gmf_nce_v_kernel(tc, uT, vT, y, us, ts, offs, uoffs, out):
                 by_slot = kept([P, P, 2], BF16, "h_by_slot%d_%d" % (n, u))
                 nc.vector.scalar_tensor_tensor(
                     by_slot[:], sums[b, g][:, 2 * u : 2 * u + 2, :].rearrange("p e s -> p s e"), 1.0,
-                    scale_by_slot[g][:, j, u], ALU.subtract, ALU.mult,
+                    scale_by_slot[b, g][:, u], ALU.subtract, ALU.mult,
                 )
                 nc.tensor.transpose(bank[:, u, :], by_slot[:].rearrange("p s e -> p (s e)").bitcast(F32), ident[:])
             nc.scalar.copy(early_h[g][:, j * K : (j + 1) * K].bitcast(F32).rearrange("p (i u) -> p i u", u=2), bank[:].rearrange("p u i -> p i u"))
 
-        late_h = {(0, 0): placed([P, K], BF16, "late_h00", 9 * PLANE + 4096)}
-        for at, unit in enumerate(((0, 1), (1, 0), (1, 1))):
-            late_h[unit] = placed([P, K], BF16, "late_h%d%d" % unit, 6 * PLANE - 960 + 1024 * at)
+        late_h = {(0, 0): placed([P, K], BF16, "late_h00", 9 * PLANE + 6144)}
+        late_h[0, 1] = placed([P, K], BF16, "late_h01", 6 * PLANE + 64)
+        last_h = placed([P, PASSES, K], BF16, "late_h1", 6 * PLANE + 1088)
+        late_h = {unit: tile[:] for unit, tile in late_h.items()}
+        for g in range(PASSES):
+            late_h[1, g] = last_h[:, g, :]
 
         def weigh_by_row(b, g):
             nc.vector.tensor_tensor(
-                late_h[b, g][:].rearrange("p (c i t) -> p c t i", i=4, t=PACK),
+                late_h[b, g].rearrange("p (c i t) -> p c t i", i=4, t=PACK),
                 z[b, g][:].rearrange("p t (c i) -> p c t i", i=4),
                 scale_by_row[g][:, :, b * P : (b + 1) * P].rearrange("p t (c i) -> p c t i", i=4),
                 ALU.mult,
@@ -245,7 +254,7 @@ def tile_attend_gmf_nce_v_kernel(tc, uT, vT, y, us, ts, offs, uoffs, out):
             width = values.shape[1] // PACK
             codes = placed([P, width], U32, name + "_codes", offset) if offset else kept([P, width], U32, name + "_codes")
             scales = kept([P, width], U8, name + "_scales")
-            nc.vector.quantize_mx(codes[:].bitcast(E5M2), scales[:], values[:])
+            nc.vector.quantize_mx(codes[:].bitcast(E5M2), scales[:], values)
             return codes, scales
 
         def product(acc, td, moving):
@@ -257,10 +266,10 @@ def tile_attend_gmf_nce_v_kernel(tc, uT, vT, y, us, ts, offs, uoffs, out):
                     rhs=codes.bitcast(E5M2), rhs_scale=scales, start=(g == 0), stop=(g == PASSES - 1),
                 )
 
-        early = [quantised(early_h[0], "early0", 9 * PLANE + 6144)]
+        early = [quantised(early_h[0][:], "early0", 9 * PLANE + 5120)]
         weigh_by_row(0, 0)
-        early.append(quantised(early_h[1], "early1"))
-        late = {(0, 0): quantised(late_h[0, 0], "late00")}
+        early.append(quantised(early_h[1][:], "early1"))
+        late = {(0, 0): quantised(late_h[0, 0], "late00", 6 * PLANE - 448)}
         weigh_by_row(0, 1)
         weigh_by_row(1, 0)
         late[0, 1] = quantised(late_h[0, 1], "late01")

@@ -195,7 +195,7 @@ def tile_attend_gmf_nce_v_kernel(tc, uT, vT, y, us, ts, offs, uoffs, out):
         for n, (b, g) in enumerate(units):
             slots = slice(b * P, (b + 1) * P)
             z[b, g] = placed([P, PACK, P], F32, "z%d" % n, n * BANK)
-            for number, first, count in ((n if n < 6 else n - 2, 0, PACK),) if n else ((7, 0, 2), (0, 2, 2)):
+            for number, first, count in (((n - 1) % 3 + 1, 0, PACK),) if n else ((7, 0, 2), (0, 2, 2)):
                 acc = in_bank(number, [P, count, P], "score%d_%d" % (n, first))
                 for t in range(first, first + count):
                     rows = slice(g * K + t * P, g * K + (t + 1) * P)
@@ -216,16 +216,16 @@ def tile_attend_gmf_nce_v_kernel(tc, uT, vT, y, us, ts, offs, uoffs, out):
         summed = [(b, g) for b, g in units if b >= 2]
         sums = {}
         for n, (b, g) in enumerate(summed):
-            sums[b, g] = in_bank(n, [P, PACK, P], "sum%d" % n)
+            sums[b, g] = in_bank((0, 7, 2, 3)[n], [P, PACK, P], "sum%d" % n)
             for t in range(PACK):
                 nc.tensor.matmul(sums[b, g][:, t, :], labels[g][:, t, b * P : (b + 1) * P], ident[:], start=(t == 0), stop=False, is_transpose=True)
             for t in range(PACK):
                 nc.tensor.matmul(sums[b, g][:, t, :], z[b, g][:, t, :], ident[:], start=False, stop=(t == PACK - 1), is_transpose=True)
 
-        early_h = [kept([P, HALF * PACK], BF16, "early_h0"), placed([P, HALF * PACK], BF16, "early_h1", 6 * PLANE)]
+        early_h = [kept([P, HALF * PACK], BF16, "early_h0"), kept([P, K], BF16, "early_h12"), placed([P, K], BF16, "early_h13", 6 * PLANE + 512)]
+        early_parts = [early_h[0][:, 0:K], early_h[0][:, K:], early_h[1][:], early_h[2][:]]
         for n, (b, g) in enumerate(summed):
-            j = b - 2
-            bank = in_bank((6, 7, 4, 5)[n], [P, 2, P], "h_turned%d" % n)
+            bank = in_bank((4, 5, 6, 1)[n], [P, 2, P], "h_turned%d" % n)
             for u in range(2):
                 by_slot = kept([P, P, 2], BF16, "h_by_slot%d_%d" % (n, u))
                 nc.vector.scalar_tensor_tensor(
@@ -233,11 +233,11 @@ def tile_attend_gmf_nce_v_kernel(tc, uT, vT, y, us, ts, offs, uoffs, out):
                     scale_by_slot[b, g][:, u], ALU.subtract, ALU.mult,
                 )
                 nc.tensor.transpose(bank[:, u, :], by_slot[:].rearrange("p s e -> p (s e)").bitcast(F32), ident[:])
-            nc.scalar.copy(early_h[g][:, j * K : (j + 1) * K].bitcast(F32).rearrange("p (i u) -> p i u", u=2), bank[:].rearrange("p u i -> p i u"))
+            nc.scalar.copy(early_parts[n].bitcast(F32).rearrange("p (i u) -> p i u", u=2), bank[:].rearrange("p u i -> p i u"))
 
         late_h = {(0, 0): placed([P, K], BF16, "late_h00", 9 * PLANE + 6144)}
-        late_h[0, 1] = placed([P, K], BF16, "late_h01", 6 * PLANE + 64)
-        last_h = placed([P, PASSES, K], BF16, "late_h1", 6 * PLANE + 1088)
+        late_h[0, 1] = placed([P, K], BF16, "late_h01", 6 * PLANE + 64 + 320)
+        last_h = placed([P, PASSES, K], BF16, "late_h1", 6 * PLANE + 1088 + 320)
         late_h = {unit: tile[:] for unit, tile in late_h.items()}
         for g in range(PASSES):
             late_h[1, g] = last_h[:, g, :]
@@ -267,9 +267,13 @@ def tile_attend_gmf_nce_v_kernel(tc, uT, vT, y, us, ts, offs, uoffs, out):
                 )
 
         early = [quantised(early_h[0][:], "early0", 9 * PLANE + 5120)]
+        codes = placed([P, HALF], U32, "early1_codes", 9 * PLANE + 4096)
+        scales = kept([P, HALF], U8, "early1_scales")
+        nc.vector.quantize_mx(codes[:, 0:P].bitcast(E5M2), scales[:, 0:P], early_h[1][:])
         weigh_by_row(0, 0)
-        early.append(quantised(early_h[1][:], "early1"))
-        late = {(0, 0): quantised(late_h[0, 0], "late00", 6 * PLANE - 448)}
+        nc.vector.quantize_mx(codes[:, P:].bitcast(E5M2), scales[:, P:], early_h[2][:])
+        early.append((codes, scales))
+        late = {(0, 0): quantised(late_h[0, 0], "late00")}
         weigh_by_row(0, 1)
         weigh_by_row(1, 0)
         late[0, 1] = quantised(late_h[0, 1], "late01")
@@ -290,11 +294,16 @@ def tile_attend_gmf_nce_v_kernel(tc, uT, vT, y, us, ts, offs, uoffs, out):
         def scatter_early(td):
             nc.scalar.activation(listed(windows[td], tail_list, HALF, HALF), early_grads[:, td, :], ACT.Copy)
 
-        for td in range(2):
-            bank = in_bank(td, [P, HALF], "early%d" % td)
-            product(bank[:], td, whole(early))
-            nc.scalar.copy(early_grads[:, td, :], bank[:])
-            scatter_early(td)
+        for j, number in enumerate((0, 7)):
+            slots = slice(j * P, (j + 1) * P)
+            bank = in_bank(number, [P, P], "early0_%d" % j)
+            product(bank[:], 0, [(codes[:, slots], scales[:, slots]) for codes, scales in early])
+            nc.scalar.copy(early_grads[:, 0, slots], bank[:])
+        scatter_early(0)
+        bank = in_bank(2, [P, HALF], "early1")
+        product(bank[:], 1, whole(early))
+        nc.scalar.copy(early_grads[:, 1, :], bank[:])
+        scatter_early(1)
         closing = [in_bank(3 + b, [P, P], "late_first%d" % b) for b in range(2)]
         for b in range(2):
             multiply(closing[b][:], 0, b)
@@ -306,7 +315,7 @@ def tile_attend_gmf_nce_v_kernel(tc, uT, vT, y, us, ts, offs, uoffs, out):
         others = [in_bank(3, [P, 2, P], "late_plane1")]
         for b in range(2):
             multiply(others[0][:, b, :], 1, b)
-        bank = in_bank(1, [P, 2, HALF], "early23")
+        bank = in_bank(2, [P, 2, HALF], "early23")
         for td in (2, 3):
             product(bank[:, td - 2, :], td, whole(early))
         nc.scalar.copy(early_grads[:, 2:, :], bank[:])

@@ -83,9 +83,9 @@ def tile_attend_gmf_nce_v_kernel(tc, uT, vT, y, us, ts, offs, uoffs, out):
             nc.sync.dma_start(labels[g][:], y_rows[g])
 
         heads = kept([P, PACK * R], BF16, "heads")
-        late_heads = heads[:, 3 * R + K - 16 : 3 * R + K + 16].bitcast(F32)
+        late_heads = heads[:, PACK * R - K :].bitcast(F32)
         ts_cols = late_heads[:, 0:BLOCKS]
-        ts_minus = late_heads[:, 7:9]
+        ts_minus = late_heads[:, 8:10]
         ts_picked = kept([P, N], F32, "ts_picked")
         nc.vector.tensor_copy(ts_picked[:], listed(ts_window, tail_list, 0, N))
         bank = in_bank(0, [P, BLOCKS, P], "ts_turned")
@@ -115,12 +115,18 @@ def tile_attend_gmf_nce_v_kernel(tc, uT, vT, y, us, ts, offs, uoffs, out):
                 nc.scalar.activation(tile[:], us_rows[:].rearrange("p (u e) s -> p u s e", e=2), ACT.Copy, scale=ts_minus[:, b - 2 : b - 1])
                 scale_by_slot[b, g] = tile
 
-        scale_by_row = [kept([P, PACK, N], F32, "scale_by_row0")]
+        scale_by_row = [kept([P, PACK, N], F32, "scale_by_row0"), placed([P, PACK, N], F32, "scale_by_row1", 11 * PLANE)]
+
+        def spread_by_row(places):
+            for t in places:
+                nc.scalar.activation(scale_by_row[1][:, t, :], ts_signed[:], ACT.Copy, scale=row_scale[:, 1, t : t + 1])
+
+        spread_by_row((0, 1))
         for t in range(PACK):
             nc.gpsimd.tensor_scalar(scale_by_row[0][:, t, :], ts_signed[:], row_scale[:, 0, t : t + 1], 0.0, ALU.mult, ALU.add)
 
         plane = PASSES * P
-        turned = [placed([P, 2 * plane * PACK], BF16, "turned%d" % n, (11 * PLANE + 4096, 10 * PLANE)[n]) for n in range(2)]
+        turned = [placed([P, 2 * plane * PACK], BF16, "turned%d" % n, (10 * PLANE + 4096, 10 * PLANE)[n]) for n in range(2)]
         woven = kept([P, R * PACK], BF16, "woven")
 
         def turn_heads(td):
@@ -135,13 +141,13 @@ def tile_attend_gmf_nce_v_kernel(tc, uT, vT, y, us, ts, offs, uoffs, out):
 
         for td in range(PACK - 1):
             nc.vector.tensor_copy(heads[:, td * R : (td + 1) * R], listed(u_raw[td], head_list, 0, R))
-        nc.vector.tensor_copy(heads[:, 3 * R : 3 * R + HALF], listed(u_raw[3], head_list, 0, HALF))
+        nc.vector.tensor_copy(heads[:, 3 * R : 3 * R + K], listed(u_raw[3], head_list, 0, K))
         for td in range(2):
             turn_heads(td)
-        for first, count in ((HALF, HALF), (K, K)):
-            nc.scalar.activation(heads[:, 3 * R + first : 3 * R + first + count], listed(u_raw[3], head_list, first, count), ACT.Copy)
+        nc.scalar.activation(heads[:, 3 * R + K :], listed(u_raw[3], head_list, K, K), ACT.Copy)
         for td in range(2, PACK):
             turn_heads(td)
+        spread_by_row((2, 3))
         for g in range(PASSES):
             nc.vector.tensor_copy(
                 woven[:, g * K * PACK : (g + 1) * K * PACK].rearrange("p (t c e d) -> p c t e d", t=PACK, e=2, d=PACK),
@@ -156,10 +162,6 @@ def tile_attend_gmf_nce_v_kernel(tc, uT, vT, y, us, ts, offs, uoffs, out):
             codes = kept([P, 2 * plane], U32, "xt_codes%d" % n)
             nc.vector.quantize_mx(codes[:].bitcast(E4M3), xt_scales[:, 2 * n * plane : 2 * (n + 1) * plane], turned[n][:])
             xt_codes.extend(codes[:, e * plane : (e + 1) * plane] for e in range(2))
-        scale_by_row.append(placed([P, PACK, N], F32, "scale_by_row1", 11 * PLANE))
-        for t in range(PACK):
-            nc.vector.tensor_scalar(scale_by_row[1][:, t, :], ts_signed[:], row_scale[:, 1, t : t + 1], None, ALU.mult)
-
         first_scale = placed([P, 2, P], F32, "first_scale", 8 * PLANE + 2048)
         nc.scalar.copy(first_scale[:], scale_by_row[0][:, 0:2, 0:P])
 

@@ -115,18 +115,16 @@ def tile_attend_gmf_nce_v_kernel(tc, uT, vT, y, us, ts, offs, uoffs, out):
                 nc.scalar.activation(tile[:], us_rows[:].rearrange("p (u e) s -> p u s e", e=2), ACT.Copy, scale=ts_minus[:, b - 2 : b - 1])
                 scale_by_slot[b, g] = tile
 
-        scale_by_row = [kept([P, PACK, N], F32, "scale_by_row0"), placed([P, PACK, N], F32, "scale_by_row1", 11 * PLANE)]
+        second_scales = kept([P, PACK * N], F32, "scale_by_row1")
+        scale_by_row = [kept([P, PACK, N], F32, "scale_by_row0")[:], second_scales[:].rearrange("p (t i) -> p t i", t=PACK)]
 
-        def spread_by_row(places):
-            for t in places:
-                nc.scalar.activation(scale_by_row[1][:, t, :], ts_signed[:], ACT.Copy, scale=row_scale[:, 1, t : t + 1])
-
-        spread_by_row((0, 1))
+        for t in range(2):
+            nc.scalar.activation(scale_by_row[1][:, t, :], ts_signed[:], ACT.Copy, scale=row_scale[:, 1, t : t + 1])
         for t in range(PACK):
             nc.gpsimd.tensor_scalar(scale_by_row[0][:, t, :], ts_signed[:], row_scale[:, 0, t : t + 1], 0.0, ALU.mult, ALU.add)
 
         plane = PASSES * P
-        turned = [placed([P, 2 * plane * PACK], BF16, "turned%d" % n, (10 * PLANE + 4096, 10 * PLANE)[n]) for n in range(2)]
+        turned = [second_scales[:, 2 * N :].bitcast(BF16), kept([P, 2 * plane * PACK], BF16, "turned1")[:]]
         woven = kept([P, R * PACK], BF16, "woven")
 
         def turn_heads(td):
@@ -136,7 +134,7 @@ def tile_attend_gmf_nce_v_kernel(tc, uT, vT, y, us, ts, offs, uoffs, out):
                 words = heads[:, first : first + K].bitcast(F32)
                 for u in range(2):
                     nc.tensor.transpose(bank[:, g, u, :], words[:, u : K // 2 : 2], ident[:])
-            words = turned[td // 2][:].bitcast(F32).rearrange("m (d g p u) -> m d g p u", g=PASSES, d=2, u=2)
+            words = turned[td // 2].bitcast(F32).rearrange("m (d g p u) -> m d g p u", g=PASSES, d=2, u=2)
             nc.scalar.copy(words[:, td % 2], bank[:].rearrange("m g u p -> m g p u"))
 
         for td in range(PACK - 1):
@@ -147,7 +145,6 @@ def tile_attend_gmf_nce_v_kernel(tc, uT, vT, y, us, ts, offs, uoffs, out):
         nc.scalar.activation(heads[:, 3 * R + K :], listed(u_raw[3], head_list, K, K), ACT.Copy)
         for td in range(2, PACK):
             turn_heads(td)
-        spread_by_row((2, 3))
         for g in range(PASSES):
             nc.vector.tensor_copy(
                 woven[:, g * K * PACK : (g + 1) * K * PACK].rearrange("p (t c e d) -> p c t e d", t=PACK, e=2, d=PACK),
@@ -160,10 +157,10 @@ def tile_attend_gmf_nce_v_kernel(tc, uT, vT, y, us, ts, offs, uoffs, out):
         xt_codes = []
         for n in range(2):
             codes = kept([P, 2 * plane], U32, "xt_codes%d" % n)
-            nc.vector.quantize_mx(codes[:].bitcast(E4M3), xt_scales[:, 2 * n * plane : 2 * (n + 1) * plane], turned[n][:])
+            nc.vector.quantize_mx(codes[:].bitcast(E4M3), xt_scales[:, 2 * n * plane : 2 * (n + 1) * plane], turned[n])
             xt_codes.extend(codes[:, e * plane : (e + 1) * plane] for e in range(2))
-        first_scale = placed([P, 2, P], F32, "first_scale", 8 * PLANE + 2048)
-        nc.scalar.copy(first_scale[:], scale_by_row[0][:, 0:2, 0:P])
+        for t in range(2, PACK):
+            nc.vector.tensor_scalar(scale_by_row[1][:, t, :], ts_signed[:], row_scale[:, 1, t : t + 1], None, ALU.mult)
 
         parts = ((0, P), (P, P), (HALF, HALF))
         pair = placed([P, 2, N], BF16, "pair", 3 * PLANE)
@@ -182,14 +179,14 @@ def tile_attend_gmf_nce_v_kernel(tc, uT, vT, y, us, ts, offs, uoffs, out):
 
         def quantise_tails(n):
             first, count = parts[n]
-            codes = placed([P, count], U32, "w_codes2", 8 * PLANE + 2048) if n == 2 else kept([P, count], U32, "w_codes%d" % n)
+            codes = kept([P, count], U32, "w_codes%d" % n)
             scales = kept([P, count], U8, "w_scales%d" % n)
             nc.vector.quantize_mx(codes[:].bitcast(E4M3), scales[:], tails[n][:].rearrange("p i d -> p (i d)"))
             for at in range(0, count, P):
                 w_codes.append(codes[:, at : at + P])
                 w_scales.append(scales[:, at : at + P])
 
-        for n in range(2):
+        for n in range(len(parts)):
             quantise_tails(n)
 
         units = [(0, 0), (0, 1), (1, 0), (2, 0), (3, 0), (2, 1), (3, 1), (1, 1)]
@@ -206,10 +203,7 @@ def tile_attend_gmf_nce_v_kernel(tc, uT, vT, y, us, ts, offs, uoffs, out):
                         rhs=w_codes[b].bitcast(E4M3), rhs_scale=w_scales[b], start=True, stop=True,
                     )
                 places = slice(first, first + count)
-                scale = scale_by_row[g][:, places, slots] if n or first else first_scale[:]
-                nc.vector.tensor_tensor(z[b, g][:, places, :], acc[:], scale, ALU.mult)
-            if n == 0:
-                quantise_tails(2)
+                nc.vector.tensor_tensor(z[b, g][:, places, :], acc[:], scale_by_row[g][:, places, slots], ALU.mult)
             nc.scalar.activation(z[b, g][:], z[b, g][:], ACT.Sigmoid)
         for g in range(PASSES):
             for b in range(2):

from contextlib import ExitStack

import concourse.mybir as mybir
from concourse.masks import make_identity

F32 = mybir.dt.float32
BF16 = mybir.dt.bfloat16
U32 = mybir.dt.uint32
I32 = mybir.dt.int32
U16 = mybir.dt.uint16
U8 = mybir.dt.uint8
E4M3 = mybir.dt.float8_e4m3fn_x4
E5M2 = mybir.dt.float8_e5m2_x4
ACT = mybir.ActivationFunctionType
ALU = mybir.AluOpType

P = 128
D, R, N, T = 512, 1024, 512, 2048
PACK = 4
K = P * PACK
PASSES = R // K
BLOCKS = N // P
HALF = N // 2
BANK = 2048
PLANE = 4 * T
FLOPS = 2 * 2 * D * R * N


def tile_attend_gmf_nce_v_kernel(tc, uT, vT, y, us, ts, offs, uoffs, out):
    nc = tc.nc
    with ExitStack() as ctx:
        keep = ctx.enter_context(tc.tile_pool(name="keep", bufs=1))
        shared = ctx.enter_context(tc.tile_pool(name="shared", bufs=1))
        psum = ctx.enter_context(tc.psum_pool(name="psum", bufs=1))

        def in_bank(number, shape, name):
            return psum.tile(shape, F32, name=name, tag=name, offset=number * BANK)

        def kept(shape, dtype, name, align=64):
            return keep.tile(shape, dtype, name=name, tag=name, align_bytes=align)

        def placed(shape, dtype, name, offset, align=64):
            return shared.tile(shape, dtype, name=name, tag=name, align_bytes=align, offset=offset)

        tail_list = kept([P, N // 16], U16, "tail_list")
        head_list = kept([P, R // 16], U16, "head_list")

        def listed(window, offsets, first, count):
            return window[:].indirect(offsets[:, first // 16 : (first + count) // 16])

        warm = kept([P, 2], F32, "warm")
        nc.gpsimd.memset(warm[:, 0:1], 0.0)
        nc.scalar.activation(warm[:, 1:2], warm[:, 0:1], ACT.Sigmoid)
        ident = kept([P, P], F32, "ident")
        make_identity(nc, ident[:])
        ts_window = placed([P, T], F32, "ts_window", 4 * PLANE)
        us_line = placed([P, R], F32, "us_line", 5 * PLANE)
        nc.gpsimd.memset(ts_window[0 : P - 1, :].bitcast(I32), 0)
        zeros = placed([P, P], F32, "zeros", 8 * PLANE)
        nc.vector.memset(zeros[:], 0.0)
        nc.vector.memset(us_line[0 : P - 1, :].bitcast(I32), 0)
        windows = [kept([P, T], F32, "window%d" % td, 256) for td in range(3)]
        for window in windows:
            nc.gpsimd.memset(window[:].bitcast(I32), 0)

        nc.scalar.dma_start(ts_window[P - 1 : P, :], ts[0:1, :])
        nc.scalar.dma_start(us_line[P - 1 : P, :], us[0].rearrange("r o -> o r"))
        nc.sync.dma_start(tail_list[:], offs)

        def load_plane(tile, table, td):
            nc.sync.dma_start(tile[:], table.rearrange("(p t) c -> t p c", t=PACK)[td])
            return tile

        u_raw = []
        for td in range(PACK):
            u_raw.append(load_plane(placed([P, T], F32, "u_raw%d" % td, td * PLANE, 256), uT, td))
            if td == 0:
                nc.sync.dma_start(head_list[:], uoffs)
        v_raw = [load_plane(kept([P, T], F32, "v_raw%d" % td, 256), vT, td) for td in range(PACK)]
        y_rows = y[0].rearrange("(g p t) i -> g p t i", g=PASSES, t=PACK)
        labels = [kept([P, PACK, N], F32, "labels%d" % g, 256) for g in range(PASSES)]
        for g in range(PASSES):
            nc.sync.dma_start(labels[g][:], y_rows[g])

        heads = kept([P, PACK * R], BF16, "heads")
        late_heads = heads[:, PACK * R - K :].bitcast(F32)
        ts_cols = late_heads[:, 0:BLOCKS]
        ts_minus = late_heads[:, 8:10]
        ts_picked = kept([P, N], F32, "ts_picked")
        nc.vector.tensor_copy(ts_picked[:], listed(ts_window, tail_list, 0, N))
        bank = in_bank(0, [P, BLOCKS, P], "ts_turned")
        for b in range(BLOCKS):
            nc.tensor.transpose(bank[:, b, :], ts_picked[:, b * P : (b + 1) * P], ident[:])
        nc.scalar.copy(ts_cols, bank[:, :, P - 1])
        nc.scalar.activation(ts_minus, bank[:, 2:4, P - 1], ACT.Copy, scale=-1.0)
        ts_rows = in_bank(1, [P, N], "ts_rows")
        for b in range(BLOCKS):
            nc.tensor.transpose(ts_rows[:, b * P : (b + 1) * P], ts_cols[:, b : b + 1].to_broadcast([P, P]), ident[:])
        ts_signed = kept([P, N], F32, "ts_signed")
        nc.scalar.copy(ts_signed[:, 0:HALF], ts_rows[:, 0:HALF])
        nc.scalar.activation(ts_signed[:, HALF:], ts_rows[:, HALF:], ACT.Copy, scale=-1.0)
        row_scale = kept([P, PASSES, PACK], F32, "row_scale")
        for g in range(PASSES):
            bank = in_bank(6 + g, [P, PACK, P], "us_turned%d" % g)
            for t in range(PACK):
                nc.tensor.transpose(bank[:, t, :], us_line[:, g * K + t : (g + 1) * K : PACK], ident[:])
            nc.scalar.copy(row_scale[:, g, :], bank[:, :, P - 1])
        scale_by_slot = {}
        for g in range(PASSES):
            us_rows = in_bank(2 + g, [P, PACK, P], "us_rows%d" % g)
            for t in range(PACK):
                nc.tensor.transpose(us_rows[:, t, :], row_scale[:, g, t : t + 1].to_broadcast([P, P]), ident[:])
            for b in (2, 3):
                tile = placed([P, 2, P, 2], F32, "scale_by_slot%d_%d" % (b, g), 9 * PLANE + BANK * len(scale_by_slot))
                nc.scalar.activation(tile[:], us_rows[:].rearrange("p (u e) s -> p u s e", e=2), ACT.Copy, scale=ts_minus[:, b - 2 : b - 1])
                scale_by_slot[b, g] = tile

        second_scales = kept([P, PACK * N], F32, "scale_by_row1")
        scale_by_row = [kept([P, PACK, N], F32, "scale_by_row0")[:], second_scales[:].rearrange("p (t i) -> p t i", t=PACK)]

        for t in range(2):
            nc.scalar.activation(scale_by_row[1][:, t, :], ts_signed[:], ACT.Copy, scale=row_scale[:, 1, t : t + 1])
        for t in range(PACK):
            nc.gpsimd.tensor_scalar(scale_by_row[0][:, t, :], ts_signed[:], row_scale[:, 0, t : t + 1], 0.0, ALU.mult, ALU.add)

        plane = PASSES * P
        turned = [second_scales[:, 2 * N :].bitcast(BF16), kept([P, 2 * plane * PACK], BF16, "turned1")[:]]
        woven = kept([P, R * PACK], BF16, "woven")

        def turn_heads(td):
            bank = in_bank(4 + td, [P, PASSES, 2, P], "heads_turned%d" % td)
            for g in range(PASSES):
                first = td * R + g * K
                words = heads[:, first : first + K].bitcast(F32)
                for u in range(2):
                    nc.tensor.transpose(bank[:, g, u, :], words[:, u : K // 2 : 2], ident[:])
            words = turned[td // 2].bitcast(F32).rearrange("m (d g p u) -> m d g p u", g=PASSES, d=2, u=2)
            nc.scalar.copy(words[:, td % 2], bank[:].rearrange("m g u p -> m g p u"))

        for td in range(PACK - 1):
            nc.vector.tensor_copy(heads[:, td * R : (td + 1) * R], listed(u_raw[td], head_list, 0, R))
        nc.vector.tensor_copy(heads[:, 3 * R : 3 * R + K], listed(u_raw[3], head_list, 0, K))
        for td in range(2):
            turn_heads(td)
        nc.scalar.activation(heads[:, 3 * R + K :], listed(u_raw[3], head_list, K, K), ACT.Copy)
        for td in range(2, PACK):
            turn_heads(td)
        for g in range(PASSES):
            nc.vector.tensor_copy(
                woven[:, g * K * PACK : (g + 1) * K * PACK].rearrange("p (t c e d) -> p c t e d", t=PACK, e=2, d=PACK),
                heads[:].rearrange("p (d g c e t) -> p g c t e d", d=PACK, g=PASSES, e=2, t=PACK)[:, g],
            )
        x_codes = kept([P, R], U32, "x_codes")
        x_scales = kept([P, R], U8, "x_scales")
        nc.vector.quantize_mx(x_codes[:].bitcast(E4M3), x_scales[:], woven[:])
        xt_scales = kept([P, PACK * plane], U8, "xt_scales")
        xt_codes = []
        for n in range(2):
            codes = kept([P, 2 * plane], U32, "xt_codes%d" % n)
            nc.vector.quantize_mx(codes[:].bitcast(E4M3), xt_scales[:, 2 * n * plane : 2 * (n + 1) * plane], turned[n])
            xt_codes.extend(codes[:, e * plane : (e + 1) * plane] for e in range(2))
        for t in range(2, PACK):
            nc.vector.tensor_scalar(scale_by_row[1][:, t, :], ts_signed[:], row_scale[:, 1, t : t + 1], None, ALU.mult)

        parts = ((0, P), (P, P), (HALF, HALF))
        pair = placed([P, 2, N], BF16, "pair", 3 * PLANE)
        for td in range(2):
            nc.scalar.activation(pair[:, td, :], listed(v_raw[td], tail_list, 0, N), ACT.Copy)
        tails = [placed([P, count, PACK], BF16, "tails%d" % first, 3 * PLANE + 2048 + 8 * first) for first, count in parts]
        for tile, (first, count) in zip(tails, parts):
            nc.vector.tensor_copy(
                tile[:, :, 0:2].rearrange("p (c i) d -> p c d i", i=4),
                pair[:, :, first : first + count].rearrange("p d (c i) -> p c d i", i=4),
            )
        for td in (2, 3):
            for tile, (first, count) in zip(tails, parts):
                nc.scalar.activation(tile[:, :, td], listed(v_raw[td], tail_list, first, count), ACT.Copy)
        w_codes, w_scales = [], []

        def quantise_tails(n):
            first, count = parts[n]
            codes = kept([P, count], U32, "w_codes%d" % n)
            scales = kept([P, count], U8, "w_scales%d" % n)
            nc.vector.quantize_mx(codes[:].bitcast(E4M3), scales[:], tails[n][:].rearrange("p i d -> p (i d)"))
            for at in range(0, count, P):
                w_codes.append(codes[:, at : at + P])
                w_scales.append(scales[:, at : at + P])

        for n in range(len(parts)):
            quantise_tails(n)

        units = [(0, 0), (0, 1), (1, 0), (2, 0), (3, 0), (2, 1), (3, 1), (1, 1)]
        z = {}
        for n, (b, g) in enumerate(units):
            slots = slice(b * P, (b + 1) * P)
            z[b, g] = placed([P, PACK, P], F32, "z%d" % n, n * BANK)
            for number, first, count in (((n - 1) % 3 + 1, 0, PACK),) if n else ((7, 0, 2), (0, 2, 2)):
                acc = in_bank(number, [P, count, P], "score%d_%d" % (n, first))
                for t in range(first, first + count):
                    rows = slice(g * K + t * P, g * K + (t + 1) * P)
                    nc.tensor.matmul_mx(
                        out=acc[:, t - first, :], lhsT=x_codes[:, rows].bitcast(E4M3), lhsT_scale=x_scales[:, rows],
                        rhs=w_codes[b].bitcast(E4M3), rhs_scale=w_scales[b], start=True, stop=True,
                    )
                places = slice(first, first + count)
                nc.vector.tensor_tensor(z[b, g][:, places, :], acc[:], scale_by_row[g][:, places, slots], ALU.mult)
            nc.scalar.activation(z[b, g][:], z[b, g][:], ACT.Sigmoid)
        for g in range(PASSES):
            for b in range(2):
                nc.gpsimd.tensor_tensor(z[b, g][:], z[b, g][:], labels[g][:, :, b * P : (b + 1) * P], ALU.subtract)

        summed = [(b, g) for b, g in units if b >= 2]
        sums = {}
        for n, (b, g) in enumerate(summed):
            sums[b, g] = in_bank((0, 7, 2, 3)[n], [P, PACK, P], "sum%d" % n)
            for t in range(PACK):
                nc.tensor.matmul(sums[b, g][:, t, :], labels[g][:, t, b * P : (b + 1) * P], ident[:], start=(t == 0), stop=False, is_transpose=True)
            for t in range(PACK):
                nc.tensor.matmul(sums[b, g][:, t, :], z[b, g][:, t, :], ident[:], start=False, stop=(t == PACK - 1), is_transpose=True)

        early_h = [kept([P, HALF * PACK], BF16, "early_h0"), kept([P, K], BF16, "early_h12"), placed([P, K], BF16, "early_h13", 6 * PLANE + 512)]
        early_parts = [early_h[0][:, 0:K], early_h[0][:, K:], early_h[1][:], early_h[2][:]]
        for n, (b, g) in enumerate(summed):
            bank = in_bank((4, 5, 6, 1)[n], [P, 2, P], "h_turned%d" % n)
            for u in range(2):
                by_slot = kept([P, P, 2], BF16, "h_by_slot%d_%d" % (n, u))
                nc.vector.scalar_tensor_tensor(
                    by_slot[:], sums[b, g][:, 2 * u : 2 * u + 2, :].rearrange("p e s -> p s e"), 1.0,
                    scale_by_slot[b, g][:, u], ALU.subtract, ALU.mult,
                )
                nc.tensor.transpose(bank[:, u, :], by_slot[:].rearrange("p s e -> p (s e)").bitcast(F32), ident[:])
            nc.scalar.copy(early_parts[n].bitcast(F32).rearrange("p (i u) -> p i u", u=2), bank[:].rearrange("p u i -> p i u"))

        late_h = {(0, 0): placed([P, K], BF16, "late_h00", 9 * PLANE + 6144)}
        late_h[0, 1] = placed([P, K], BF16, "late_h01", 6 * PLANE + 64 + 320)
        last_h = placed([P, PASSES, K], BF16, "late_h1", 6 * PLANE + 1088 + 320)
        late_h = {unit: tile[:] for unit, tile in late_h.items()}
        for g in range(PASSES):
            late_h[1, g] = last_h[:, g, :]

        def weigh_by_row(b, g):
            nc.vector.tensor_tensor(
                late_h[b, g].rearrange("p (c i t) -> p c t i", i=4, t=PACK),
                z[b, g][:].rearrange("p t (c i) -> p c t i", i=4),
                scale_by_row[g][:, :, b * P : (b + 1) * P].rearrange("p t (c i) -> p c t i", i=4),
                ALU.mult,
            )

        def quantised(values, name, offset=None):
            width = values.shape[1] // PACK
            codes = placed([P, width], U32, name + "_codes", offset) if offset else kept([P, width], U32, name + "_codes")
            scales = kept([P, width], U8, name + "_scales")
            nc.vector.quantize_mx(codes[:].bitcast(E5M2), scales[:], values)
            return codes, scales

        def product(acc, td, moving):
            for g in range(PASSES):
                codes, scales = moving[g]
                nc.tensor.matmul_mx(
                    out=acc, lhsT=xt_codes[td][:, g * P : (g + 1) * P].bitcast(E4M3),
                    lhsT_scale=xt_scales[:, td * plane + g * P : td * plane + (g + 1) * P],
                    rhs=codes.bitcast(E5M2), rhs_scale=scales, start=(g == 0), stop=(g == PASSES - 1),
                )

        early = [quantised(early_h[0][:], "early0", 9 * PLANE + 5120)]
        codes = placed([P, HALF], U32, "early1_codes", 9 * PLANE + 4096)
        scales = kept([P, HALF], U8, "early1_scales")
        nc.vector.quantize_mx(codes[:, 0:P].bitcast(E5M2), scales[:, 0:P], early_h[1][:])
        weigh_by_row(0, 0)
        nc.vector.quantize_mx(codes[:, P:].bitcast(E5M2), scales[:, P:], early_h[2][:])
        early.append((codes, scales))
        late = {(0, 0): quantised(late_h[0, 0], "late00")}
        weigh_by_row(0, 1)
        weigh_by_row(1, 0)
        late[0, 1] = quantised(late_h[0, 1], "late01")
        weigh_by_row(1, 1)
        for g in range(PASSES):
            late[1, g] = quantised(late_h[1, g], "late1%d" % g)

        out_planes = out.rearrange("(p t) c -> t p c", t=PACK)
        early_grads = placed([P, PACK, HALF], F32, "early_grads", 2 * PLANE)
        first_grads = placed([P, 2, P], F32, "first_grads", 2 * PLANE + 4096)

        def whole(pairs):
            return [(codes[:], scales[:]) for codes, scales in pairs]

        def multiply(acc, td, b):
            product(acc, td, whole([late[b, g] for g in range(PASSES)]))

        def scatter_early(td):
            nc.scalar.activation(listed(windows[td], tail_list, HALF, HALF), early_grads[:, td, :], ACT.Copy)

        for j, number in enumerate((0, 7)):
            slots = slice(j * P, (j + 1) * P)
            bank = in_bank(number, [P, P], "early0_%d" % j)
            product(bank[:], 0, [(codes[:, slots], scales[:, slots]) for codes, scales in early])
            nc.scalar.copy(early_grads[:, 0, slots], bank[:])
        scatter_early(0)
        bank = in_bank(2, [P, HALF], "early1")
        product(bank[:], 1, whole(early))
        nc.scalar.copy(early_grads[:, 1, :], bank[:])
        scatter_early(1)
        closing = [in_bank(3 + b, [P, P], "late_first%d" % b) for b in range(2)]
        for b in range(2):
            multiply(closing[b][:], 0, b)
            nc.vector.tensor_copy(first_grads[:, b, :], closing[b][:])
            nc.vector.tensor_tensor(listed(windows[0], tail_list, b * P, P), first_grads[:, b, :], zeros[:], ALU.add)
        nc.sync.dma_start(out_planes[0], windows[0][:])
        windows.append(placed([P, T], F32, "window3", 7 * PLANE + 256, 256))
        nc.gpsimd.memset(windows[3][:].bitcast(I32), 0)
        others = [in_bank(3, [P, 2, P], "late_plane1")]
        for b in range(2):
            multiply(others[0][:, b, :], 1, b)
        bank = in_bank(2, [P, 2, HALF], "early23")
        for td in (2, 3):
            product(bank[:, td - 2, :], td, whole(early))
        nc.scalar.copy(early_grads[:, 2:, :], bank[:])
        for td in (2, 3):
            scatter_early(td)
        others.append(in_bank(4, [P, 2, HALF], "late_planes23"))
        for td in (2, 3):
            for b in range(2):
                multiply(others[1][:, td - 2, b * P : (b + 1) * P], td, b)
        second_grads = kept([P, HALF], F32, "second_grads")
        nc.vector.tensor_copy(second_grads[:], others[0][:].rearrange("p b i -> p (b i)"))
        nc.vector.tensor_copy(listed(windows[1], tail_list, 0, HALF), second_grads[:])
        nc.sync.dma_start(out_planes[1], windows[1][:])
        late_grads = placed([P, 2, HALF], F32, "late_grads", 8 * PLANE + 256)
        nc.vector.tensor_copy(late_grads[:], others[1][:])
        for td in range(2, PACK):
            nc.vector.tensor_copy(listed(windows[td], tail_list, 0, HALF), late_grads[:, td - 2, :])
            nc.sync.dma_start(out_planes[td], windows[td][:])
